import numpy as np, ml_dtypes
CORES = [36,164,52,180,100,228,116,244]
N = 8
BF = ml_dtypes.bfloat16
S, A, L, M, R, D = 128, 64, 32, 2, 32, 8
def steps(nx, sy):
    g = np.arange(8); s = np.zeros(8, np.int64); place = np.zeros((N * L, 8), np.int64); cnt = np.zeros((N * L, 8), np.int64)
    for i in range(N * L):
        place[i] = sy[i // L, :, i % L].astype(np.int64) * S + s
        v = nx[i // L, g, place[i]].astype(np.int64)
        s = v % S; cnt[i] = v // S
    return place, cnt
def counts(rng, uneven=False):
    k = np.argsort(rng.random((N, 8, S, A)), -1)
    w = rng.integers(0, 2, k.shape) * M if uneven else rng.integers(0, M + 1, k.shape)
    return np.ascontiguousarray(np.where(k <= M, k, w).transpose(0, 1, 3, 2))
def perms(rng):
    return np.argsort(rng.random((N, 8, A, S)), -1)
def bounds(rng):
    e = np.zeros((8, N + 1), np.int64)
    e[:, 1:N] = np.arange(1, N) * R + rng.integers(-D, D + 1, (8, N - 1)); e[:, N] = N * R - rng.integers(0, D + 1, 8)
    e[0, N] = N * R - D; e[7, N] = N * R
    return e
def draw(rng, to, ct, e, burst=False):
    n = (e[:, 1:] - e[:, :-1])[:, :, None]
    k = (np.arange(L * M) - M * rng.integers(0, L, (8, N, 1))) % (L * M) if burst else np.argsort(rng.random((8, N, L * M)), -1)
    c = np.sum((k < n).reshape(8, N, L, M), axis=-1)
    g = np.arange(8); s = np.zeros(8, np.int64); sy = np.zeros((N, 8, L), np.int32)
    for i in range(N * L):
        q = i // L; ok = ct[q][g, :, s] == c[:, q, i % L][:, None]
        a = np.argmax(np.where(ok, rng.random((8, A)), -1.0), axis=1)
        sy[q, :, i % L] = a; s = to[q][g, a, s]
    return {"nx": (ct * S + to).reshape(N, 8, A * S).astype(np.int32), "em": rng.integers(0, 64 ** M, (N, 8, A * S)).astype(np.int32), "sy": sy}
def setup_inputs(rng):
    to = np.where(rng.random((N, 8, A, 1)) < 0.125, rng.integers(0, S, (N, 8, A, S)), perms(rng))
    return draw(rng, to, counts(rng), bounds(rng))
def setup_inputs_edge(rng):
    e = bounds(rng); g = np.arange(8)[:, None]; r = np.arange(1, N)[None, :]
    e[:, 1:N] = r * R + D * np.where(g % 2 == 0, 1 - 2 * ((r + g // 2) % 2), 1 - 2 * (g // 2 % 2)); e[:, N] = N * R - D * (np.arange(8) // 4)
    return draw(rng, perms(rng), counts(rng), e)
def setup_inputs_even(rng):
    e = bounds(rng); e[:] = np.arange(N + 1) * R
    return draw(rng, perms(rng), counts(rng), e)
def setup_inputs_merge(rng):
    kind = (np.argsort(rng.random((N, 8, A)), -1) % 4)[:, :, :, None]; h = (N, 8, A, 1); s = np.arange(S)
    one = np.where(rng.random(h) < 0.5, rng.integers(0, 2, h) * (S - 1), rng.integers(0, S, h))
    to = np.where(kind == 0, one, np.where(kind == 1, s, np.where(kind == 2, (s + 1) % S, rng.integers(0, S, (N, 8, A, S)))))
    return draw(rng, to, counts(rng), bounds(rng))
def setup_inputs_spread(rng):
    to = np.minimum(np.floor(S * rng.random((N, 8, A, S)) ** 6), S - 1).astype(np.int64)
    d = draw(rng, to, counts(rng, True), bounds(rng), True)
    h = (N, 8, A * S); d["em"] = (d["em"] >> np.where(rng.random(h) < 0.5, rng.integers(0, 6 * M, h), 0)).astype(np.int32)
    return d
def check_inputs(d):
    bad = []
    for k, top in (("nx", (M + 1) * S), ("em", 64 ** M), ("sy", A)):
        if d[k].min() < 0 or d[k].max() >= top: bad.append("range of " + k)
    if bad: return bad
    place, cnt = steps(d["nx"], d["sy"])
    off = np.add.accumulate(cnt, 0)[L - 1::L] - R * np.arange(1, N + 1)[:, None]
    if (np.abs(off) > D).any(): bad.append("running totals")
    if (off[-1] > 0).any(): bad.append("whole total")
    return bad
def reference(nx, em, sy):
    place, cnt = steps(nx, sy); g = np.broadcast_to(np.arange(8), (N * L, 8)); r = (np.arange(N * L) // L)[:, None]
    e = em[r, g, place].astype(np.int64); beg = np.add.accumulate(cnt, 0) - cnt
    z = np.full((8, N * R), -1, np.int64)
    for m in range(M):
        on = cnt > m
        z[g[on], beg[on] + m] = ((e >> (6 * m)) & 63)[on]
    return {"y": np.ascontiguousarray(z.reshape(8, N, R).transpose(1, 0, 2)).astype(np.float32)}

@@ -1,0 +1,332 @@
+from concourse.bass import DstId, RemoteDMATransfer
+from concourse.mybir import AluOpType, ActivationFunctionType
+
+ALU = AluOpType
+ACTF = ActivationFunctionType
+F, B, H, I4, U2 = "float32", "bfloat16", "float16", "int32", "uint16"
+SBUF = {
+    I4: "nxi:512 emi:512 ipi:8 qgi:8 v2:96 ei:16",
+    B: "syr:256 ones:128 zw:128 zw0:128 wx:128 c1:256 cc:256 tri:128 wb:128 cab:16 gsv:96 oh:384",
+    H: "nxh:512 emh:512 sela:128 pfx:32",
+    F: "ipf:8 qgf:8 hm:8 mq:128 mg:128 mi:128 io2:256 idw:256 rm:16 n0:8 cu:8 bias:24 sg:128 g8:96 gsr:96 l2:8 iot:64 "
+       "tri0:128 ab:4096 w0:256 w1:256 big:2304 cnt:2304 xpb:256 pay:768 cf:256 ef:16 val:16 ys:32",
+    U2: "uo:256 ui:2048 s:64 lst:8 lsc:24 gl:8",
+}
+SCRATCH = {w.split(":")[0]: ("sbuf", [128, int(w.split(":")[1])], d) for d, ws in SBUF.items() for w in ws.split()}
+SCRATCH.update({
+    "syi": ("sbuf", [128, 8, 32], I4),
+    "selm": ("sbuf", [128, 8, 32], H), "tb": ("sbuf", [128, 32, 32], H),
+    "oi": ("sbuf", [128, 16, 16], I4), "oi2": ("sbuf", [128, 16, 16], I4),
+    "off": ("sbuf", [128, 16, 16], U2),
+    "mdo": ("dram", [128, 16], F), "mdi": ("dram", [8, 128, 16], F),
+    "cdo": ("dram", [128, 16], F), "cdi": ("dram", [8, 128, 16], F),
+    "xdo": ("dram", [128, 16], F), "xdi": ("dram", [8, 128, 16], F),
+})
+SCRATCH.update({n: ("psum", [128, 512], F) for n in "pb0 pb1 pb2 pa0 pa1 pa2".split()})
+SEMAPHORES = ("v a t p ds dn0 dn1 de mo xo co yo lx lw lm lc".split()
+              + [s + str(r) for s in ("x", "w", "m", "c", "ld", "lx", "lc") for r in range(8)])
+
+
+def rank_program(g, core, T, topo):
+    r = T.rank_of(core)
+    if r is None:
+        return
+    cores = T.cores
+    N = len(cores)
+    V, A, P, Y = g.vector, g.scalar, g.tensor, g.sync
+    eng = {"v": V, "a": A, "t": P, "p": g, "y": Y}
+    cnt = {"v": 0, "a": 0, "t": 0, "p": 0}
+    seen = {}
+    nb = [d for d in (r + 1, r - 1) if 0 <= d < N]
+
+    def wait(q, name, val):
+        if val > seen.get((q, name), 0):
+            seen[(q, name)] = val
+            eng[q].wait_ge(T.sem[name], val)
+
+    def do(q, fn, *deps):
+        for name, val in deps:
+            wait(q, name, val)
+        fn().then_inc(T.sem[q], 1)
+        cnt[q] += 1
+        return (q, cnt[q])
+
+    def ts(out, in0, s1, s2, op0, *op1, dep=()):
+        return do("v", lambda: V.tensor_scalar(out, in0, s1, s2, op0, *op1), *dep)
+
+    def tt(out, in0, in1, op, dep=()):
+        return do("v", lambda: V.tensor_tensor(out, in0, in1, op), *dep)
+
+    def cp(out, in_, dep=()):
+        return do("v", lambda: V.tensor_copy(out, in_), *dep)
+
+    def mm(out, lh, rh, start, stop, dep=()):
+        return do("t", lambda: P.matmul(out, lh, rh, start, stop), *dep)
+
+    def act(out, in_, func, dep=(), **kw):
+        return do("a", lambda: A.activation(out, in_, func, **kw), *dep)
+
+    def blk(buf, d):
+        return buf[:, 256 * d:256 * d + 256]
+    hf = [slice(0, 128), slice(128, 256)]
+    slot = {r: 0}
+    for d in nb:
+        slot[d] = len(slot)
+
+    for h in range(2):
+        (Y, A)[h].dma_start(T.syi[0:1, 4 * h:4 * h + 4, :], T.sy[h::2, :]).then_inc(T.sem.ds, 16)
+    for t in range(4):
+        (Y, A)[t % 2].dma_start(T.nxi[:, 128 * t:128 * t + 128], T.nx[2 * t:2 * t + 2, :]).then_inc(T.sem["dn%d" % (t // 2)], 16)
+    for t in range(4):
+        (Y, A)[t % 2].dma_start(T.emi[:, 128 * t:128 * t + 128], T.em[2 * t:2 * t + 2, :]).then_inc(T.sem.de, 16)
+    DS, DN, DE = ("ds", 32), [("dn0", 32), ("dn1", 32)], ("de", 64)
+
+    def iota(ap, pattern, base, cm):
+        return do("p", lambda: g.iota(ap, pattern, base, cm, allow_small_or_imprecise_dtypes=True))
+    iota(T.ipi[:, 0:1], [[0, 1]], 0, 1)
+    iota(T.ipf[:, 0:1], [[0, 1]], 0, 1)
+    pq = iota(T.rm[:, 0:16], [[1, 16]], 0, 0)
+    pc = iota(T.mi[:, :], [[1, 128]], 0, 0)
+    pi2 = iota(T.io2[:, :], [[1, 256]], 0, 0)
+    iota(T.mq[:, :], [[0, 8], [1, 16]], 0, 0)
+    iota(T.mg[:, :], [[1, 8], [0, 16]], 0, 0)
+    iota(T.iot[:, 0:32], [[1, 32]], 32 * r, 0)
+    iota(T.iot[:, 32:64], [[1, 32]], 32 * r - 1, 0)
+    iota(T.l2[:, 0:6], [[2, 6]], 0, 0)
+    pio = iota(T.g8[:, :], [[0, 12], [1, 8]], 0, 0)
+    pz = pio
+    if r:
+        pz = iota(T.big[:, 0:256 * r], [[0, 256 * r]], 0, 0)
+    zeros = 256 * min(N, r + 2)
+    pcz = iota(T.cnt[:, 0:zeros], [[0, zeros]], 0, 0)
+
+    CB = 129
+    BZ = 2047.0 - 4096 * CB
+    von = do("v", lambda: V.memset(T.ones[:, :], 1.0))
+    ts(T.qgi[:, 0:1], T.ipi[:, 0:1], 15, None, ALU.bitwise_and, dep=[pq])
+    ts(T.qgi[:, 2:3], T.ipi[:, 0:1], 63, None, ALU.bitwise_and)
+    v = ts(T.qgi[:, 1:2], T.ipi[:, 0:1], 4, None, ALU.logical_shift_right)
+    qcol, gcol, pcol, m0 = T.qgf[:, 0:1], T.qgf[:, 1:2], T.ipf[:, 0:1], T.rm[:, 0:1]
+    ts(T.hm[:, 0:1], pcol, 64.0, None, ALU.is_lt)
+    ts(T.hm[:, 1:2], pcol, 64.0, None, ALU.is_ge)
+    vqg = cp(T.qgf[:, 0:3], T.qgi[:, 0:3], dep=[v])
+    vrm = ts(T.rm[:, :], T.rm[:, :], qcol, None, ALU.is_equal, dep=[vqg])
+    vg16 = tt(T.qgf[:, 3:4], pcol, qcol, ALU.subtract)
+    vbi = ts(T.bias[:, 0:16], T.rm[:, :], BZ, None, ALU.mult, dep=[vrm])
+    vwx = ts(T.wx[:, :], T.mi[:, :], pcol, 4096.0, ALU.is_equal, ALU.mult, dep=[pc])
+    v = ts(T.zw[:, :], T.mi[:, :], T.qgf[:, 3:4], 1.0 / 256, ALU.is_equal, ALU.mult, dep=[vg16])
+    vzw = ts(T.zw0[:, :], T.zw[:, :], m0, None, ALU.mult, dep=[v])
+    for seg in range(2):
+        mm(T["pa%d" % seg][:, 0:128], T.ones[0:1, :], T.ones[0:1, :], True, False, dep=[von])
+    for seg in range(2):
+        vrow = cp(T.syr[0:1, seg:256:2], T.syi[0:1, :, 16 * seg:16 * seg + 16], dep=[DS])
+    tbc = mm(T.pb0[:, 0:256], T.ones[0:1, :], T.syr[0:1, :], True, True, dep=[von, vrow])
+    act(T.bias[:, 16:17], m0, ACTF.Copy, scale=float(128 * (2 * r + 1)), dep=[vrm])
+    act(T.bias[:, 18:19], m0, ACTF.Copy, scale=-17 * CB / 256.0)
+    act(T.cu[:, 0:1], m0, ACTF.Identity, scale=255.0, bias=1.0)
+    act(T.cu[:, 1:2], m0, ACTF.Identity, scale=-255.0 / 256, bias=1.0)
+    acu = act(T.cu[:, 2:3], m0, ACTF.Copy, scale=float(128 * (2 * r + 3)))
+    aid = act(T.idw[:, :], T.io2[:, :], ACTF.Identity, scale=m0, bias=T.bias[:, 16:17], dep=[acu, pi2])
+
+    def cast(h):
+        return cp(T.nxh[:, 256 * h:256 * h + 256], T.nxi[:, 256 * h:256 * h + 256], dep=[DN[h]])
+    vn = [cast(0)]
+    for h in range(2):
+        for seg in range(2):
+            vsm = ts(T.selm[:, seg:8:2, 16 * h:16 * h + 16], T.pb0[:, 128 * h + seg:128 * h + 128:2], T.qgf[:, 2:3], T.hm[:, h:h + 1],
+                     ALU.is_equal, ALU.mult, dep=[tbc])
+    vn.append(cast(1))
+    hs = [slice(0, 64), slice(64, 128)]
+    for h in range(2):
+        vsa = ts(T.sela[hs[h], :], T.pb0[hs[h], 128 * h:128 * h + 128], T.qgf[hs[h], 2:3], None, ALU.is_equal)
+    vt = []
+    for u in range(2):
+        for h in range(2):
+            v = ts(T.tb[:, 16 * u:16 * u + 16, 16 * h:16 * h + 16], T.nxh[:, 256 * u:256 * u + 256], T.hm[:, h:h + 1], None, ALU.mult,
+                   dep=[vn[u]])
+        vt.append(v)
+    vem = ts(T.emh[:, :], T.emi[:, :], -2048, None, ALU.add, dep=[DE])
+
+    for t in range(4):
+        for seg in range(2):
+            txn = mm(T.pb2[32 * t:32 * t + 32, hf[seg]], T.selm[:, 2 * t + seg, :], T.nxh[:, 128 * t:128 * t + 128],
+                     True, True, dep=[vsm, vn[t // 2]])
+    for t in range(4):
+        for c in range(8):
+            tof = mm(T.pb1[32 * t:32 * t + 32, c:256:8], T.tb[:, 8 * t + c, :], T.sela[:, 32 * t:32 * t + 32], True, True,
+                     dep=[vt[t // 2], vsa])
+    ac1 = act(T.c1[:, :], T.pb2[:, 0:256], ACTF.Copy, scale=1.0 / 128, bias=CB - 0.498, dep=[txn])
+    tpx = []
+    for seg in range(2):
+        for t in range(4):
+            mm(T["pa%d" % seg][32 * t:32 * t + 32, 0:128], T.selm[:, 2 * t + seg, :], T.emh[:, 128 * t:128 * t + 128], False, False,
+               dep=[vem])
+        tpx.append(mm(T["pa%d" % seg][:, 0:128], T.wx[:, :], T.c1[:, hf[seg]], False, True, dep=[vwx, ac1]))
+    aa = {}
+    for i in [15, 14, 13, 0, 12, 11, 10, 9, 8, 7, 6, 5, 4, 3, 2, 1]:
+        for seg in range(2):
+            o = T.ab[:, 256 * i + 128 * seg:256 * i + 128 * seg + 128] if i else T.xpb[:, hf[seg]]
+            aa[i, seg] = act(o, T["pa%d" % seg][:, 0:128], ACTF.Identity, dep=[tpx[seg], vbi], scale=T.rm[:, i:i + 1],
+                             bias=T.bias[:, i:i + 1])
+    ax = aa[0, 1]
+
+    vof = {}
+
+    def lists(lo, hi, part):
+        a, b = 16 * lo, 16 * hi
+        if part == 0:
+            vof["x"] = cp(T.oi[:, lo:hi, :], T.pb1[:, a:b], dep=[tof])
+        elif part == 1:
+            vof["x"] = ts(T.oi2[:, lo:hi, :], T.oi[:, lo:hi, :], 127, None, ALU.bitwise_and, dep=[vof["x"]])
+        else:
+            cp(T.off[:, lo:hi, 0:8], T.oi2[:, lo:hi, 0:8], dep=[vof["x"]])
+            x = ts(T.off[:, lo:hi, 8:16], T.oi2[:, lo:hi, 8:16], 128, None, ALU.add)
+            for i in range(lo, hi):
+                vof[i] = x
+    todo = [(lo, hi, part) for lo, hi in [(12, 16), (8, 12), (0, 8)] for part in range(3)]
+    for _ in range(3):
+        lists(*todo.pop(0))
+
+    prev, vw = T.idw[:, :], aid
+    for i in range(15, -1, -1):
+        o = T["w%d" % (i % 2)][:, :] if i else blk(T.big, r)
+        if i == 15:
+            for seg in range(2):
+                vw = tt(o[:, hf[seg]], prev.indirect(T.off[:, i, 8 * seg:8 * seg + 8]),
+                        T.ab[:, 256 * i + 128 * seg:256 * i + 128 * seg + 128], ALU.add, dep=[vof[i], aid, aa[i, seg]])
+        elif i:
+            vw = tt(o, prev.indirect(T.off[:, i, :]), T.ab[:, 256 * i:256 * i + 256], ALU.add, dep=[vof[i], vw, aa[i, 1]])
+        else:
+            vw = cp(o, prev.indirect(T.off[:, i, :]), dep=[vof[i], vw])
+        prev = o
+        if todo:
+            lists(*todo.pop(0))
+    vu = ts(T.uo[:, :], blk(T.big, r), T.bias[:, 16:17], T.cu[:, 0:1], ALU.subtract, ALU.mult, dep=[vw, acu])
+    pcn = T.pa2[:, 0:256]
+    mm(pcn, T.zw0[:, :], T.c1[:, :], True, False, dep=[vzw])
+    acc = act(T.cc[:, :], blk(T.big, r), ACTF.Copy, scale=1.0 / 4096, bias=CB - 0.5 + 1.0 / 8192, dep=[vw])
+    tcn = mm(pcn, T.zw[:, :], T.cc[:, :], False, True, dep=[acc])
+    acn = act(blk(T.cnt, r), pcn, ACTF.Identity, bias=T.bias[:, 18:19], dep=[tcn, pcz, acu])
+    apy = act(blk(T.pay, 0), blk(T.big, r), ACTF.Copy)
+
+    def send(buf_src, buf_dst, sem, lsem, dests):
+        mask = topo.mask(core, cores[dests[0]])
+        ids = []
+        for d in dests:
+            rid, pid = topo.addr(cores[d], core)
+            ids.append(DstId(rid=rid, pnc=pid))
+        g.remote_dma_fused([RemoteDMATransfer(dst_ids=ids, dma_engine_mask=mask, remote_sem=T.sem[sem],
+                                              srcs=[buf_src], dsts=[buf_dst] * len(ids))], local_sem=T.sem[lsem])
+        return len(topo.engines(core, cores[dests[0]]))
+    wait("y", *ax)
+    Y.dma_start(T.xdo[:, :], T.xpb[0:128:16, :]).then_inc(T.sem.xo, 16)
+    wait("p", "xo", 16)
+    ne = send(T.xdo[:, :], T.xdi[r], "x%d" % r, "lx", nb)
+    wait("p", *vu)
+    send(T.uo[:, :], blk(T.ui, r), "w%d" % r, "lw", nb)
+    far = list(range(N - 1, r, -1))
+    if far:
+        wait("y", *vw)
+        Y.dma_start(T.mdo[:, :], blk(T.big, r)[0:128:16, :]).then_inc(T.sem.mo, 16)
+        wait("p", "mo", 16)
+        send(T.mdo[:, :], T.mdi[r], "m%d" % r, "lm", far)
+    wait("y", *acn)
+    Y.dma_start(T.cdo[:, :], blk(T.cnt, r)[0:128:16, :]).then_inc(T.sem.co, 16)
+    wait("p", "co", 16)
+    send(T.cdo[:, :], T.cdi[r], "c%d" % r, "lc", far + ([r - 1] if r else []))
+    wait("a", "xo", 16)
+    wait("a", *apy)
+    A.dma_start(blk(T.pay, 0)[0:128:16, :], T.xdo[:, :]).then_inc(T.sem["lx%d" % r], 16)
+    for d in range(r):
+        qn = "ya"[d % 2]
+        wait(qn, *pz)
+        wait(qn, "m%d" % d, ne)
+        eng[qn].dma_start(blk(T.big, d)[0:128:16, :], T.mdi[d]).then_inc(T.sem["ld%d" % d], 16)
+
+    kmin, kmax = max(0, 2 * r - 2), min(2 * N - 1, 2 * r + 3)
+    nk = kmax - kmin + 1
+    do("v", lambda: V.memset(T.s[:, :], 0))
+    ts(T.pfx[:, 0:32], T.io2[:, 0:32], 0.0, None, ALU.mult)
+    vsg = ts(T.sg[:, :], T.mg[:, :], gcol, None, ALU.is_equal, dep=[pio])
+    v = ts(T.tri0[:, :], T.mq[:, :], qcol, None, ALU.is_gt)
+    tt(T.tri[:, :], T.tri0[:, :], T.sg[:, :], ALU.mult, dep=[v, vsg])
+    ts(T.wb[:, :], T.sg[:, :], m0, 256.0, ALU.mult, ALU.mult)
+    v = ts(T.n0[:, 2:3], qcol, 8.0, None, ALU.is_ge)
+    ts(T.gl[:, 0:6], T.l2[:, 0:6], T.n0[:, 2:3], None, ALU.add, dep=[v, pio])
+    vcn = ts(T.gsr[:, :], T.g8[:, :], gcol, None, ALU.is_equal)
+
+    for e in nb:
+        wait("y", "x%d" % e, ne)
+        wait("y", *cp(blk(T.pay, slot[e]), blk(T.ui, e), dep=[("w%d" % e, ne)]))
+        Y.dma_start(blk(T.pay, slot[e])[0:128:16, :], T.xdi[e]).then_inc(T.sem["lx%d" % e], 16)
+        if e > r:
+            vcv = ts(blk(T.big, e), blk(T.ui, e), T.cu[:, 1:2], T.cu[:, 2:3], ALU.mult, ALU.add, dep=[acu])
+    cin = [d for d in range(min(N, r + 2)) if d != r]
+    for d in cin:
+        wait("y", *pcz)
+        wait("y", "c%d" % d, ne)
+        Y.dma_start(blk(T.cnt, d)[0:128:16, :], T.cdi[d]).then_inc(T.sem["lc%d" % d], 16)
+
+    vs = vcn
+    wait("v", *pz)
+    ka = max(0, kmax - 5)
+    for k in range(kmax + 1):
+        if k in (ka, kmax) and k:
+            a = 0 if k == ka else ka
+            b = a + a % 2
+            v = cp(T.lsc[:, b:b + k - a], T.s[:, 2 * a:2 * k:2], dep=[vs])
+            acf = act(T.cf[:, 16 * a:16 * k], T.cnt[:, 0:zeros].indirect(T.lsc[:, b:b + k - a]), ACTF.Copy, scale=m0,
+                      dep=[v, acn, pcz] + [("lc%d" % d, 16) for d in cin])
+        if k == kmax:
+            break
+        d = k // 2
+        win = T.big[:, 0:256 * d + 256]
+        off = T.s[:, 2 * k:2 * k + 1]
+        vs = ts(T.s[:, 2 * k + 2:2 * k + 18], win.indirect(off), m0, None, ALU.mult,
+                dep=[vs] + ([("ld%d" % d, 16)] if d < r else [vw]) + ([vcv] if d > r else []))
+    kl = 2 if r else 0
+    if r:
+        ts(T.lst[:, 0:2], T.s[:, 2 * kmin:2 * kmin + 4:2], 256 * (slot[r - 1] - (r - 1)), None, ALU.add, dep=[vs])
+    vl = ts(T.lst[:, kl:nk], T.s[:, 2 * (kmin + kl):2 * (kmin + nk):2], -256 * r, None, ALU.add, dep=[vs])
+    lst = T.lst[:, 0:nk]
+    m = 16 * nk
+    v2 = cp(T.v2[:, 0:m], T.pay[:, 0:256 * len(slot)].indirect(lst), dep=[vl] + [("lx%d" % d, 16) for d in slot])
+    vv = T.v2[:, 0:m:16]
+    ts(T.cab[:, 0:nk], vv, 4096, None, ALU.is_ge, dep=[v2])
+    vca = ts(T.cab[:, nk:2 * nk], vv, 8192, None, ALU.is_ge)
+    ts(T.ei[:, 0:nk], vv, 63, None, ALU.bitwise_and)
+    ve = ts(T.ei[:, nk:2 * nk], vv, 6, 63, ALU.logical_shift_right, ALU.bitwise_and)
+    vpx = do("v", lambda: V.tensor_tensor_scan(T.pfx[:, 1:1 + kmax], T.cf[:, 0:16 * kmax:16], T.cf[:, 0:16 * kmax:16], 0.0, ALU.add, ALU.max),
+             acf)
+    pp = T.pb1[:, 0:nk]
+    mm(pp, T.tri[:, :], T.cab[:, 0:nk], True, False, dep=[vca, vcn])
+    mm(pp, T.tri[:, :], T.cab[:, nk:2 * nk], False, False)
+    tp = mm(pp, T.wb[:, :], T.pfx[:, kmin:kmax + 1], False, True, dep=[vpx])
+
+    vo = {}
+
+    def onehot(kk):
+        vo[kk] = ts(T.oh[:, 64 * kk:64 * kk + 64], T.iot[:, :], T.pb1[:, kk:kk + 1], None, ALU.is_equal, dep=[tp])
+    v = ts(T.ef[:, 0:2 * nk], T.ei[:, 0:2 * nk], 1, None, ALU.add, dep=[ve])
+    v = tt(T.val[:, 0:2 * nk], T.ef[:, 0:2 * nk], T.cab[:, 0:2 * nk], ALU.mult, dep=[v])
+    vgv = tt(T.gsv[:, 0:m], T.val[:, 0:2 * nk].indirect(T.gl[:, 0:nk]), T.gsr[:, 0:m], ALU.mult, dep=[v])
+    yp = T.pb2[0:8, 0:32]
+    for kk in range(nk):
+        onehot(kk)
+        for mh in range(2):
+            x = mh * nk + kk
+            ty = mm(yp, T.gsv[:, 8 * x:8 * x + 8], T.oh[:, 64 * kk + 32 * mh:64 * kk + 32 * mh + 32], kk + mh == 0, kk + mh == nk,
+                    dep=[vo[kk], vgv])
+    vy = ts(T.ys[0:8, :], yp, -1.0, None, ALU.add, dep=[ty])
+    wait("y", *vy)
+    Y.dma_start(T.y[:, :], T.ys[0:8, :]).then_inc(T.sem.yo, 16)
+
+    wait("y", "yo", 16)
+    wait("p", "lx", ne)
+    wait("p", "lw", ne)
+    wait("p", "lc", ne)
+    if far:
+        wait("p", "lm", ne)
+    for name in ("v", "a", "t"):
+        wait("p", name, cnt[name])
+    wait("v", "p", cnt["p"])

@@ -5,39 +5,76 @@ ALU = AluOpType
 ACTF = ActivationFunctionType
 F, B, H, I4, U2 = "float32", "bfloat16", "float16", "int32", "uint16"
 SBUF = {
-    I4: "nxi:512 emi:512 ipi:8 qgi:8 v2:96 ei:16",
-    B: "syr:256 ones:128 zw:128 zw0:128 wx:128 c1:256 cc:256 tri:128 wb:128 cab:16 gsv:96 oh:384",
-    H: "nxh:512 emh:512 sela:128 pfx:32",
-    F: "ipf:8 qgf:8 hm:8 mq:128 mg:128 mi:128 io2:256 idw:256 rm:16 n0:8 cu:8 bias:24 sg:128 g8:96 gsr:96 l2:8 iot:64 "
-       "tri0:128 ab:4096 w0:256 w1:256 big:2304 cnt:2304 xpb:256 pay:768 cf:256 ef:16 val:16 ys:32",
-    U2: "uo:256 ui:2048 s:64 lst:8 lsc:24 gl:8",
+    I4: "nxi:512 emi:512 ipi:8 qgi:8 vi:8 si3:64 ei:16",
+    B: "ones:128 iob:128 jj:2048 wa0:128 wa1:128 wb0:128 wb1:128 rep:128 sg:128 sga:128 sgb:128 gt:128 lt:128 ee:24 gsv:96 oh:384",
+    H: "emh:512 sela:128",
+    F: "ipf:8 qgf:8 hm:8 mq:128 kq:128 mg:128 rm:16 n0:8 iot:40 iotb:40 tri0:128 tri1:128 big:1024 xe:1152 xo:1152 w0f:128 dg:128 "
+       "rs:128 md:128 ms:128 mk1:112 mk3:64 thr:8 g8:96 gsr:96 gsc:96 l2:8 g2:112 g3:64 sc1:112 sc3:64 cab:16 eef:24 ef:16 "
+       "tot:4 cin:32 ys:32",
+    U2: "s:48 lm0:8 ls2:8 gl:8",
 }
 SCRATCH = {w.split(":")[0]: ("sbuf", [128, int(w.split(":")[1])], d) for d, ws in SBUF.items() for w in ws.split()}
 SCRATCH.update({
-    "syi": ("sbuf", [128, 8, 32], I4),
+    "syi": ("sbuf", [128, 8, 32], I4), "syr": ("sbuf", [128, 16, 16], B),
     "selm": ("sbuf", [128, 8, 32], H), "tb": ("sbuf", [128, 32, 32], H),
-    "oi": ("sbuf", [128, 16, 16], I4), "oi2": ("sbuf", [128, 16, 16], I4),
-    "off": ("sbuf", [128, 16, 16], U2),
-    "mdo": ("dram", [128, 16], F), "mdi": ("dram", [8, 128, 16], F),
-    "cdo": ("dram", [128, 16], F), "cdi": ("dram", [8, 128, 16], F),
-    "xdo": ("dram", [128, 16], F), "xdi": ("dram", [8, 128, 16], F),
+    "oi": ("sbuf", [128, 4, 64], I4), "oi2": ("sbuf", [128, 4, 64], I4), "off": ("sbuf", [128, 4, 64], U2),
+    "mdo": ("dram", [128, 8], F), "mdi": ("dram", [8, 128, 8], F),
+    "pl": ("psum", [128, 8, 64], F),
 })
-SCRATCH.update({n: ("psum", [128, 512], F) for n in "pb0 pb1 pb2 pa0 pa1 pa2".split()})
-SEMAPHORES = ("v a t p ds dn0 dn1 de mo xo co yo lx lw lm lc".split()
-              + [s + str(r) for s in ("x", "w", "m", "c", "ld", "lx", "lc") for r in range(8)])
+SCRATCH.update({n: ("psum", [128, 512], F) for n in "pb px pq pt py".split()})
+SEMAPHORES = ("v a t p ds mo yo xh lx lw lm lc".split() + [s + str(t) for s in ("dn", "de") for t in range(4)]
+              + [s + str(r) for s in ("x", "w", "m", "c", "ld") for r in range(8)])
+CUT = 14
+
+
+def tellers(r):
+    m, out = r - 1, []
+    while m > 0:
+        out.append((m - 2, 2) if m >= 3 else (0, m - 1))
+        m -= 3
+    return out
 
 
 def rank_program(g, core, T, topo):
-    r = T.rank_of(core)
-    if r is None:
-        return
     cores = T.cores
     N = len(cores)
+
+    def transfer(src, dst, sem, to, engines):
+        ids = []
+        for c in to:
+            rid, pid = topo.addr(c, core)
+            ids.append(DstId(rid=rid, pnc=pid))
+        return RemoteDMATransfer(dst_ids=ids, dma_engine_mask=sum(1 << e for e in engines), remote_sem=T.sem[sem],
+                                 srcs=[src], dsts=[dst] * len(ids))
+
+    def helpers(d):
+        return [c for c in topo.cores_of(cores[d]) if topo.die(c) != topo.die(cores[d])][:2]
+
+    def blk(buf, d, n=128):
+        return buf[:, n * d:n * d + n]
+
+    def xoff(d):
+        return 384 * (d % 3)
+
+    def xtab(d, eo, k=0):
+        return blk(T.xo, 3 * (d % 3) + k) if eo else blk(T.xe, d)
+    r = T.rank_of(core)
+    if r is None:
+        for d in range(N):
+            if core in helpers(d):
+                to = [cores[e] for e in (d + 1, d - 1) if 0 <= e < N]
+                tab, out = xtab(d, helpers(d).index(core)), topo.engines(core, to[0])
+                g.wait_ge(T.sem.xh, len(topo.engines(cores[d], core)) // 2)
+                g.remote_dma_fused([transfer(tab, tab, "x%d" % d, to, out)], local_sem=T.sem.lx)
+                g.wait_ge(T.sem.lx, len(out))
+        return
     V, A, P, Y = g.vector, g.scalar, g.tensor, g.sync
     eng = {"v": V, "a": A, "t": P, "p": g, "y": Y}
     cnt = {"v": 0, "a": 0, "t": 0, "p": 0}
     seen = {}
     nb = [d for d in (r + 1, r - 1) if 0 <= d < N]
+    near = sorted(nb + [r])
+    nu = len(near)
 
     def wait(q, name, val):
         if val > seen.get((q, name), 0):
@@ -60,49 +97,44 @@ def rank_program(g, core, T, topo):
     def cp(out, in_, dep=()):
         return do("v", lambda: V.tensor_copy(out, in_), *dep)
 
+    def fill(out, x, dep=()):
+        return do("v", lambda: V.memset(out, x), *dep)
+
+    def scan(out, d0, d1, op0, op1, dep=()):
+        return do("v", lambda: V.tensor_tensor_scan(out, d0, d1, 0.0, op0, op1), *dep)
+
     def mm(out, lh, rh, start, stop, dep=()):
         return do("t", lambda: P.matmul(out, lh, rh, start, stop), *dep)
 
     def act(out, in_, func, dep=(), **kw):
         return do("a", lambda: A.activation(out, in_, func, **kw), *dep)
 
-    def blk(buf, d):
-        return buf[:, 256 * d:256 * d + 256]
-    hf = [slice(0, 128), slice(128, 256)]
-    slot = {r: 0}
-    for d in nb:
-        slot[d] = len(slot)
-
     for h in range(2):
         (Y, A)[h].dma_start(T.syi[0:1, 4 * h:4 * h + 4, :], T.sy[h::2, :]).then_inc(T.sem.ds, 16)
     for t in range(4):
-        (Y, A)[t % 2].dma_start(T.nxi[:, 128 * t:128 * t + 128], T.nx[2 * t:2 * t + 2, :]).then_inc(T.sem["dn%d" % (t // 2)], 16)
+        (Y, A)[t % 2].dma_start(blk(T.nxi, t), T.nx[2 * t:2 * t + 2, :]).then_inc(T.sem["dn%d" % t], 16)
+    wait("y", "dn2", 16)
     for t in range(4):
-        (Y, A)[t % 2].dma_start(T.emi[:, 128 * t:128 * t + 128], T.em[2 * t:2 * t + 2, :]).then_inc(T.sem.de, 16)
-    DS, DN, DE = ("ds", 32), [("dn0", 32), ("dn1", 32)], ("de", 64)
+        Y.dma_start(blk(T.emi, t), T.em[2 * t:2 * t + 2, :]).then_inc(T.sem["de%d" % t], 16)
 
     def iota(ap, pattern, base, cm):
         return do("p", lambda: g.iota(ap, pattern, base, cm, allow_small_or_imprecise_dtypes=True))
     iota(T.ipi[:, 0:1], [[0, 1]], 0, 1)
     iota(T.ipf[:, 0:1], [[0, 1]], 0, 1)
     pq = iota(T.rm[:, 0:16], [[1, 16]], 0, 0)
-    pc = iota(T.mi[:, :], [[1, 128]], 0, 0)
-    pi2 = iota(T.io2[:, :], [[1, 256]], 0, 0)
+    pib = iota(T.iob[:, :], [[1, 128]], 0, 0)
     iota(T.mq[:, :], [[0, 8], [1, 16]], 0, 0)
-    iota(T.mg[:, :], [[1, 8], [0, 16]], 0, 0)
-    iota(T.iot[:, 0:32], [[1, 32]], 32 * r, 0)
-    iota(T.iot[:, 32:64], [[1, 32]], 32 * r - 1, 0)
-    iota(T.l2[:, 0:6], [[2, 6]], 0, 0)
-    pio = iota(T.g8[:, :], [[0, 12], [1, 8]], 0, 0)
-    pz = pio
-    if r:
-        pz = iota(T.big[:, 0:256 * r], [[0, 256 * r]], 0, 0)
-    zeros = 256 * min(N, r + 2)
-    pcz = iota(T.cnt[:, 0:zeros], [[0, zeros]], 0, 0)
+    pmg = iota(T.mg[:, :], [[1, 8], [0, 16]], 0, 0)
+    iota(T.kq[:, :], [[0, 8], [1, 16]], 0, 0)
+    iota(T.iot[:, 0:33], [[1, 33]], 32 * r - 1, 0)
+    iota(T.l2[:, 0:6], [[2, 6]], 4 if r else 0, 0)
+    iota(T.g8[:, :], [[0, 12], [1, 8]], 0, 0)
+    pz = iota(blk(T.xe, near[-1] + 1), [[0, 128]], 0, 0)
+    if r > 1:
+        iota(T.xe[:, 0:128 * (r - 1)], [[0, 128 * (r - 1)]], 0, 0)
+        pz = iota(T.big[:, 0:128 * (r - 1)], [[0, 128 * (r - 1)]], 0, 0)
 
-    CB = 129
-    BZ = 2047.0 - 4096 * CB
-    von = do("v", lambda: V.memset(T.ones[:, :], 1.0))
+    von = fill(T.ones[:, :], 1.0)
     ts(T.qgi[:, 0:1], T.ipi[:, 0:1], 15, None, ALU.bitwise_and, dep=[pq])
     ts(T.qgi[:, 2:3], T.ipi[:, 0:1], 63, None, ALU.bitwise_and)
     v = ts(T.qgi[:, 1:2], T.ipi[:, 0:1], 4, None, ALU.logical_shift_right)
@@ -111,220 +143,215 @@ def rank_program(g, core, T, topo):
     ts(T.hm[:, 1:2], pcol, 64.0, None, ALU.is_ge)
     vqg = cp(T.qgf[:, 0:3], T.qgi[:, 0:3], dep=[v])
     vrm = ts(T.rm[:, :], T.rm[:, :], qcol, None, ALU.is_equal, dep=[vqg])
-    vg16 = tt(T.qgf[:, 3:4], pcol, qcol, ALU.subtract)
-    vbi = ts(T.bias[:, 0:16], T.rm[:, :], BZ, None, ALU.mult, dep=[vrm])
-    vwx = ts(T.wx[:, :], T.mi[:, :], pcol, 4096.0, ALU.is_equal, ALU.mult, dep=[pc])
-    v = ts(T.zw[:, :], T.mi[:, :], T.qgf[:, 3:4], 1.0 / 256, ALU.is_equal, ALU.mult, dep=[vg16])
-    vzw = ts(T.zw0[:, :], T.zw[:, :], m0, None, ALU.mult, dep=[v])
-    for seg in range(2):
-        mm(T["pa%d" % seg][:, 0:128], T.ones[0:1, :], T.ones[0:1, :], True, False, dep=[von])
-    for seg in range(2):
-        vrow = cp(T.syr[0:1, seg:256:2], T.syi[0:1, :, 16 * seg:16 * seg + 16], dep=[DS])
-    tbc = mm(T.pb0[:, 0:256], T.ones[0:1, :], T.syr[0:1, :], True, True, dep=[von, vrow])
-    act(T.bias[:, 16:17], m0, ACTF.Copy, scale=float(128 * (2 * r + 1)), dep=[vrm])
-    act(T.bias[:, 18:19], m0, ACTF.Copy, scale=-17 * CB / 256.0)
-    act(T.cu[:, 0:1], m0, ACTF.Identity, scale=255.0, bias=1.0)
-    act(T.cu[:, 1:2], m0, ACTF.Identity, scale=-255.0 / 256, bias=1.0)
-    acu = act(T.cu[:, 2:3], m0, ACTF.Copy, scale=float(128 * (2 * r + 3)))
-    aid = act(T.idw[:, :], T.io2[:, :], ACTF.Identity, scale=m0, bias=T.bias[:, 16:17], dep=[acu, pi2])
-
-    def cast(h):
-        return cp(T.nxh[:, 256 * h:256 * h + 256], T.nxi[:, 256 * h:256 * h + 256], dep=[DN[h]])
-    vn = [cast(0)]
-    for h in range(2):
-        for seg in range(2):
-            vsm = ts(T.selm[:, seg:8:2, 16 * h:16 * h + 16], T.pb0[:, 128 * h + seg:128 * h + 128:2], T.qgf[:, 2:3], T.hm[:, h:h + 1],
-                     ALU.is_equal, ALU.mult, dep=[tbc])
-    vn.append(cast(1))
-    hs = [slice(0, 64), slice(64, 128)]
-    for h in range(2):
-        vsa = ts(T.sela[hs[h], :], T.pb0[hs[h], 128 * h:128 * h + 128], T.qgf[hs[h], 2:3], None, ALU.is_equal)
+    jd = {}
+    for j in (0, 7, 15, 6, 14, 5, 13, 4, 12, 3):
+        jd[j] = act(blk(T.jj, j), T.iob[:, :], ACTF.Copy, scale=T.rm[:, j:j + 1], dep=[vrm, pib])
+    for j in (11, 2, 10, 1, 9, 8):
+        jd[j] = ts(blk(T.jj, j), T.iob[:, :], T.rm[:, j:j + 1], None, ALU.mult, dep=[vrm, pib])
+    acol = act(T.n0[:, 0:1], m0, ACTF.Identity, scale=128.0, bias=128.0 * r)
+    vsg = ts(T.sg[:, :], T.mg[:, :], gcol, None, ALU.is_equal, dep=[pmg])
+    for eo in range(2):
+        vrow = cp(T.syr[0:1, eo:16:2, :], T.syi[0:1, :, eo:32:2], dep=[("ds", 32)])
+    tbc = mm(T.pb[:, 0:256], T.ones[0:1, :], T.syr[0:1, :, :], True, True, dep=[von, vrow])
+    arep = act(T.rep[:, :], T.sg[:, :], ACTF.Copy, scale=T.rm[:, CUT // 2:CUT // 2 + 1], dep=[vsg])
     vt = []
-    for u in range(2):
-        for h in range(2):
-            v = ts(T.tb[:, 16 * u:16 * u + 16, 16 * h:16 * h + 16], T.nxh[:, 256 * u:256 * u + 256], T.hm[:, h:h + 1], None, ALU.mult,
-                   dep=[vn[u]])
-        vt.append(v)
-    vem = ts(T.emh[:, :], T.emi[:, :], -2048, None, ALU.add, dep=[DE])
-
     for t in range(4):
-        for seg in range(2):
-            txn = mm(T.pb2[32 * t:32 * t + 32, hf[seg]], T.selm[:, 2 * t + seg, :], T.nxh[:, 128 * t:128 * t + 128],
-                     True, True, dep=[vsm, vn[t // 2]])
+        for h in range(2):
+            v = ts(T.tb[:, 8 * t:8 * t + 8, 16 * h:16 * h + 16], blk(T.nxi, t), T.hm[:, h:h + 1], None, ALU.mult,
+                   dep=[("dn%d" % t, 16)])
+        vt.append(v)
+        if t == 0:
+            for h in range(2):
+                hs = slice(64 * h, 64 * h + 64)
+                vsa = ts(T.sela[hs, :], T.pb[hs, 128 * h:128 * h + 128], T.qgf[hs, 2:3], None, ALU.is_equal, dep=[tbc])
+
     for t in range(4):
         for c in range(8):
-            tof = mm(T.pb1[32 * t:32 * t + 32, c:256:8], T.tb[:, 8 * t + c, :], T.sela[:, 32 * t:32 * t + 32], True, True,
-                     dep=[vt[t // 2], vsa])
-    ac1 = act(T.c1[:, :], T.pb2[:, 0:256], ACTF.Copy, scale=1.0 / 128, bias=CB - 0.498, dep=[txn])
-    tpx = []
-    for seg in range(2):
-        for t in range(4):
-            mm(T["pa%d" % seg][32 * t:32 * t + 32, 0:128], T.selm[:, 2 * t + seg, :], T.emh[:, 128 * t:128 * t + 128], False, False,
-               dep=[vem])
-        tpx.append(mm(T["pa%d" % seg][:, 0:128], T.wx[:, :], T.c1[:, hf[seg]], False, True, dep=[vwx, ac1]))
-    aa = {}
-    for i in [15, 14, 13, 0, 12, 11, 10, 9, 8, 7, 6, 5, 4, 3, 2, 1]:
-        for seg in range(2):
-            o = T.ab[:, 256 * i + 128 * seg:256 * i + 128 * seg + 128] if i else T.xpb[:, hf[seg]]
-            aa[i, seg] = act(o, T["pa%d" % seg][:, 0:128], ACTF.Identity, dep=[tpx[seg], vbi], scale=T.rm[:, i:i + 1],
-                             bias=T.bias[:, i:i + 1])
-    ax = aa[0, 1]
+            tof = mm(T.pl[32 * t:32 * t + 32, 0:4, c:64:8], T.tb[:, 8 * t + c, :], T.sela[:, 32 * t:32 * t + 32], True, True,
+                     dep=[vt[t], vsa])
+    last = {}
 
-    vof = {}
-
-    def lists(lo, hi, part):
-        a, b = 16 * lo, 16 * hi
+    def lists(k, part):
+        cs = slice(16 * k, 16 * k + 16)
         if part == 0:
-            vof["x"] = cp(T.oi[:, lo:hi, :], T.pb1[:, a:b], dep=[tof])
+            last["x"] = cp(T.oi[:, :, cs], T.pl[:, 0:4, cs], dep=[tof])
         elif part == 1:
-            vof["x"] = ts(T.oi2[:, lo:hi, :], T.oi[:, lo:hi, :], 127, None, ALU.bitwise_and, dep=[vof["x"]])
+            last["x"] = ts(T.oi2[:, :, cs], T.oi[:, :, cs], 127, None, ALU.bitwise_and, dep=[last["x"]])
         else:
-            cp(T.off[:, lo:hi, 0:8], T.oi2[:, lo:hi, 0:8], dep=[vof["x"]])
-            x = ts(T.off[:, lo:hi, 8:16], T.oi2[:, lo:hi, 8:16], 128, None, ALU.add)
-            for i in range(lo, hi):
-                vof[i] = x
-    todo = [(lo, hi, part) for lo, hi in [(12, 16), (8, 12), (0, 8)] for part in range(3)]
-    for _ in range(3):
-        lists(*todo.pop(0))
+            last[k] = cp(T.off[:, :, cs], T.oi2[:, :, cs], dep=[last["x"]])
 
-    prev, vw = T.idw[:, :], aid
-    for i in range(15, -1, -1):
-        o = T["w%d" % (i % 2)][:, :] if i else blk(T.big, r)
-        if i == 15:
-            for seg in range(2):
-                vw = tt(o[:, hf[seg]], prev.indirect(T.off[:, i, 8 * seg:8 * seg + 8]),
-                        T.ab[:, 256 * i + 128 * seg:256 * i + 128 * seg + 128], ALU.add, dep=[vof[i], aid, aa[i, seg]])
-        elif i:
-            vw = tt(o, prev.indirect(T.off[:, i, :]), T.ab[:, 256 * i:256 * i + 256], ALU.add, dep=[vof[i], vw, aa[i, 1]])
-        else:
-            vw = cp(o, prev.indirect(T.off[:, i, :]), dep=[vof[i], vw])
-        prev = o
-        if todo:
-            lists(*todo.pop(0))
-    vu = ts(T.uo[:, :], blk(T.big, r), T.bias[:, 16:17], T.cu[:, 0:1], ALU.subtract, ALU.mult, dep=[vw, acu])
-    pcn = T.pa2[:, 0:256]
-    mm(pcn, T.zw0[:, :], T.c1[:, :], True, False, dep=[vzw])
-    acc = act(T.cc[:, :], blk(T.big, r), ACTF.Copy, scale=1.0 / 4096, bias=CB - 0.5 + 1.0 / 8192, dep=[vw])
-    tcn = mm(pcn, T.zw[:, :], T.cc[:, :], False, True, dep=[acc])
-    acn = act(blk(T.cnt, r), pcn, ACTF.Identity, bias=T.bias[:, 18:19], dep=[tcn, pcz, acu])
-    apy = act(blk(T.pay, 0), blk(T.big, r), ACTF.Copy)
+    def entries(t):
+        v = ts(blk(T.emh, t), blk(T.emi, t), -2048, 1.0 / 4096, ALU.add, ALU.mult, dep=[("de%d" % t, 16)])
+        for eo in range(2):
+            o, lh = T.px[32 * t:32 * t + 32, 128 * eo:128 * eo + 128], T.selm[:, 2 * t + eo, :]
+            for h in range(2):
+                mm(o, lh, T.tb[:, 8 * t:8 * t + 8, 16 * h:16 * h + 16], h == 0, False, dep=[last["m"]])
+            last["e"] = mm(o, lh, blk(T.emh, t), False, True, dep=[v])
+
+    def table(eo):
+        last["t"] = act(xtab(r, eo), blk(T.px, eo), ACTF.Copy, scale=4096.0, bias=2048.0 + (0 if eo else 4096.0 * xoff(r)),
+                        dep=[last["e"]])
+
+    def diag():
+        ts(T.dg[:, :], T.mq[:, :], qcol, None, ALU.is_equal)
+
+    def restart():
+        last["c"] = ts(T.rs[:, :], T.mq[:, :], 0.0, None, ALU.is_gt)
+    for h in range(2):
+        last["m"] = ts(T.selm[:, :, 16 * h:16 * h + 16], T.sela[:, :], T.hm[:, h:h + 1], None, ALU.mult, dep=[vsa])
+    for k in (3, 2):
+        for part in range(3):
+            lists(k, part)
+    vfill = ([(lists, 1, part) for part in range(3)] + [(entries, t) for t in range(4)] + [(lists, 0, part) for part in range(3)]
+             + [(diag,), (restart,)])
+    afill = {10: (table, 0), 11: (table, 1)}
+
+    prev = [(blk(T.jj, j), jd[j]) for j in (CUT // 2, 0)]
+    for n in range(32 - CUT):
+        for ch, i in ((1, 31 - n), (0, CUT - n)):
+            if not 0 <= i < (32 if ch else CUT):
+                continue
+            win, dw = prev[ch]
+            o = T["w%s%d" % ("ab"[ch], i % 2)][:, :]
+            c = 8 * (i % 16 // 2)
+            src = win.indirect(T.off[:, 2 * (i % 2) + i // 16, c:c + 8])
+            dep = [last[i % 16 // 4], dw]
+            if i % 2 or i == CUT:
+                dw = act(o, src, ACTF.Copy, dep=dep)
+                if n in afill:
+                    afill[n][0](*afill[n][1:])
+            else:
+                dw = tt(o, src, blk(T.jj, i // 2), ALU.add, dep=dep + [jd[i // 2]]) if i else cp(o, src, dep=dep)
+                if vfill:
+                    f = vfill.pop(0)
+                    f[0](*f[1:])
+            prev[ch] = (o, dw)
+            if i == 0:
+                trep = mm(T.pb[:, 0:128], T.rep[:, :], o, True, True, dep=[arep, dw])
+            if i == CUT + 2:
+                aw0 = act(T.w0f[:, :], prev[0][0], ACTF.Identity, bias=T.n0[:, 0:1], dep=[prev[0][1], acol])
+    v = tt(T.md[:, :], T.pb[:, 0:128], T.dg[:, :], ALU.mult, dep=[trep, last["c"]])
+    v = scan(T.ms[:, :], T.rs[:, :], T.md[:, :], ALU.mult, ALU.add, dep=[v])
+    v = cp(T.lm0[:, :], T.ms[:, 15:128:16], dep=[v])
+    vw = tt(blk(T.big, r), prev[1][0].indirect(T.lm0[:, :]), T.w0f[:, :], ALU.add, dep=[v, prev[1][1], aw0])
 
     def send(buf_src, buf_dst, sem, lsem, dests):
-        mask = topo.mask(core, cores[dests[0]])
-        ids = []
-        for d in dests:
-            rid, pid = topo.addr(cores[d], core)
-            ids.append(DstId(rid=rid, pnc=pid))
-        g.remote_dma_fused([RemoteDMATransfer(dst_ids=ids, dma_engine_mask=mask, remote_sem=T.sem[sem],
-                                              srcs=[buf_src], dsts=[buf_dst] * len(ids))], local_sem=T.sem[lsem])
-        return len(topo.engines(core, cores[dests[0]]))
-    wait("y", *ax)
-    Y.dma_start(T.xdo[:, :], T.xpb[0:128:16, :]).then_inc(T.sem.xo, 16)
-    wait("p", "xo", 16)
-    ne = send(T.xdo[:, :], T.xdi[r], "x%d" % r, "lx", nb)
-    wait("p", *vu)
-    send(T.uo[:, :], blk(T.ui, r), "w%d" % r, "lw", nb)
-    far = list(range(N - 1, r, -1))
+        g.remote_dma_fused([transfer(buf_src, buf_dst, sem, [cores[d] for d in dests], topo.engines(core, cores[dests[0]]))],
+                           local_sem=T.sem[lsem])
+    ne = len(topo.engines(core, cores[nb[0]]))
+    on = topo.engines(core, helpers(r)[0])
+    wait("p", *last["t"])
+    g.remote_dma_fused([transfer(xtab(r, eo), xtab(r, eo), "xh", [c], on[eo * len(on) // 2:(eo + 1) * len(on) // 2])
+                        for eo, c in enumerate(helpers(r))], local_sem=T.sem.lx)
+    wait("p", *vw)
+    send(blk(T.big, r), blk(T.big, r), "w%d" % r, "lw", nb[:1])
+    far = list(range(N - 1, r + 1, -1))
     if far:
         wait("y", *vw)
         Y.dma_start(T.mdo[:, :], blk(T.big, r)[0:128:16, :]).then_inc(T.sem.mo, 16)
         wait("p", "mo", 16)
         send(T.mdo[:, :], T.mdi[r], "m%d" % r, "lm", far)
-    wait("y", *acn)
-    Y.dma_start(T.cdo[:, :], blk(T.cnt, r)[0:128:16, :]).then_inc(T.sem.co, 16)
-    wait("p", "co", 16)
-    send(T.cdo[:, :], T.cdi[r], "c%d" % r, "lc", far + ([r - 1] if r else []))
-    wait("a", "xo", 16)
-    wait("a", *apy)
-    A.dma_start(blk(T.pay, 0)[0:128:16, :], T.xdo[:, :]).then_inc(T.sem["lx%d" % r], 16)
-    for d in range(r):
+    if nb[1:]:
+        send(blk(T.big, r), blk(T.big, r), "w%d" % r, "lw", nb[1:])
+    for d in range(r - 1):
         qn = "ya"[d % 2]
         wait(qn, *pz)
         wait(qn, "m%d" % d, ne)
         eng[qn].dma_start(blk(T.big, d)[0:128:16, :], T.mdi[d]).then_inc(T.sem["ld%d" % d], 16)
+    for d in [r] + nb:
+        for k in (1, 2):
+            ax = act(xtab(d, 1, k), xtab(d, 1), ACTF.Copy, dep=[last["t"] if d == r else ("x%d" % d, 2 * ne)])
 
-    kmin, kmax = max(0, 2 * r - 2), min(2 * N - 1, 2 * r + 3)
-    nk = kmax - kmin + 1
-    do("v", lambda: V.memset(T.s[:, :], 0))
-    ts(T.pfx[:, 0:32], T.io2[:, 0:32], 0.0, None, ALU.mult)
-    vsg = ts(T.sg[:, :], T.mg[:, :], gcol, None, ALU.is_equal, dep=[pio])
-    v = ts(T.tri0[:, :], T.mq[:, :], qcol, None, ALU.is_gt)
-    tt(T.tri[:, :], T.tri0[:, :], T.sg[:, :], ALU.mult, dep=[v, vsg])
-    ts(T.wb[:, :], T.sg[:, :], m0, 256.0, ALU.mult, ALU.mult)
-    v = ts(T.n0[:, 2:3], qcol, 8.0, None, ALU.is_ge)
-    ts(T.gl[:, 0:6], T.l2[:, 0:6], T.n0[:, 2:3], None, ALU.add, dep=[v, pio])
-    vcn = ts(T.gsr[:, :], T.g8[:, :], gcol, None, ALU.is_equal)
+    nc = nu + 1
+    m = 4 * nc
+    n0 = T.n0[:, 1:2]
+    fill(T.s[:, 0:16], 0)
+    fill(T.ee[:, :], 0.0)
+    fill(T.eef[:, :], 0.0)
+    fill(T.mk1[:, :], 0.0, dep=[pz])
+    fill(T.kq[:, 0:128:16], 16.0)
+    ts(n0, m0, -1.0, 1.0, ALU.mult, ALU.add)
+    ts(T.n0[:, 2:3], m0, 16.0, qcol, ALU.mult, ALU.add)
+    v = ts(T.n0[:, 3:4], qcol, 8.0, None, ALU.is_ge)
+    ts(T.gsr[:, :], T.g8[:, :], gcol, None, ALU.is_equal)
+    for u in range(nc):
+        d = near[0] - 1 + u
+        for k in range(2):
+            a, b = (4096.0 * (xoff(e) + 128 * (k + 1)) for e in (d, d + 1))
+            ts(T.thr[:, 4 * k + u:4 * k + u + 1], m0, b - a, a, ALU.mult, ALU.add)
+        for o in (blk(T.mk1, 2 * u, 16), blk(T.mk3, u, 16)):
+            if 0 < u < nu:
+                cp(o, T.dg[:, 0:16], dep=[v])
+            else:
+                ts(o, T.dg[:, 0:16], n0 if u else m0, None, ALU.mult, dep=[v])
+    ts(T.gl[:, 0:6], T.l2[:, 0:6], T.n0[:, 3:4], None, ALU.add)
+    ts(T.tri0[:, :], T.kq[:, :], T.n0[:, 2:3], None, ALU.is_gt)
+    v = ts(T.tri1[:, :], T.kq[:, :], T.n0[:, 2:3], None, ALU.is_lt)
+    ts(T.sga[:, :], T.sg[:, :], n0, None, ALU.mult)
+    ts(T.sgb[:, :], T.sg[:, :], m0, None, ALU.mult)
+    tt(T.lt[:, :], T.tri0[:, :], T.sg[:, :], ALU.mult, dep=[v])
+    vs = tt(T.gt[:, :], T.tri1[:, :], T.sg[:, :], ALU.mult)
 
-    for e in nb:
-        wait("y", "x%d" % e, ne)
-        wait("y", *cp(blk(T.pay, slot[e]), blk(T.ui, e), dep=[("w%d" % e, ne)]))
-        Y.dma_start(blk(T.pay, slot[e])[0:128:16, :], T.xdi[e]).then_inc(T.sem["lx%d" % e], 16)
-        if e > r:
-            vcv = ts(blk(T.big, e), blk(T.ui, e), T.cu[:, 1:2], T.cu[:, 2:3], ALU.mult, ALU.add, dep=[acu])
-    cin = [d for d in range(min(N, r + 2)) if d != r]
-    for d in cin:
-        wait("y", *pcz)
-        wait("y", "c%d" % d, ne)
-        Y.dma_start(blk(T.cnt, d)[0:128:16, :], T.cdi[d]).then_inc(T.sem["lc%d" % d], 16)
+    for d in range(near[-1] + 1):
+        vs = cp(T.s[:, 2 * d + 2:2 * d + 18], T.big[:, 0:128 * d + 128].indirect(T.s[:, 2 * d:2 * d + 1]),
+                dep=[vs] + ([] if d == r else [("w%d" % d, ne)] if d in near else [("ld%d" % d, 16)]))
+    a, n1, n3 = 2 * near[0], 32 * nc - 16, 16 * nc
+    v = tt(T.g2[:, 0:n1], T.xe[:, 0:128 * (near[-1] + 2)].indirect(T.s[:, a:a + 2 * nc - 1]), T.mk1[:, 0:n1], ALU.mult, dep=[vs, ax])
+    v = scan(T.sc1[:, 0:n1], T.rs[:, 0:n1], T.g2[:, 0:n1], ALU.mult, ALU.add, dep=[v])
+    ve, vo = T.sc1[:, 15:n1:32], T.sc3[:, 15:n3:16]
+    v = ts(T.ls2[:, 0:nc], ve, 1.0 / 4096, 1.0 / 8192 - 0.5, ALU.mult, ALU.add, dep=[v])
+    vi = cp(T.vi[:, 0:nc], ve)
+    v = tt(T.g3[:, 0:n3], T.xo[:, 0:384 * nu].indirect(T.ls2[:, 0:nc]), T.mk3[:, 0:n3], ALU.mult, dep=[v])
+    for k in range(2):
+        tt(T.cab[:, k:m:4], ve, T.thr[:, 4 * k:4 * k + nc], ALU.is_ge)
+    scan(T.sc3[:, 0:n3], T.rs[:, 0:n3], T.g3[:, 0:n3], ALU.mult, ALU.add, dep=[v])
+    v = scan(T.si3[:, 0:n3], T.rs[:, 0:n3], T.g3[:, 0:n3], ALU.mult, ALU.add)
 
-    vs = vcn
-    wait("v", *pz)
-    ka = max(0, kmax - 5)
-    for k in range(kmax + 1):
-        if k in (ka, kmax) and k:
-            a = 0 if k == ka else ka
-            b = a + a % 2
-            v = cp(T.lsc[:, b:b + k - a], T.s[:, 2 * a:2 * k:2], dep=[vs])
-            acf = act(T.cf[:, 16 * a:16 * k], T.cnt[:, 0:zeros].indirect(T.lsc[:, b:b + k - a]), ACTF.Copy, scale=m0,
-                      dep=[v, acn, pcz] + [("lc%d" % d, 16) for d in cin])
-        if k == kmax:
-            break
-        d = k // 2
-        win = T.big[:, 0:256 * d + 256]
-        off = T.s[:, 2 * k:2 * k + 1]
-        vs = ts(T.s[:, 2 * k + 2:2 * k + 18], win.indirect(off), m0, None, ALU.mult,
-                dep=[vs] + ([("ld%d" % d, 16)] if d < r else [vw]) + ([vcv] if d > r else []))
-    kl = 2 if r else 0
-    if r:
-        ts(T.lst[:, 0:2], T.s[:, 2 * kmin:2 * kmin + 4:2], 256 * (slot[r - 1] - (r - 1)), None, ALU.add, dep=[vs])
-    vl = ts(T.lst[:, kl:nk], T.s[:, 2 * (kmin + kl):2 * (kmin + nk):2], -256 * r, None, ALU.add, dep=[vs])
-    lst = T.lst[:, 0:nk]
-    m = 16 * nk
-    v2 = cp(T.v2[:, 0:m], T.pay[:, 0:256 * len(slot)].indirect(lst), dep=[vl] + [("lx%d" % d, 16) for d in slot])
-    vv = T.v2[:, 0:m:16]
-    ts(T.cab[:, 0:nk], vv, 4096, None, ALU.is_ge, dep=[v2])
-    vca = ts(T.cab[:, nk:2 * nk], vv, 8192, None, ALU.is_ge)
-    ts(T.ei[:, 0:nk], vv, 63, None, ALU.bitwise_and)
-    ve = ts(T.ei[:, nk:2 * nk], vv, 6, 63, ALU.logical_shift_right, ALU.bitwise_and)
-    vpx = do("v", lambda: V.tensor_tensor_scan(T.pfx[:, 1:1 + kmax], T.cf[:, 0:16 * kmax:16], T.cf[:, 0:16 * kmax:16], 0.0, ALU.add, ALU.max),
-             acf)
-    pp = T.pb1[:, 0:nk]
-    mm(pp, T.tri[:, :], T.cab[:, 0:nk], True, False, dep=[vca, vcn])
-    mm(pp, T.tri[:, :], T.cab[:, nk:2 * nk], False, False)
-    tp = mm(pp, T.wb[:, :], T.pfx[:, kmin:kmax + 1], False, True, dep=[vpx])
+    def numbers(eo, src, dep):
+        ts(T.ei[:, 2 * eo:m:4], src, 63, None, ALU.bitwise_and, dep=[dep])
+        return ts(T.ei[:, 2 * eo + 1:m:4], src, 6, 63, ALU.logical_shift_right, ALU.bitwise_and)
+    numbers(0, T.vi[:, 0:nc], vi)
+    for k in range(2):
+        vc = ts(T.cab[:, 2 + k:m:4], vo, 4096.0 * 128 * (k + 1), None, ALU.is_ge, dep=[v])
+    v = numbers(1, T.si3[:, 15:n3:16], v)
+    vee = scan(T.ee[:, 1:m + 1], T.cab[:, 0:m], T.cab[:, 0:m], ALU.add, ALU.max, dep=[vc])
+    told = [d for d in range(N - 1, r, -1) if r in [s for s, _ in tellers(d)]]
+    if told:
+        mm(T.pt[:, 0:nu], T.sga[:, :], T.ee[:, 8:m + 1:4], True, False, dep=[vee])
+        ttot = mm(T.pt[:, 0:nu], T.sgb[:, :], T.ee[:, 4:m - 3:4], False, True)
+    mm(T.pq[:, 0:nc], T.gt[:, :], T.ee[:, 0:m:4], True, False, dep=[vee])
+    tp = mm(T.pq[:, 0:nc], T.lt[:, :], T.ee[:, 4:m + 1:4], False, True)
+    if told:
+        wait("p", *act(T.tot[:, 0:nu], T.pt[:, 0:nu], ACTF.Copy, dep=[ttot]))
+        send(T.tot[:, 0:nu], T.cin[:, 4 * r:4 * r + nu], "c%d" % r, "lc", told)
 
-    vo = {}
-
-    def onehot(kk):
-        vo[kk] = ts(T.oh[:, 64 * kk:64 * kk + 64], T.iot[:, :], T.pb1[:, kk:kk + 1], None, ALU.is_equal, dep=[tp])
-    v = ts(T.ef[:, 0:2 * nk], T.ei[:, 0:2 * nk], 1, None, ALU.add, dep=[ve])
-    v = tt(T.val[:, 0:2 * nk], T.ef[:, 0:2 * nk], T.cab[:, 0:2 * nk], ALU.mult, dep=[v])
-    vgv = tt(T.gsv[:, 0:m], T.val[:, 0:2 * nk].indirect(T.gl[:, 0:nk]), T.gsr[:, 0:m], ALU.mult, dep=[v])
-    yp = T.pb2[0:8, 0:32]
-    for kk in range(nk):
-        onehot(kk)
-        for mh in range(2):
-            x = mh * nk + kk
-            ty = mm(yp, T.gsv[:, 8 * x:8 * x + 8], T.oh[:, 64 * kk + 32 * mh:64 * kk + 32 * mh + 32], kk + mh == 0, kk + mh == nk,
-                    dep=[vo[kk], vgv])
+    u0 = 1 if r else 0
+    nx_ = 2 * (nc - u0)
+    scan(T.eef[:, 1:m + 1], T.cab[:, 0:m], T.cab[:, 0:m], ALU.add, ALU.max)
+    ts(T.ef[:, 0:m], T.ei[:, 0:m], 1, None, ALU.add, dep=[v])
+    v = tt(T.gsc[:, 0:16 * nx_], T.cab[:, 0:m].indirect(T.gl[:, 0:nx_]), T.gsr[:, 0:16 * nx_], ALU.mult)
+    vgv = tt(T.gsv[:, 0:16 * nx_], T.ef[:, 0:m].indirect(T.gl[:, 0:nx_]), T.gsc[:, 0:16 * nx_], ALU.mult, dep=[v])
+    iot, dep = T.iot[:, 0:33], [tp]
+    if r > 1:
+        cols = [T.cin[:, 4 * s + c:4 * s + c + 1] for s, c in tellers(r)]
+        more = (cols[1], ALU.subtract, ALU.subtract) if cols[1:] else (None, ALU.subtract)
+        dep.append(ts(T.iotb[:, 0:33], iot, cols[0], *more, dep=[("c%d" % s, ne) for s, _ in tellers(r)]))
+        iot = T.iotb[:, 0:33]
+    yp = T.py[0:8, 0:32]
+    for x in range(nx_):
+        e = 2 * (x + 2 * u0)
+        vo = ts(T.oh[:, 64 * x:64 * x + 33], iot, T.eef[:, e:e + 1], T.pq[:, e // 4:e // 4 + 1], ALU.subtract, ALU.is_equal, dep=dep)
+        for k in range(2):
+            ty = mm(yp, blk(T.gsv, 2 * x + k, 8), T.oh[:, 64 * x + 1 - k:64 * x + 33 - k], x + k == 0, x + k == nx_, dep=[vo, vgv])
     vy = ts(T.ys[0:8, :], yp, -1.0, None, ALU.add, dep=[ty])
     wait("y", *vy)
     Y.dma_start(T.y[:, :], T.ys[0:8, :]).then_inc(T.sem.yo, 16)
 
     wait("y", "yo", 16)
-    wait("p", "lx", ne)
-    wait("p", "lw", ne)
-    wait("p", "lc", ne)
+    wait("p", "lx", len(on))
+    wait("p", "lw", ne * len(nb))
+    if told:
+        wait("p", "lc", ne)
     if far:
         wait("p", "lm", ne)
     for name in ("v", "a", "t"):

@@ -6,12 +6,13 @@ ACTF = ActivationFunctionType
 F, B, H, I4, U2 = "float32", "bfloat16", "float16", "int32", "uint16"
 SBUF = {
     I4: "nxi:512 emi:512 ipi:8 qgi:8 vi:8 si3:64 ei:16",
-    B: "ones:128 iob:128 jj:2048 wa0:128 wa1:128 wb0:128 wb1:128 rep:128 sg:128 sga:128 sgb:128 gt:128 lt:128 ee:24 gsv:96 oh:384",
+    B: "ones:128 iob:128 jj:2048 wa0:128 wa1:128 wb0:128 wb1:128 wc0:128 wc1:128 wu:128 rep:256 sg:128 sga:128 sgb:128 "
+       "gt:128 lt:128 ee:24 gs:144 oh:384",
     H: "emh:512 sela:128",
-    F: "ipf:8 qgf:8 hm:8 mq:128 kq:128 mg:128 rm:16 n0:8 iot:40 iotb:40 tri0:128 tri1:128 big:1024 xe:1152 xo:1152 w0f:128 dg:128 "
-       "rs:128 md:128 ms:128 mk1:112 mk3:64 thr:8 g8:96 gsr:96 gsc:96 l2:8 g2:112 g3:64 sc1:112 sc3:64 cab:16 eef:24 ef:16 "
-       "tot:4 cin:32 ys:32",
-    U2: "s:48 lm0:8 ls2:8 gl:8",
+    F: "ipf:8 qgf:8 hm:8 mq:128 kq:128 mg:128 rm:16 n0:8 iot:56 iq:8 tri0:128 tri1:128 big:1024 xe:1152 xo:1152 w0f:128 dg:128 "
+       "rs:128 md:256 ms:256 mk1:112 mk3:64 thr:8 val:16 g2:112 g3:64 sc1:112 sc3:64 cab:16 eef:24 ef:16 "
+       "tot:4 cin:32 zl:48 ys:32",
+    U2: "s:48 lm:16 ls2:8 gl:8 lsh:8",
 }
 SCRATCH = {w.split(":")[0]: ("sbuf", [128, int(w.split(":")[1])], d) for d, ws in SBUF.items() for w in ws.split()}
 SCRATCH.update({
@@ -24,7 +25,7 @@ SCRATCH.update({
 SCRATCH.update({n: ("psum", [128, 512], F) for n in "pb px pq pt py".split()})
 SEMAPHORES = ("v a t p ds mo yo xh lx lw lm lc".split() + [s + str(t) for s in ("dn", "de") for t in range(4)]
               + [s + str(r) for s in ("x", "w", "m", "c", "ld") for r in range(8)])
-CUT = 14
+CUTS = (0, 10, 20, 32)
 
 
 def tellers(r):
@@ -126,9 +127,10 @@ def rank_program(g, core, T, topo):
     iota(T.mq[:, :], [[0, 8], [1, 16]], 0, 0)
     pmg = iota(T.mg[:, :], [[1, 8], [0, 16]], 0, 0)
     iota(T.kq[:, :], [[0, 8], [1, 16]], 0, 0)
-    iota(T.iot[:, 0:33], [[1, 33]], 32 * r - 1, 0)
-    iota(T.l2[:, 0:6], [[2, 6]], 4 if r else 0, 0)
-    iota(T.g8[:, :], [[0, 12], [1, 8]], 0, 0)
+    wide = 48 if r > 1 else 32
+    base = 24 if r > 1 else 32 * r
+    iota(T.iot[:, 0:wide + 1], [[1, wide + 1]], base - 1, 0)
+    iota(T.iq[:, 0:2], [[16, 2]], 32 * r - base, 0)
     pz = iota(blk(T.xe, near[-1] + 1), [[0, 128]], 0, 0)
     if r > 1:
         iota(T.xe[:, 0:128 * (r - 1)], [[0, 128 * (r - 1)]], 0, 0)
@@ -144,16 +146,20 @@ def rank_program(g, core, T, topo):
     vqg = cp(T.qgf[:, 0:3], T.qgi[:, 0:3], dep=[v])
     vrm = ts(T.rm[:, :], T.rm[:, :], qcol, None, ALU.is_equal, dep=[vqg])
     jd = {}
-    for j in (0, 7, 15, 6, 14, 5, 13, 4, 12, 3):
+    for j in range(12):
         jd[j] = act(blk(T.jj, j), T.iob[:, :], ACTF.Copy, scale=T.rm[:, j:j + 1], dep=[vrm, pib])
-    for j in (11, 2, 10, 1, 9, 8):
+    for j in range(12, 16):
         jd[j] = ts(blk(T.jj, j), T.iob[:, :], T.rm[:, j:j + 1], None, ALU.mult, dep=[vrm, pib])
     acol = act(T.n0[:, 0:1], m0, ACTF.Identity, scale=128.0, bias=128.0 * r)
     vsg = ts(T.sg[:, :], T.mg[:, :], gcol, None, ALU.is_equal, dep=[pmg])
+    ts(T.dg[:, :], T.mq[:, :], qcol, None, ALU.is_equal)
+    ts(T.rs[:, :], T.mq[:, :], 0.0, None, ALU.is_gt)
     for eo in range(2):
         vrow = cp(T.syr[0:1, eo:16:2, :], T.syi[0:1, :, eo:32:2], dep=[("ds", 32)])
     tbc = mm(T.pb[:, 0:256], T.ones[0:1, :], T.syr[0:1, :, :], True, True, dep=[von, vrow])
-    arep = act(T.rep[:, :], T.sg[:, :], ACTF.Copy, scale=T.rm[:, CUT // 2:CUT // 2 + 1], dep=[vsg])
+    for ch in range(2):
+        j = CUTS[ch + 1] // 2
+        arep = act(blk(T.rep, ch), T.sg[:, :], ACTF.Copy, scale=T.rm[:, j:j + 1], dep=[vsg])
     vt = []
     for t in range(4):
         for h in range(2):
@@ -171,14 +177,14 @@ def rank_program(g, core, T, topo):
                      dep=[vt[t], vsa])
     last = {}
 
-    def lists(k, part):
-        cs = slice(16 * k, 16 * k + 16)
+    def lists(eo, part):
+        cs = slice(2 * eo, 2 * eo + 2)
         if part == 0:
-            last["x"] = cp(T.oi[:, :, cs], T.pl[:, 0:4, cs], dep=[tof])
+            last[eo] = cp(T.oi[:, cs, :], T.pl[:, cs, :], dep=[tof])
         elif part == 1:
-            last["x"] = ts(T.oi2[:, :, cs], T.oi[:, :, cs], 127, None, ALU.bitwise_and, dep=[last["x"]])
+            last[eo] = ts(T.oi2[:, cs, :], T.oi[:, cs, :], 127, None, ALU.bitwise_and, dep=[last[eo]])
         else:
-            last[k] = cp(T.off[:, :, cs], T.oi2[:, :, cs], dep=[last["x"]])
+            last[eo] = cp(T.off[:, cs, :], T.oi2[:, cs, :], dep=[last[eo]])
 
     def entries(t):
         v = ts(blk(T.emh, t), blk(T.emi, t), -2048, 1.0 / 4096, ALU.add, ALU.mult, dep=[("de%d" % t, 16)])
@@ -192,48 +198,43 @@ def rank_program(g, core, T, topo):
         last["t"] = act(xtab(r, eo), blk(T.px, eo), ACTF.Copy, scale=4096.0, bias=2048.0 + (0 if eo else 4096.0 * xoff(r)),
                         dep=[last["e"]])
 
-    def diag():
-        ts(T.dg[:, :], T.mq[:, :], qcol, None, ALU.is_equal)
-
-    def restart():
-        last["c"] = ts(T.rs[:, :], T.mq[:, :], 0.0, None, ALU.is_gt)
     for h in range(2):
         last["m"] = ts(T.selm[:, :, 16 * h:16 * h + 16], T.sela[:, :], T.hm[:, h:h + 1], None, ALU.mult, dep=[vsa])
-    for k in (3, 2):
-        for part in range(3):
-            lists(k, part)
-    vfill = ([(lists, 1, part) for part in range(3)] + [(entries, t) for t in range(4)] + [(lists, 0, part) for part in range(3)]
-             + [(diag,), (restart,)])
-    afill = {10: (table, 0), 11: (table, 1)}
+    for part in range(3):
+        for eo in (1, 0):
+            lists(eo, part)
 
-    prev = [(blk(T.jj, j), jd[j]) for j in (CUT // 2, 0)]
-    for n in range(32 - CUT):
-        for ch, i in ((1, 31 - n), (0, CUT - n)):
-            if not 0 <= i < (32 if ch else CUT):
+    prev = [(blk(T.jj, e // 2 % 16), jd[e // 2 % 16]) for e in CUTS[1:]]
+    trep = {}
+    for n in range(CUTS[3] - CUTS[2]):
+        for ch in (1, 0, 2):
+            i = CUTS[ch + 1] - 1 - n
+            if i < CUTS[ch]:
                 continue
             win, dw = prev[ch]
-            o = T["w%s%d" % ("ab"[ch], i % 2)][:, :]
+            o = T["w%s%d" % ("abc"[ch], i % 2)][:, :]
             c = 8 * (i % 16 // 2)
             src = win.indirect(T.off[:, 2 * (i % 2) + i // 16, c:c + 8])
-            dep = [last[i % 16 // 4], dw]
-            if i % 2 or i == CUT:
+            dep = [last[i % 2], dw]
+            if i % 2 or i == CUTS[ch]:
                 dw = act(o, src, ACTF.Copy, dep=dep)
-                if n in afill:
-                    afill[n][0](*afill[n][1:])
             else:
-                dw = tt(o, src, blk(T.jj, i // 2), ALU.add, dep=dep + [jd[i // 2]]) if i else cp(o, src, dep=dep)
-                if vfill:
-                    f = vfill.pop(0)
-                    f[0](*f[1:])
+                dw = tt(o, src, blk(T.jj, i // 2), ALU.add, dep=dep + [jd[i // 2]])
             prev[ch] = (o, dw)
-            if i == 0:
-                trep = mm(T.pb[:, 0:128], T.rep[:, :], o, True, True, dep=[arep, dw])
-            if i == CUT + 2:
-                aw0 = act(T.w0f[:, :], prev[0][0], ACTF.Identity, bias=T.n0[:, 0:1], dep=[prev[0][1], acol])
-    v = tt(T.md[:, :], T.pb[:, 0:128], T.dg[:, :], ALU.mult, dep=[trep, last["c"]])
-    v = scan(T.ms[:, :], T.rs[:, :], T.md[:, :], ALU.mult, ALU.add, dep=[v])
-    v = cp(T.lm0[:, :], T.ms[:, 15:128:16], dep=[v])
-    vw = tt(blk(T.big, r), prev[1][0].indirect(T.lm0[:, :]), T.w0f[:, :], ALU.add, dep=[v, prev[1][1], aw0])
+            if i == CUTS[ch] and ch < 2:
+                trep[ch] = mm((T.pt, T.pb)[ch][:, 0:128], blk(T.rep, ch), o, True, True, dep=[arep, dw])
+        if n in (1, 3):
+            entries(n - 1)
+            entries(n)
+        if n == 6:
+            table(0)
+            table(1)
+    aw0 = act(T.w0f[:, :], prev[0][0], ACTF.Identity, bias=T.n0[:, 0:1], dep=[prev[0][1], acol])
+    vm = {ch: tt(blk(T.md, ch), (T.pt, T.pb)[ch][:, 0:128], T.dg[:, :], ALU.mult, dep=[trep[ch]]) for ch in (1, 0)}
+    vm = {ch: scan(blk(T.ms, ch), T.rs[:, :], blk(T.md, ch), ALU.mult, ALU.add, dep=[vm[ch]]) for ch in (1, 0)}
+    vm = {ch: cp(blk(T.lm, ch, 8), blk(T.ms, ch)[:, 15:128:16], dep=[vm[ch]]) for ch in (1, 0)}
+    v = tt(T.wu[:, :], prev[2][0].indirect(blk(T.lm, 1, 8)), prev[1][0], ALU.add, dep=[vm[1], prev[2][1]])
+    vw = tt(blk(T.big, r), T.wu[:, :].indirect(blk(T.lm, 0, 8)), T.w0f[:, :], ALU.add, dep=[v, aw0])
 
     def send(buf_src, buf_dst, sem, lsem, dests):
         g.remote_dma_fused([transfer(buf_src, buf_dst, sem, [cores[d] for d in dests], topo.engines(core, cores[dests[0]]))],
@@ -272,8 +273,11 @@ def rank_program(g, core, T, topo):
     fill(T.kq[:, 0:128:16], 16.0)
     ts(n0, m0, -1.0, 1.0, ALU.mult, ALU.add)
     ts(T.n0[:, 2:3], m0, 16.0, qcol, ALU.mult, ALU.add)
-    v = ts(T.n0[:, 3:4], qcol, 8.0, None, ALU.is_ge)
-    ts(T.gsr[:, :], T.g8[:, :], gcol, None, ALU.is_equal)
+    fill(T.gs[:, 128:144], 0.0)
+    fill(T.cab[:, :], 0.0)
+    fill(T.ef[:, :], 0.0)
+    ts(T.iq[:, 0:2], T.iq[:, 0:2], qcol, None, ALU.add)
+    v = ts(T.gl[:, :], T.mg[:, 0:8], qcol, None, ALU.add)
     for u in range(nc):
         d = near[0] - 1 + u
         for k in range(2):
@@ -284,7 +288,6 @@ def rank_program(g, core, T, topo):
                 cp(o, T.dg[:, 0:16], dep=[v])
             else:
                 ts(o, T.dg[:, 0:16], n0 if u else m0, None, ALU.mult, dep=[v])
-    ts(T.gl[:, 0:6], T.l2[:, 0:6], T.n0[:, 3:4], None, ALU.add)
     ts(T.tri0[:, :], T.kq[:, :], T.n0[:, 2:3], None, ALU.is_gt)
     v = ts(T.tri1[:, :], T.kq[:, :], T.n0[:, 2:3], None, ALU.is_lt)
     ts(T.sga[:, :], T.sg[:, :], n0, None, ALU.mult)
@@ -328,24 +331,27 @@ def rank_program(g, core, T, topo):
     u0 = 1 if r else 0
     nx_ = 2 * (nc - u0)
     scan(T.eef[:, 1:m + 1], T.cab[:, 0:m], T.cab[:, 0:m], ALU.add, ALU.max)
-    ts(T.ef[:, 0:m], T.ei[:, 0:m], 1, None, ALU.add, dep=[v])
-    v = tt(T.gsc[:, 0:16 * nx_], T.cab[:, 0:m].indirect(T.gl[:, 0:nx_]), T.gsr[:, 0:16 * nx_], ALU.mult)
-    vgv = tt(T.gsv[:, 0:16 * nx_], T.ef[:, 0:m].indirect(T.gl[:, 0:nx_]), T.gsc[:, 0:16 * nx_], ALU.mult, dep=[v])
-    iot, dep = T.iot[:, 0:33], [tp]
+    v = ts(T.ef[:, 0:m], T.ei[:, 0:m], 1, None, ALU.add, dep=[v])
+    v = tt(T.val[:, :], T.ef[:, :], T.cab[:, :], ALU.mult, dep=[v])
+    vgv = tt(T.gs[:, 0:128], T.val[:, :].indirect(T.gl[:, :]), T.sg[:, :], ALU.mult, dep=[v])
+    yp = T.py[:, 0:wide]
+    for x in range(nx_):
+        e = 2 * (x + 2 * u0)
+        vo = ts(T.oh[:, 64 * x:64 * x + wide + 1], T.iot[:, 0:wide + 1], T.eef[:, e:e + 1], T.pq[:, e // 4:e // 4 + 1],
+                ALU.subtract, ALU.is_equal, dep=[tp])
+        for k in range(2):
+            ty = mm(yp, T.gs[:, e + k:e + k + 128], T.oh[:, 64 * x + 1 - k:64 * x + 1 - k + wide], x + k == 0, x + k == nx_,
+                    dep=[vo, vgv])
     if r > 1:
         cols = [T.cin[:, 4 * s + c:4 * s + c + 1] for s, c in tellers(r)]
         more = (cols[1], ALU.subtract, ALU.subtract) if cols[1:] else (None, ALU.subtract)
-        dep.append(ts(T.iotb[:, 0:33], iot, cols[0], *more, dep=[("c%d" % s, ne) for s, _ in tellers(r)]))
-        iot = T.iotb[:, 0:33]
-    yp = T.py[0:8, 0:32]
-    for x in range(nx_):
-        e = 2 * (x + 2 * u0)
-        vo = ts(T.oh[:, 64 * x:64 * x + 33], iot, T.eef[:, e:e + 1], T.pq[:, e // 4:e // 4 + 1], ALU.subtract, ALU.is_equal, dep=dep)
-        for k in range(2):
-            ty = mm(yp, blk(T.gsv, 2 * x + k, 8), T.oh[:, 64 * x + 1 - k:64 * x + 33 - k], x + k == 0, x + k == nx_, dep=[vo, vgv])
-    vy = ts(T.ys[0:8, :], yp, -1.0, None, ALU.add, dep=[ty])
+        vl = ts(T.lsh[:, 0:2], T.iq[:, 0:2], cols[0], *more, dep=[("c%d" % s, ne) for s, _ in tellers(r)])
+        v = cp(T.zl[:, :], yp, dep=[ty])
+        vy = ts(T.ys[:, :], T.zl[:, :].indirect(T.lsh[:, 0:2]), -1.0, None, ALU.add, dep=[v, vl])
+    else:
+        vy = ts(T.ys[:, :], yp, -1.0, None, ALU.add, dep=[ty])
     wait("y", *vy)
-    Y.dma_start(T.y[:, :], T.ys[0:8, :]).then_inc(T.sem.yo, 16)
+    Y.dma_start(T.y[:, :], T.ys[0:128:16, :]).then_inc(T.sem.yo, 16)
 
     wait("y", "yo", 16)
     wait("p", "lx", len(on))

@@ -6,12 +6,12 @@ ACTF = ActivationFunctionType
 F, B, H, I4, U2 = "float32", "bfloat16", "float16", "int32", "uint16"
 SBUF = {
     I4: "nxi:512 emi:512 ipi:8 qgi:8 vi:8 si3:64 ei:16",
-    B: "ones:128 iob:128 jj:2048 wa0:128 wa1:128 wb0:128 wb1:128 wc0:128 wc1:128 wu:128 rep:256 sg:128 sga:128 sgb:128 "
-       "gt:128 lt:128 ee:24 gs:144 oh:384",
+    B: "ones:128 nil:128 iob:128 jj:2048 wa0:128 wa1:128 wb0:128 wb1:128 wc0:128 wc1:128 wu:128 big:1024 rep:256 sg:128 sga:128 "
+       "sgb:128 gt:128 lt:128 ee:24 cin:192 gs:144 oh:384",
     H: "emh:512 sela:128",
-    F: "ipf:8 qgf:8 hm:8 mq:128 kq:128 mg:128 rm:16 n0:8 iot:56 iq:8 tri0:128 tri1:128 big:1024 xe:1152 xo:1152 w0f:128 dg:128 "
-       "rs:128 md:256 ms:256 mk1:112 mk3:64 thr:8 val:16 g2:112 g3:64 sc1:112 sc3:64 cab:16 eef:24 ef:16 "
-       "tot:4 cin:32 zl:48 ys:32",
+    F: "qgf:8 hm:8 mq:128 kq:128 mg:128 rm:16 n0:8 iot:56 iq:8 tri0:128 tri1:128 nw:384 xe:512 xo:1152 dg:128 "
+       "rs:128 md:256 ms:256 mk1:112 mk3:64 thr:8 val:24 g2:112 g3:64 sc1:112 sc3:64 ca:8 cab:16 eef:24 gl0:8 "
+       "zl:48 ys:32",
     U2: "s:48 lm:16 ls2:8 gl:8 lsh:8",
 }
 SCRATCH = {w.split(":")[0]: ("sbuf", [128, int(w.split(":")[1])], d) for d, ws in SBUF.items() for w in ws.split()}
@@ -19,13 +19,15 @@ SCRATCH.update({
     "syi": ("sbuf", [128, 8, 32], I4), "syr": ("sbuf", [128, 16, 16], B),
     "selm": ("sbuf", [128, 8, 32], H), "tb": ("sbuf", [128, 32, 32], H),
     "oi": ("sbuf", [128, 4, 64], I4), "oi2": ("sbuf", [128, 4, 64], I4), "off": ("sbuf", [128, 4, 64], U2),
-    "mdo": ("dram", [128, 8], F), "mdi": ("dram", [8, 128, 8], F),
+    "mdo": ("dram", [128, 8], B), "mdi": ("dram", [8, 128, 8], B),
     "pl": ("psum", [128, 8, 64], F),
 })
-SCRATCH.update({n: ("psum", [128, 512], F) for n in "pb px pq pt py".split()})
+SCRATCH.update({n: ("psum", [128, 512], F) for n in "pb pe po pq pt py".split()})
 SEMAPHORES = ("v a t p ds mo yo xh lx lw lm lc".split() + [s + str(t) for s in ("dn", "de") for t in range(4)]
-              + [s + str(r) for s in ("x", "w", "m", "c", "ld") for r in range(8)])
+              + [s + str(r) for s in ("x", "e", "w", "m", "c", "ld") for r in range(8)])
 CUTS = (0, 10, 20, 32)
+TURNS = (1, 0, 2)
+ONE = 64.0
 
 
 def tellers(r):
@@ -40,16 +42,19 @@ def rank_program(g, core, T, topo):
     cores = T.cores
     N = len(cores)
 
-    def transfer(src, dst, sem, to, engines):
+    def transfer(src, dsts, sem, to, engines):
         ids = []
         for c in to:
             rid, pid = topo.addr(c, core)
             ids.append(DstId(rid=rid, pnc=pid))
         return RemoteDMATransfer(dst_ids=ids, dma_engine_mask=sum(1 << e for e in engines), remote_sem=T.sem[sem],
-                                 srcs=[src], dsts=[dst] * len(ids))
+                                 srcs=[src], dsts=dsts)
 
-    def helpers(d):
-        return [c for c in topo.cores_of(cores[d]) if topo.die(c) != topo.die(cores[d])][:2]
+    def helper(d):
+        return [c for c in topo.cores_of(cores[d]) if topo.die(c) != topo.die(cores[d])][0]
+
+    def inside(d):
+        return [e for e in topo.engines(cores[d], helper(d)) if e not in topo.engines(cores[d], cores[(d + 1) % N])]
 
     def blk(buf, d, n=128):
         return buf[:, n * d:n * d + n]
@@ -57,16 +62,17 @@ def rank_program(g, core, T, topo):
     def xoff(d):
         return 384 * (d % 3)
 
-    def xtab(d, eo, k=0):
-        return blk(T.xo, 3 * (d % 3) + k) if eo else blk(T.xe, d)
+    def xtab(d, eo, at, k=0):
+        return blk(T.xo, 3 * (d % 3) + k) if eo else blk(T.xe, d - max(at - 1, 0))
     r = T.rank_of(core)
     if r is None:
         for d in range(N):
-            if core in helpers(d):
-                to = [cores[e] for e in (d + 1, d - 1) if 0 <= e < N]
-                tab, out = xtab(d, helpers(d).index(core)), topo.engines(core, to[0])
-                g.wait_ge(T.sem.xh, len(topo.engines(cores[d], core)) // 2)
-                g.remote_dma_fused([transfer(tab, tab, "x%d" % d, to, out)], local_sem=T.sem.lx)
+            if core == helper(d):
+                to = [e for e in (d + 1, d - 1) if 0 <= e < N]
+                out = topo.engines(core, cores[to[0]])
+                g.wait_ge(T.sem.xh, len(inside(d)))
+                g.remote_dma_fused([transfer(xtab(d, 0, d), [xtab(d, 0, e) for e in to], "e%d" % d, [cores[e] for e in to], out)],
+                                   local_sem=T.sem.lx)
                 g.wait_ge(T.sem.lx, len(out))
         return
     V, A, P, Y = g.vector, g.scalar, g.tensor, g.sync
@@ -114,53 +120,53 @@ def rank_program(g, core, T, topo):
         (Y, A)[h].dma_start(T.syi[0:1, 4 * h:4 * h + 4, :], T.sy[h::2, :]).then_inc(T.sem.ds, 16)
     for t in range(4):
         (Y, A)[t % 2].dma_start(blk(T.nxi, t), T.nx[2 * t:2 * t + 2, :]).then_inc(T.sem["dn%d" % t], 16)
-    wait("y", "dn2", 16)
+    wait("y", "dn0", 16)
     for t in range(4):
         Y.dma_start(blk(T.emi, t), T.em[2 * t:2 * t + 2, :]).then_inc(T.sem["de%d" % t], 16)
 
     def iota(ap, pattern, base, cm):
         return do("p", lambda: g.iota(ap, pattern, base, cm, allow_small_or_imprecise_dtypes=True))
-    iota(T.ipi[:, 0:1], [[0, 1]], 0, 1)
-    iota(T.ipf[:, 0:1], [[0, 1]], 0, 1)
+    pi = iota(T.ipi[:, 0:1], [[0, 1]], 0, 1)
     pq = iota(T.rm[:, 0:16], [[1, 16]], 0, 0)
     pib = iota(T.iob[:, :], [[1, 128]], 0, 0)
-    iota(T.mq[:, :], [[0, 8], [1, 16]], 0, 0)
+    pmq = iota(T.mq[:, :], [[0, 8], [1, 16]], 0, 0)
     pmg = iota(T.mg[:, :], [[1, 8], [0, 16]], 0, 0)
     iota(T.kq[:, :], [[0, 8], [1, 16]], 0, 0)
     wide = 48 if r > 1 else 32
     base = 24 if r > 1 else 32 * r
-    iota(T.iot[:, 0:wide + 1], [[1, wide + 1]], base - 1, 0)
+    iota(T.iot[:, 0:wide + 1], [[int(ONE), wide + 1]], int(ONE) * (base - 1), 0)
     iota(T.iq[:, 0:2], [[16, 2]], 32 * r - base, 0)
-    pz = iota(blk(T.xe, near[-1] + 1), [[0, 128]], 0, 0)
+    pz = iota(blk(T.xe, nu), [[0, 128]], 0, 0)
     if r > 1:
-        iota(T.xe[:, 0:128 * (r - 1)], [[0, 128 * (r - 1)]], 0, 0)
         pz = iota(T.big[:, 0:128 * (r - 1)], [[0, 128 * (r - 1)]], 0, 0)
 
-    von = fill(T.ones[:, :], 1.0)
-    ts(T.qgi[:, 0:1], T.ipi[:, 0:1], 15, None, ALU.bitwise_and, dep=[pq])
+    fill(T.nil[0:1, :], 0.0)
+    von = fill(T.ones[0:1, :], 1.0)
+    ts(T.qgi[:, 0:1], T.ipi[:, 0:1], 15, None, ALU.bitwise_and, dep=[pi])
     ts(T.qgi[:, 2:3], T.ipi[:, 0:1], 63, None, ALU.bitwise_and)
     v = ts(T.qgi[:, 1:2], T.ipi[:, 0:1], 4, None, ALU.logical_shift_right)
-    qcol, gcol, pcol, m0 = T.qgf[:, 0:1], T.qgf[:, 1:2], T.ipf[:, 0:1], T.rm[:, 0:1]
-    ts(T.hm[:, 0:1], pcol, 64.0, None, ALU.is_lt)
-    ts(T.hm[:, 1:2], pcol, 64.0, None, ALU.is_ge)
+    qcol, gcol, m0 = T.qgf[:, 0:1], T.qgf[:, 1:2], T.rm[:, 0:1]
+    ts(T.hm[:, 0:1], T.ipi[:, 0:1], 64.0, None, ALU.is_lt)
+    ts(T.hm[:, 1:2], T.ipi[:, 0:1], 64.0, None, ALU.is_ge)
     vqg = cp(T.qgf[:, 0:3], T.qgi[:, 0:3], dep=[v])
-    vrm = ts(T.rm[:, :], T.rm[:, :], qcol, None, ALU.is_equal, dep=[vqg])
+    vrm = ts(T.rm[:, :], T.rm[:, :], qcol, None, ALU.is_equal, dep=[vqg, pq])
+    px = (T.pe[:, 0:128], T.po[:, 0:128])
+    for o in px:
+        mm(o, T.ones[0:1, :], T.nil[0:1, :], True, False, dep=[von])
     jd = {}
     for j in range(12):
         jd[j] = act(blk(T.jj, j), T.iob[:, :], ACTF.Copy, scale=T.rm[:, j:j + 1], dep=[vrm, pib])
     for j in range(12, 16):
         jd[j] = ts(blk(T.jj, j), T.iob[:, :], T.rm[:, j:j + 1], None, ALU.mult, dep=[vrm, pib])
-    acol = act(T.n0[:, 0:1], m0, ACTF.Identity, scale=128.0, bias=128.0 * r)
-    vsg = ts(T.sg[:, :], T.mg[:, :], gcol, None, ALU.is_equal, dep=[pmg])
-    ts(T.dg[:, :], T.mq[:, :], qcol, None, ALU.is_equal)
-    ts(T.rs[:, :], T.mq[:, :], 0.0, None, ALU.is_gt)
+    for u in range(nu):
+        acol = act(T.n0[:, 4 + u:5 + u], m0, ACTF.Identity, scale=128.0, bias=128.0 * u)
     for eo in range(2):
         vrow = cp(T.syr[0:1, eo:16:2, :], T.syi[0:1, :, eo:32:2], dep=[("ds", 32)])
-    tbc = mm(T.pb[:, 0:256], T.ones[0:1, :], T.syr[0:1, :, :], True, True, dep=[von, vrow])
-    for ch in range(2):
-        j = CUTS[ch + 1] // 2
-        arep = act(blk(T.rep, ch), T.sg[:, :], ACTF.Copy, scale=T.rm[:, j:j + 1], dep=[vsg])
+    tbc = mm(T.pb[:, 0:256], T.ones[0:1, :], T.syr[0:1, :, :], True, True, dep=[vrow])
+    ts(T.dg[:, :], T.mq[:, :], qcol, None, ALU.is_equal, dep=[pmq])
+    ts(T.rs[:, :], T.mq[:, :], 0.0, None, ALU.is_gt)
     vt = []
+    last = {}
     for t in range(4):
         for h in range(2):
             v = ts(T.tb[:, 8 * t:8 * t + 8, 16 * h:16 * h + 16], blk(T.nxi, t), T.hm[:, h:h + 1], None, ALU.mult,
@@ -170,98 +176,129 @@ def rank_program(g, core, T, topo):
             for h in range(2):
                 hs = slice(64 * h, 64 * h + 64)
                 vsa = ts(T.sela[hs, :], T.pb[hs, 128 * h:128 * h + 128], T.qgf[hs, 2:3], None, ALU.is_equal, dep=[tbc])
+    for h in range(2):
+        vsm = ts(T.selm[:, :, 16 * h:16 * h + 16], T.sela[:, :], T.hm[:, h:h + 1], None, ALU.mult, dep=[vsa])
+    vsg = ts(T.sg[:, :], T.mg[:, :], gcol, None, ALU.is_equal, dep=[pmg])
+    for ch in range(2):
+        j = CUTS[ch + 1] // 2
+        arep = act(blk(T.rep, ch), T.sg[:, :], ACTF.Copy, scale=T.rm[:, j:j + 1], dep=[vsg])
 
     for t in range(4):
         for c in range(8):
             tof = mm(T.pl[32 * t:32 * t + 32, 0:4, c:64:8], T.tb[:, 8 * t + c, :], T.sela[:, 32 * t:32 * t + 32], True, True,
                      dep=[vt[t], vsa])
-    last = {}
+    for k in range(6):
+        for part in (2, 1, 0):
+            if 0 <= k - part < 4:
+                b = 3 - (k - part)
+                if part == 0:
+                    last[b] = cp(T.oi[:, b, :], T.pl[:, b, :], dep=[tof])
+                elif part == 1:
+                    last[b] = ts(T.oi2[:, b, :], T.oi[:, b, :], 127, None, ALU.bitwise_and, dep=[last[b]])
+                else:
+                    last[b] = cp(T.off[:, b, :], T.oi2[:, b, :], dep=[last[b]])
 
-    def lists(eo, part):
-        cs = slice(2 * eo, 2 * eo + 2)
-        if part == 0:
-            last[eo] = cp(T.oi[:, cs, :], T.pl[:, cs, :], dep=[tof])
-        elif part == 1:
-            last[eo] = ts(T.oi2[:, cs, :], T.oi[:, cs, :], 127, None, ALU.bitwise_and, dep=[last[eo]])
-        else:
-            last[eo] = cp(T.off[:, cs, :], T.oi2[:, cs, :], dep=[last[eo]])
+    def add(t, eo, rhs, dep):
+        mm(px[eo][32 * t:32 * t + 32, :], T.selm[:, 2 * t + eo, :], rhs, False, False, dep=dep)
+
+    def nexts(t, eo):
+        for h in range(2):
+            add(t, eo, T.tb[:, 8 * t:8 * t + 8, 16 * h:16 * h + 16], [vsm])
+    for t in range(4):
+        nexts(t, 1)
 
     def entries(t):
         v = ts(blk(T.emh, t), blk(T.emi, t), -2048, 1.0 / 4096, ALU.add, ALU.mult, dep=[("de%d" % t, 16)])
-        for eo in range(2):
-            o, lh = T.px[32 * t:32 * t + 32, 128 * eo:128 * eo + 128], T.selm[:, 2 * t + eo, :]
-            for h in range(2):
-                mm(o, lh, T.tb[:, 8 * t:8 * t + 8, 16 * h:16 * h + 16], h == 0, False, dep=[last["m"]])
-            last["e"] = mm(o, lh, blk(T.emh, t), False, True, dep=[v])
+        if t < 3:
+            nexts(t, 0)
+        add(t, 1, blk(T.emh, t), [v])
+        if t == 3:
+            last["e1"] = mm(px[1], T.ones[0:1, :], T.nil[0:1, :], False, True)
+            nexts(t, 0)
+            for k in range(4):
+                add(k, 0, blk(T.emh, k), [])
+            last["e0"] = mm(px[0], T.ones[0:1, :], T.nil[0:1, :], False, True)
 
     def table(eo):
-        last["t"] = act(xtab(r, eo), blk(T.px, eo), ACTF.Copy, scale=4096.0, bias=2048.0 + (0 if eo else 4096.0 * xoff(r)),
-                        dep=[last["e"]])
-
-    for h in range(2):
-        last["m"] = ts(T.selm[:, :, 16 * h:16 * h + 16], T.sela[:, :], T.hm[:, h:h + 1], None, ALU.mult, dep=[vsa])
-    for part in range(3):
-        for eo in (1, 0):
-            lists(eo, part)
+        last["t%d" % eo] = act(xtab(r, eo, r), px[eo], ACTF.Copy, scale=4096.0, bias=2048.0 + (0 if eo else 4096.0 * xoff(r)),
+                               dep=[last["e%d" % eo]])
+    entries(0)
+    entries(1)
 
     prev = [(blk(T.jj, e // 2 % 16), jd[e // 2 % 16]) for e in CUTS[1:]]
-    trep = {}
+    vm = {}
+
+    def listed(ch, part):
+        ps = (T.pt, T.pb)[ch][:, 0:128]
+        if part == 0:
+            vm[ch] = tt(blk(T.md, ch), ps, T.dg[:, :], ALU.mult, dep=[mm(ps, blk(T.rep, ch), prev[ch][0], True, True, dep=[arep, prev[ch][1]])])
+        elif part == 1:
+            vm[ch] = scan(blk(T.ms, ch), T.rs[:, :], blk(T.md, ch), ALU.mult, ALU.add, dep=[vm[ch]])
+        else:
+            vm[ch] = cp(blk(T.lm, ch, 8), blk(T.ms, ch)[:, 15:128:16], dep=[vm[ch]])
+    todo = [(ch, part) for part in range(3) for ch in (1, 0)]
     for n in range(CUTS[3] - CUTS[2]):
-        for ch in (1, 0, 2):
+        for ch in TURNS:
             i = CUTS[ch + 1] - 1 - n
             if i < CUTS[ch]:
                 continue
             win, dw = prev[ch]
             o = T["w%s%d" % ("abc"[ch], i % 2)][:, :]
-            c = 8 * (i % 16 // 2)
-            src = win.indirect(T.off[:, 2 * (i % 2) + i // 16, c:c + 8])
-            dep = [last[i % 2], dw]
-            if i % 2 or i == CUTS[ch]:
+            b, c = 2 * (i % 2) + i // 16, 8 * (i % 16 // 2)
+            src = win.indirect(T.off[:, b, c:c + 8])
+            dep = [last[b], dw]
+            if i % 2 or i == CUTS[2]:
                 dw = act(o, src, ACTF.Copy, dep=dep)
+            elif i == CUTS[ch]:
+                dw = cp(o, src, dep=dep)
             else:
                 dw = tt(o, src, blk(T.jj, i // 2), ALU.add, dep=dep + [jd[i // 2]])
             prev[ch] = (o, dw)
-            if i == CUTS[ch] and ch < 2:
-                trep[ch] = mm((T.pt, T.pb)[ch][:, 0:128], blk(T.rep, ch), o, True, True, dep=[arep, dw])
-        if n in (1, 3):
-            entries(n - 1)
-            entries(n)
-        if n == 6:
-            table(0)
-            table(1)
-    aw0 = act(T.w0f[:, :], prev[0][0], ACTF.Identity, bias=T.n0[:, 0:1], dep=[prev[0][1], acol])
-    vm = {ch: tt(blk(T.md, ch), (T.pt, T.pb)[ch][:, 0:128], T.dg[:, :], ALU.mult, dep=[trep[ch]]) for ch in (1, 0)}
-    vm = {ch: scan(blk(T.ms, ch), T.rs[:, :], blk(T.md, ch), ALU.mult, ALU.add, dep=[vm[ch]]) for ch in (1, 0)}
-    vm = {ch: cp(blk(T.lm, ch, 8), blk(T.ms, ch)[:, 15:128:16], dep=[vm[ch]]) for ch in (1, 0)}
+            if n == 1 and ch != TURNS[2]:
+                entries(2 + TURNS.index(ch))
+        if n in (3, 4):
+            table(4 - n)
+    for x in todo:
+        listed(*x)
     v = tt(T.wu[:, :], prev[2][0].indirect(blk(T.lm, 1, 8)), prev[1][0], ALU.add, dep=[vm[1], prev[2][1]])
-    vw = tt(blk(T.big, r), T.wu[:, :].indirect(blk(T.lm, 0, 8)), T.w0f[:, :], ALU.add, dep=[v, aw0])
+    vw = tt(blk(T.big, r), T.wu[:, :].indirect(blk(T.lm, 0, 8)), prev[0][0], ALU.add, dep=[v, vm[0]])
 
-    def send(buf_src, buf_dst, sem, lsem, dests):
-        g.remote_dma_fused([transfer(buf_src, buf_dst, sem, [cores[d] for d in dests], topo.engines(core, cores[dests[0]]))],
+    def send(src, dst, sem, lsem, dests):
+        g.remote_dma_fused([transfer(src, [dst] * len(dests), sem, [cores[d] for d in dests], topo.engines(core, cores[dests[0]]))],
                            local_sem=T.sem[lsem])
     ne = len(topo.engines(core, cores[nb[0]]))
-    on = topo.engines(core, helpers(r)[0])
-    wait("p", *last["t"])
-    g.remote_dma_fused([transfer(xtab(r, eo), xtab(r, eo), "xh", [c], on[eo * len(on) // 2:(eo + 1) * len(on) // 2])
-                        for eo, c in enumerate(helpers(r))], local_sem=T.sem.lx)
-    wait("p", *vw)
-    send(blk(T.big, r), blk(T.big, r), "w%d" % r, "lw", nb[:1])
+    wait("p", *last["t1"])
+    send(xtab(r, 1, r), xtab(r, 1, r), "x%d" % r, "lx", nb)
+    wait("p", *last["t0"])
+    g.remote_dma_fused([transfer(xtab(r, 0, r), [xtab(r, 0, r)], "xh", [helper(r)], inside(r))], local_sem=T.sem.lx)
     far = list(range(N - 1, r + 1, -1))
     if far:
         wait("y", *vw)
         Y.dma_start(T.mdo[:, :], blk(T.big, r)[0:128:16, :]).then_inc(T.sem.mo, 16)
         wait("p", "mo", 16)
         send(T.mdo[:, :], T.mdi[r], "m%d" % r, "lm", far)
-    if nb[1:]:
-        send(blk(T.big, r), blk(T.big, r), "w%d" % r, "lw", nb[1:])
+    wait("p", *vw)
+    send(blk(T.big, r), blk(T.big, r), "w%d" % r, "lw", nb)
+    aw = {}
+
+    def states(d):
+        u = d - near[0]
+        aw[d] = act(blk(T.nw, u), blk(T.big, d), ACTF.Identity, bias=T.n0[:, 4 + u:5 + u], dep=[acol, vw if d == r else ("w%d" % d, ne)])
+
+    def thrice(d):
+        for k in (1, 2):
+            aw["x"] = act(xtab(d, 1, r, k), xtab(d, 1, r), ACTF.Copy, dep=[last["t1"] if d == r else ("x%d" % d, ne)])
+    states(r)
+    thrice(r)
+    for d in sorted(nb):
+        thrice(d)
     for d in range(r - 1):
         qn = "ya"[d % 2]
         wait(qn, *pz)
         wait(qn, "m%d" % d, ne)
         eng[qn].dma_start(blk(T.big, d)[0:128:16, :], T.mdi[d]).then_inc(T.sem["ld%d" % d], 16)
-    for d in [r] + nb:
-        for k in (1, 2):
-            ax = act(xtab(d, 1, k), xtab(d, 1), ACTF.Copy, dep=[last["t"] if d == r else ("x%d" % d, 2 * ne)])
+    for d in sorted(nb):
+        states(d)
 
     nc = nu + 1
     m = 4 * nc
@@ -273,11 +310,11 @@ def rank_program(g, core, T, topo):
     fill(T.kq[:, 0:128:16], 16.0)
     ts(n0, m0, -1.0, 1.0, ALU.mult, ALU.add)
     ts(T.n0[:, 2:3], m0, 16.0, qcol, ALU.mult, ALU.add)
+    ts(T.n0[:, 3:4], qcol, -16.0, None, ALU.add)
     fill(T.gs[:, 128:144], 0.0)
-    fill(T.cab[:, :], 0.0)
-    fill(T.ef[:, :], 0.0)
-    ts(T.iq[:, 0:2], T.iq[:, 0:2], qcol, None, ALU.add)
-    v = ts(T.gl[:, :], T.mg[:, 0:8], qcol, None, ALU.add)
+    fill(T.val[:, :], 0.0)
+    v = ts(T.iq[:, 0:2], T.iq[:, 0:2], qcol, ONE, ALU.add, ALU.mult)
+    ts(T.gl0[:, :], T.mq[:, 0:8], gcol, T.n0[:, 3:4], ALU.is_equal, ALU.mult, dep=[v])
     for u in range(nc):
         d = near[0] - 1 + u
         for k in range(2):
@@ -285,68 +322,74 @@ def rank_program(g, core, T, topo):
             ts(T.thr[:, 4 * k + u:4 * k + u + 1], m0, b - a, a, ALU.mult, ALU.add)
         for o in (blk(T.mk1, 2 * u, 16), blk(T.mk3, u, 16)):
             if 0 < u < nu:
-                cp(o, T.dg[:, 0:16], dep=[v])
+                cp(o, T.dg[:, 0:16])
             else:
-                ts(o, T.dg[:, 0:16], n0 if u else m0, None, ALU.mult, dep=[v])
+                ts(o, T.dg[:, 0:16], n0 if u else m0, None, ALU.mult)
     ts(T.tri0[:, :], T.kq[:, :], T.n0[:, 2:3], None, ALU.is_gt)
     v = ts(T.tri1[:, :], T.kq[:, :], T.n0[:, 2:3], None, ALU.is_lt)
     ts(T.sga[:, :], T.sg[:, :], n0, None, ALU.mult)
     ts(T.sgb[:, :], T.sg[:, :], m0, None, ALU.mult)
-    tt(T.lt[:, :], T.tri0[:, :], T.sg[:, :], ALU.mult, dep=[v])
+    ts(T.gl[:, :], T.gl0[:, :], 16.0, None, ALU.add, dep=[v])
+    tt(T.lt[:, :], T.tri0[:, :], T.sg[:, :], ALU.mult)
     vs = tt(T.gt[:, :], T.tri1[:, :], T.sg[:, :], ALU.mult)
 
     for d in range(near[-1] + 1):
-        vs = cp(T.s[:, 2 * d + 2:2 * d + 18], T.big[:, 0:128 * d + 128].indirect(T.s[:, 2 * d:2 * d + 1]),
-                dep=[vs] + ([] if d == r else [("w%d" % d, ne)] if d in near else [("ld%d" % d, 16)]))
+        win = T.nw[:, 0:128 * (d - near[0] + 1)] if d in near else blk(T.big, d)
+        vs = cp(T.s[:, 2 * d + 2:2 * d + 18], win.indirect(T.s[:, 2 * d:2 * d + 1]),
+                dep=[vs, max(aw[e] for e in near if e <= d) if d in near else ("ld%d" % d, 16)])
     a, n1, n3 = 2 * near[0], 32 * nc - 16, 16 * nc
-    v = tt(T.g2[:, 0:n1], T.xe[:, 0:128 * (near[-1] + 2)].indirect(T.s[:, a:a + 2 * nc - 1]), T.mk1[:, 0:n1], ALU.mult, dep=[vs, ax])
+    v = tt(T.g2[:, 0:n1], T.xe[:, 0:128 * nc].indirect(T.s[:, a:a + 2 * nc - 1]), T.mk1[:, 0:n1], ALU.mult,
+           dep=[vs, aw["x"]] + [("e%d" % d, ne) for d in nb])
     v = scan(T.sc1[:, 0:n1], T.rs[:, 0:n1], T.g2[:, 0:n1], ALU.mult, ALU.add, dep=[v])
     ve, vo = T.sc1[:, 15:n1:32], T.sc3[:, 15:n3:16]
     v = ts(T.ls2[:, 0:nc], ve, 1.0 / 4096, 1.0 / 8192 - 0.5, ALU.mult, ALU.add, dep=[v])
     vi = cp(T.vi[:, 0:nc], ve)
     v = tt(T.g3[:, 0:n3], T.xo[:, 0:384 * nu].indirect(T.ls2[:, 0:nc]), T.mk3[:, 0:n3], ALU.mult, dep=[v])
     for k in range(2):
-        tt(T.cab[:, k:m:4], ve, T.thr[:, 4 * k:4 * k + nc], ALU.is_ge)
-    scan(T.sc3[:, 0:n3], T.rs[:, 0:n3], T.g3[:, 0:n3], ALU.mult, ALU.add, dep=[v])
+        vc = tt(T.ca[:, 4 * k:4 * k + nc], ve, T.thr[:, 4 * k:4 * k + nc], ALU.is_ge)
+    vf = scan(T.sc3[:, 0:n3], T.rs[:, 0:n3], T.g3[:, 0:n3], ALU.mult, ALU.add, dep=[v])
     v = scan(T.si3[:, 0:n3], T.rs[:, 0:n3], T.g3[:, 0:n3], ALU.mult, ALU.add)
 
     def numbers(eo, src, dep):
         ts(T.ei[:, 2 * eo:m:4], src, 63, None, ALU.bitwise_and, dep=[dep])
         return ts(T.ei[:, 2 * eo + 1:m:4], src, 6, 63, ALU.logical_shift_right, ALU.bitwise_and)
+    for k in range(2):
+        act(T.cab[:, k:m:4], T.ca[:, 4 * k:4 * k + nc], ACTF.Copy, scale=ONE, dep=[vc])
+    ac = ("a", cnt["a"])
     numbers(0, T.vi[:, 0:nc], vi)
     for k in range(2):
-        vc = ts(T.cab[:, 2 + k:m:4], vo, 4096.0 * 128 * (k + 1), None, ALU.is_ge, dep=[v])
+        vc = ts(T.cab[:, 2 + k:m:4], vo, 4096.0 * 128 * (k + 1), ONE, ALU.is_ge, ALU.mult, dep=[vf])
     v = numbers(1, T.si3[:, 15:n3:16], v)
-    vee = scan(T.ee[:, 1:m + 1], T.cab[:, 0:m], T.cab[:, 0:m], ALU.add, ALU.max, dep=[vc])
+    vee = scan(T.ee[:, 1:m + 1], T.cab[:, 0:m], T.cab[:, 0:m], ALU.add, ALU.max, dep=[vc, ac])
+    v = tt(T.val[:, 0:m], T.ei[:, 0:m], T.cab[:, 0:m], ALU.add, dep=[v])
+    ags = act(T.gs[:, 0:128], T.val[:, :].indirect(T.gl[:, :]), ACTF.Relu, bias=1.0 - ONE, dep=[v])
     told = [d for d in range(N - 1, r, -1) if r in [s for s, _ in tellers(d)]]
     if told:
-        mm(T.pt[:, 0:nu], T.sga[:, :], T.ee[:, 8:m + 1:4], True, False, dep=[vee])
-        ttot = mm(T.pt[:, 0:nu], T.sgb[:, :], T.ee[:, 4:m - 3:4], False, True)
+        wait("p", *vee)
+        send(T.ee[:, :], blk(T.cin, r, 24), "c%d" % r, "lc", told)
     mm(T.pq[:, 0:nc], T.gt[:, :], T.ee[:, 0:m:4], True, False, dep=[vee])
     tp = mm(T.pq[:, 0:nc], T.lt[:, :], T.ee[:, 4:m + 1:4], False, True)
-    if told:
-        wait("p", *act(T.tot[:, 0:nu], T.pt[:, 0:nu], ACTF.Copy, dep=[ttot]))
-        send(T.tot[:, 0:nu], T.cin[:, 4 * r:4 * r + nu], "c%d" % r, "lc", told)
 
     u0 = 1 if r else 0
     nx_ = 2 * (nc - u0)
-    scan(T.eef[:, 1:m + 1], T.cab[:, 0:m], T.cab[:, 0:m], ALU.add, ALU.max)
-    v = ts(T.ef[:, 0:m], T.ei[:, 0:m], 1, None, ALU.add, dep=[v])
-    v = tt(T.val[:, :], T.ef[:, :], T.cab[:, :], ALU.mult, dep=[v])
-    vgv = tt(T.gs[:, 0:128], T.val[:, :].indirect(T.gl[:, :]), T.sg[:, :], ALU.mult, dep=[v])
+    v = scan(T.eef[:, 1:m + 1], T.cab[:, 0:m], T.cab[:, 0:m], ALU.add, ALU.max)
     yp = T.py[:, 0:wide]
     for x in range(nx_):
         e = 2 * (x + 2 * u0)
         vo = ts(T.oh[:, 64 * x:64 * x + wide + 1], T.iot[:, 0:wide + 1], T.eef[:, e:e + 1], T.pq[:, e // 4:e // 4 + 1],
-                ALU.subtract, ALU.is_equal, dep=[tp])
+                ALU.subtract, ALU.is_equal, dep=[tp, v])
         for k in range(2):
             ty = mm(yp, T.gs[:, e + k:e + k + 128], T.oh[:, 64 * x + 1 - k:64 * x + 1 - k + wide], x + k == 0, x + k == nx_,
-                    dep=[vo, vgv])
+                    dep=[vo, ags])
     if r > 1:
-        cols = [T.cin[:, 4 * s + c:4 * s + c + 1] for s, c in tellers(r)]
-        more = (cols[1], ALU.subtract, ALU.subtract) if cols[1:] else (None, ALU.subtract)
-        vl = ts(T.lsh[:, 0:2], T.iq[:, 0:2], cols[0], *more, dep=[("c%d" % s, ne) for s, _ in tellers(r)])
+        sums = []
+        for s, c in reversed(tellers(r)):
+            a = 24 * s + 4 * c + 8
+            sums += [(s, T.sg, a)] if s or c else [(s, T.sga, a), (s, T.sgb, a - 4)]
+        for k, (s, lh, a) in enumerate(sums):
+            tb_ = mm(T.pt[:, 0:1], lh[:, :], T.cin[:, a:a + 1], k == 0, k == len(sums) - 1, dep=[("c%d" % s, ne)])
         v = cp(T.zl[:, :], yp, dep=[ty])
+        vl = ts(T.lsh[:, 0:2], T.iq[:, 0:2], T.pt[:, 0:1], 1.0 / ONE, ALU.subtract, ALU.mult, dep=[tb_])
         vy = ts(T.ys[:, :], T.zl[:, :].indirect(T.lsh[:, 0:2]), -1.0, None, ALU.add, dep=[v, vl])
     else:
         vy = ts(T.ys[:, :], yp, -1.0, None, ALU.add, dep=[ty])
@@ -354,8 +397,8 @@ def rank_program(g, core, T, topo):
     Y.dma_start(T.y[:, :], T.ys[0:128:16, :]).then_inc(T.sem.yo, 16)
 
     wait("y", "yo", 16)
-    wait("p", "lx", len(on))
-    wait("p", "lw", ne * len(nb))
+    wait("p", "lx", ne + len(inside(r)))
+    wait("p", "lw", ne)
     if told:
         wait("p", "lc", ne)
     if far:

@@ -6,13 +6,13 @@ ACTF = ActivationFunctionType
 F, B, H, I4, U2 = "float32", "bfloat16", "float16", "int32", "uint16"
 SBUF = {
     I4: "nxi:512 emi:512 ipi:8 qgi:8 vi:8 si3:64 ei:16",
-    B: "ones:128 nil:128 iob:128 jj:2048 wa0:128 wa1:128 wb0:128 wb1:128 wc0:128 wc1:128 wu:128 big:1024 rep:256 sg:128 sga:128 "
-       "sgb:128 gt:128 lt:128 ee:24 cin:192 gs:144 oh:384",
+    B: "ones:128 nil:128 iob:128 jj:2048 wa0:128 wa1:128 wb0:128 wb1:128 wc0:128 wc1:128 wu:128 big:1024 rep:256 sg:128 eye:128 low:128 "
+       "gt:128 lt:128 ee:32 cin:80 gs:96 oh:384",
     H: "emh:512 sela:128",
-    F: "qgf:8 hm:8 mq:128 kq:128 mg:128 rm:16 n0:8 iot:56 iq:8 tri0:128 tri1:128 nw:384 xe:512 xo:1152 dg:128 "
-       "rs:128 md:256 ms:256 mk1:112 mk3:64 thr:8 val:24 g2:112 g3:64 sc1:112 sc3:64 ca:8 cab:16 eef:24 gl0:8 "
-       "zl:48 ys:32",
-    U2: "s:48 lm:16 ls2:8 gl:8 lsh:8",
+    F: "qgf:8 hm:8 mq:128 kq:128 mg:128 rm:16 n0:8 iot:40 c0:8 tri0:128 tri1:128 nw:384 xe:512 xo:1152 "
+       "rs:128 ms:256 mk1:112 mk3:64 thr:8 val:24 g2:112 g3:64 sc1:112 sc3:64 ca:8 cab:20 eef:24 gl0:8 f0:48 "
+       "ys:32",
+    U2: "s:48 sr:24 s0:112 lm:16 ls2:8 gl:8",
 }
 SCRATCH = {w.split(":")[0]: ("sbuf", [128, int(w.split(":")[1])], d) for d, ws in SBUF.items() for w in ws.split()}
 SCRATCH.update({
@@ -23,10 +23,11 @@ SCRATCH.update({
     "pl": ("psum", [128, 8, 64], F),
 })
 SCRATCH.update({n: ("psum", [128, 512], F) for n in "pb pe po pq pt py".split()})
-SEMAPHORES = ("v a t p ds mo yo xh lx lw lm lc".split() + [s + str(t) for s in ("dn", "de") for t in range(4)]
+SEMAPHORES = ("v a t p ds mo yo xh h lh lx lw lm lc".split() + [s + str(t) for s in ("dn", "de") for t in range(4)]
               + [s + str(r) for s in ("x", "e", "w", "m", "c", "ld") for r in range(8)])
 CUTS = (0, 10, 20, 32)
-TURNS = (1, 0, 2)
+TURNS = (1, 2, 0)
+HEAD = 2
 ONE = 64.0
 
 
@@ -36,6 +37,10 @@ def tellers(r):
         out.append((m - 2, 2) if m >= 3 else (0, m - 1))
         m -= 3
     return out
+
+
+def maps(r):
+    return list(range(HEAD, r - 1)) if r > HEAD + 2 else []
 
 
 def rank_program(g, core, T, topo):
@@ -68,7 +73,7 @@ def rank_program(g, core, T, topo):
     if r is None:
         for d in range(N):
             if core == helper(d):
-                to = [e for e in (d + 1, d - 1) if 0 <= e < N]
+                to = [e for e in (d - 1, d + 1) if 0 <= e < N]
                 out = topo.engines(core, cores[to[0]])
                 g.wait_ge(T.sem.xh, len(inside(d)))
                 g.remote_dma_fused([transfer(xtab(d, 0, d), [xtab(d, 0, e) for e in to], "e%d" % d, [cores[e] for e in to], out)],
@@ -82,6 +87,8 @@ def rank_program(g, core, T, topo):
     nb = [d for d in (r + 1, r - 1) if 0 <= d < N]
     near = sorted(nb + [r])
     nu = len(near)
+    nc = nu + 1
+    m = 4 * nc
 
     def wait(q, name, val):
         if val > seen.get((q, name), 0):
@@ -131,14 +138,17 @@ def rank_program(g, core, T, topo):
     pib = iota(T.iob[:, :], [[1, 128]], 0, 0)
     pmq = iota(T.mq[:, :], [[0, 8], [1, 16]], 0, 0)
     pmg = iota(T.mg[:, :], [[1, 8], [0, 16]], 0, 0)
-    iota(T.kq[:, :], [[0, 8], [1, 16]], 0, 0)
-    wide = 48 if r > 1 else 32
-    base = 24 if r > 1 else 32 * r
-    iota(T.iot[:, 0:wide + 1], [[int(ONE), wide + 1]], int(ONE) * (base - 1), 0)
-    iota(T.iq[:, 0:2], [[16, 2]], 32 * r - base, 0)
+    do("p", lambda: g.affine_select(T.kq[:, :], T.mq[:, :], [[0, 8], [1, 16]], ALU.is_gt, 16.0, 0, 0), pmq)
+    p1 = iota(T.tri0[:, :], [[0, 128]], 1, 0)
+    do("p", lambda: g.affine_select(T.eye[:, :], T.tri0[:, :], [[-1, 128]], ALU.is_equal, 0.0, 0, 1), p1)
+    do("p", lambda: g.affine_select(T.rs[:, :], T.tri0[:, :], [[0, 8], [1, 16]], ALU.is_gt, 0.0, 0, 0))
+    for o in (T.ee[:, :], T.eef[:, :], T.val[:, :], T.cab[:, :], T.mk1[:, :]) + ((blk(T.nw, 0),) if r == HEAD else ()):
+        iota(o, [[0, o.shape[1]]], 0, 0)
+    iota(T.iot[:, 0:33], [[int(ONE), 33]], int(ONE) * (32 * r - 1), 0)
+    iota(T.gl0[:, :], [[2, 8]], (4 if r else 0) - 16, 0)
     pz = iota(blk(T.xe, nu), [[0, 128]], 0, 0)
-    if r > 1:
-        pz = iota(T.big[:, 0:128 * (r - 1)], [[0, 128 * (r - 1)]], 0, 0)
+    if maps(r):
+        pz = iota(T.big[:, 128 * HEAD:128 * (r - 1)], [[0, 128 * (r - 1 - HEAD)]], 0, 0)
 
     fill(T.nil[0:1, :], 0.0)
     von = fill(T.ones[0:1, :], 1.0)
@@ -160,11 +170,18 @@ def rank_program(g, core, T, topo):
         jd[j] = ts(blk(T.jj, j), T.iob[:, :], T.rm[:, j:j + 1], None, ALU.mult, dep=[vrm, pib])
     for u in range(nu):
         acol = act(T.n0[:, 4 + u:5 + u], m0, ACTF.Identity, scale=128.0, bias=128.0 * u)
+    n0 = T.n0[:, 1:2]
+    act(n0, m0, ACTF.Identity, scale=-1.0, bias=1.0)
+    for u in range(nc):
+        d = near[0] - 1 + u
+        for k in range(2):
+            a, b = (4096.0 * (xoff(e) + 128 * (k + 1)) for e in (d, d + 1))
+            acol = act(T.thr[:, 4 * k + u:4 * k + u + 1], m0, ACTF.Identity, scale=b - a, bias=a)
     for eo in range(2):
         vrow = cp(T.syr[0:1, eo:16:2, :], T.syi[0:1, :, eo:32:2], dep=[("ds", 32)])
-    tbc = mm(T.pb[:, 0:256], T.ones[0:1, :], T.syr[0:1, :, :], True, True, dep=[vrow])
-    ts(T.dg[:, :], T.mq[:, :], qcol, None, ALU.is_equal, dep=[pmq])
-    ts(T.rs[:, :], T.mq[:, :], 0.0, None, ALU.is_gt)
+    for h in range(2):
+        tbc = mm(T.pb[64 * h:64 * h + 64, 0:128], T.ones[0:1, 0:64], T.syr[0:1, 8 * h:8 * h + 8, :], True, True, dep=[vrow])
+    vlow = ts(T.low[:, :], T.mq[:, :], qcol, -256.0, ALU.not_equal, ALU.mult, dep=[pmq])
     vt = []
     last = {}
     for t in range(4):
@@ -173,9 +190,7 @@ def rank_program(g, core, T, topo):
                    dep=[("dn%d" % t, 16)])
         vt.append(v)
         if t == 0:
-            for h in range(2):
-                hs = slice(64 * h, 64 * h + 64)
-                vsa = ts(T.sela[hs, :], T.pb[hs, 128 * h:128 * h + 128], T.qgf[hs, 2:3], None, ALU.is_equal, dep=[tbc])
+            vsa = ts(T.sela[:, :], T.pb[:, 0:128], T.qgf[:, 2:3], None, ALU.is_equal, dep=[tbc])
     for h in range(2):
         vsm = ts(T.selm[:, :, 16 * h:16 * h + 16], T.sela[:, :], T.hm[:, h:h + 1], None, ALU.mult, dep=[vsa])
     vsg = ts(T.sg[:, :], T.mg[:, :], gcol, None, ALU.is_equal, dep=[pmg])
@@ -187,16 +202,15 @@ def rank_program(g, core, T, topo):
         for c in range(8):
             tof = mm(T.pl[32 * t:32 * t + 32, 0:4, c:64:8], T.tb[:, 8 * t + c, :], T.sela[:, 32 * t:32 * t + 32], True, True,
                      dep=[vt[t], vsa])
-    for k in range(6):
-        for part in (2, 1, 0):
-            if 0 <= k - part < 4:
-                b = 3 - (k - part)
-                if part == 0:
-                    last[b] = cp(T.oi[:, b, :], T.pl[:, b, :], dep=[tof])
-                elif part == 1:
-                    last[b] = ts(T.oi2[:, b, :], T.oi[:, b, :], 127, None, ALU.bitwise_and, dep=[last[b]])
-                else:
-                    last[b] = cp(T.off[:, b, :], T.oi2[:, b, :], dep=[last[b]])
+    done = [0] * 4
+    for b in (3, 2, 1, 3, 2, 0, 3, 2, 1, 0, 1, 0):
+        if done[b] == 0:
+            last[b] = cp(T.oi[:, b, :], T.pl[:, b, :], dep=[tof])
+        elif done[b] == 1:
+            last[b] = ts(T.oi2[:, b, :], T.oi[:, b, :], 127, None, ALU.bitwise_and, dep=[last[b]])
+        else:
+            last[b] = cp(T.off[:, b, :], T.oi2[:, b, :], dep=[last[b]])
+        done[b] += 1
 
     def add(t, eo, rhs, dep):
         mm(px[eo][32 * t:32 * t + 32, :], T.selm[:, 2 * t + eo, :], rhs, False, False, dep=dep)
@@ -231,14 +245,15 @@ def rank_program(g, core, T, topo):
     def listed(ch, part):
         ps = (T.pt, T.pb)[ch][:, 0:128]
         if part == 0:
-            vm[ch] = tt(blk(T.md, ch), ps, T.dg[:, :], ALU.mult, dep=[mm(ps, blk(T.rep, ch), prev[ch][0], True, True, dep=[arep, prev[ch][1]])])
-        elif part == 1:
-            vm[ch] = scan(blk(T.ms, ch), T.rs[:, :], blk(T.md, ch), ALU.mult, ALU.add, dep=[vm[ch]])
+            mm(ps, T.eye[:, :], T.low[:, :], True, False, dep=[vlow, pz])
+            v = mm(ps, blk(T.rep, ch), prev[ch][0], False, True, dep=[arep, prev[ch][1]])
+            vm[ch] = scan(blk(T.ms, ch), T.rs[:, :], ps, ALU.mult, ALU.max, dep=[v, pz])
         else:
             vm[ch] = cp(blk(T.lm, ch, 8), blk(T.ms, ch)[:, 15:128:16], dep=[vm[ch]])
-    todo = [(ch, part) for part in range(3) for ch in (1, 0)]
+    todo = [(ch, part) for part in range(2) for ch in (1, 0)]
+    turns = TURNS if r else TURNS[::-1]
     for n in range(CUTS[3] - CUTS[2]):
-        for ch in TURNS:
+        for ch in turns:
             i = CUTS[ch + 1] - 1 - n
             if i < CUTS[ch]:
                 continue
@@ -254,31 +269,50 @@ def rank_program(g, core, T, topo):
             else:
                 dw = tt(o, src, blk(T.jj, i // 2), ALU.add, dep=dep + [jd[i // 2]])
             prev[ch] = (o, dw)
-            if n == 1 and ch != TURNS[2]:
-                entries(2 + TURNS.index(ch))
+            if n == 1 and ch != turns[2]:
+                entries(2 + turns.index(ch))
         if n in (3, 4):
             table(4 - n)
-    for x in todo:
-        listed(*x)
-    v = tt(T.wu[:, :], prev[2][0].indirect(blk(T.lm, 1, 8)), prev[1][0], ALU.add, dep=[vm[1], prev[2][1]])
-    vw = tt(blk(T.big, r), T.wu[:, :].indirect(blk(T.lm, 0, 8)), prev[0][0], ALU.add, dep=[v, vm[0]])
+    if r:
+        for x in todo:
+            listed(*x)
+        v = tt(T.wu[:, :], prev[2][0].indirect(blk(T.lm, 1, 8)), prev[1][0], ALU.add, dep=[vm[1], prev[2][1]])
+        vw = tt(blk(T.big, r), T.wu[:, :].indirect(blk(T.lm, 0, 8)), prev[0][0], ALU.add, dep=[v, vm[0]])
+    else:
+        fill(T.s0[:, :], 0)
+        v = fill(T.sr[:, :], 0)
+        for ch in range(3):
+            lst, j = T.s0[:, 16 + 32 * ch:17 + 32 * ch], CUTS[ch] // 2
+            v = cp(blk(T.f0, ch, 16), prev[ch][0].indirect(lst), dep=[v, prev[ch][1]])
+            if ch < 2:
+                v = cp(T.s0[:, 48 + 32 * ch - j:64 + 32 * ch - j], prev[ch][0].indirect(lst))
+        cols = [T.f0[:, 16 * ch + CUTS[ch] // 2:16 * ch + CUTS[ch] // 2 + 1] for ch in range(3)]
+        vw = ts(T.s0[:, 2:3], cols[0], cols[1], cols[2], ALU.add, ALU.add, dep=[v])
+        ts(T.sr[:, 2:3], cols[0], cols[1], cols[2], ALU.add, ALU.add)
 
     def send(src, dst, sem, lsem, dests):
         g.remote_dma_fused([transfer(src, [dst] * len(dests), sem, [cores[d] for d in dests], topo.engines(core, cores[dests[0]]))],
                            local_sem=T.sem[lsem])
     ne = len(topo.engines(core, cores[nb[0]]))
     wait("p", *last["t1"])
-    send(xtab(r, 1, r), xtab(r, 1, r), "x%d" % r, "lx", nb)
+    send(xtab(r, 1, r), xtab(r, 1, r), "x%d" % r, "lx", sorted(nb))
     wait("p", *last["t0"])
     g.remote_dma_fused([transfer(xtab(r, 0, r), [xtab(r, 0, r)], "xh", [helper(r)], inside(r))], local_sem=T.sem.lx)
-    far = list(range(N - 1, r + 1, -1))
+    far = [d for d in range(N - 1, r + 1, -1) if r in maps(d)]
+    wait("p", *vw)
+    late = [r + 2] if r == HEAD else [r + 1] if far and maps(r + 1) else []
+    early = [d for d in reversed(nb) if d not in late]
+    if r:
+        send(blk(T.big, r), blk(T.big, r), "w%d" % r, "lw", early)
+    else:
+        send(T.s0[:, 0:8], T.sr[:, 0:8], "w0", "lw", [1, 2])
     if far:
         wait("y", *vw)
         Y.dma_start(T.mdo[:, :], blk(T.big, r)[0:128:16, :]).then_inc(T.sem.mo, 16)
         wait("p", "mo", 16)
         send(T.mdo[:, :], T.mdi[r], "m%d" % r, "lm", far)
-    wait("p", *vw)
-    send(blk(T.big, r), blk(T.big, r), "w%d" % r, "lw", nb)
+    if late:
+        send(blk(T.big, r), blk(T.big, r), "w%d" % r, "lw", late)
     aw = {}
 
     def states(d):
@@ -288,60 +322,69 @@ def rank_program(g, core, T, topo):
     def thrice(d):
         for k in (1, 2):
             aw["x"] = act(xtab(d, 1, r, k), xtab(d, 1, r), ACTF.Copy, dep=[last["t1"] if d == r else ("x%d" % d, ne)])
-    states(r)
+    for u in range(nc):
+        for o in (blk(T.mk1, 2 * u, 16), blk(T.mk3, u, 16)):
+            act(o, T.rm[:, :], ACTF.Copy, scale=1.0 if 0 < u < nu else n0 if u else m0, dep=[pz])
+    if r >= HEAD:
+        states(r)
     thrice(r)
     for d in sorted(nb):
         thrice(d)
-    for d in range(r - 1):
+
+    fill(T.s[:, 0:16], 0)
+    ts(T.n0[:, 2:3], m0, 16.0, qcol, ALU.mult, ALU.add)
+    v = ts(T.c0[:, 2:3], qcol, 8.0, None, ALU.is_ge)
+    ts(T.c0[:, 3:4], T.c0[:, 2:3], 8.0, gcol, ALU.mult, ALU.add, dep=[v, pz])
+    v = ts(T.tri0[:, :], T.kq[:, :], T.n0[:, 2:3], None, ALU.is_gt)
+    ts(T.c0[:, 4:5], T.c0[:, 3:4], qcol, None, ALU.is_equal, dep=[v])
+    v = ts(T.tri1[:, :], T.kq[:, :], T.n0[:, 2:3], None, ALU.is_lt)
+    ts(T.gl0[:, :], T.gl0[:, :], T.c0[:, 2:3], T.c0[:, 4:5], ALU.add, ALU.mult, dep=[v])
+    v = tt(T.lt[:, :], T.tri0[:, :], T.sg[:, :], ALU.mult)
+
+    def follow():
+        v = cp(T.sr[:, 4:20], blk(T.big, 1).indirect(T.sr[:, 2:3]), dep=[vw] + [("w%d" % d, ne) for d in range(HEAD) if d != r])
+        if r < HEAD:
+            wait("p", *v)
+            send(T.sr[:, 0:8], T.sr[:, 0:8], "h", "lh", [d for d in (6, 7, 5, 4, 3) if bool(maps(d)) != bool(r)])
+        return v
+    vh = follow() if r == 1 else None
+    tt(T.gt[:, :], T.tri1[:, :], T.sg[:, :], ALU.mult)
+    vs = ts(T.gl[:, :], T.gl0[:, :], 16.0, None, ALU.add, dep=[v])
+    if r in (0, HEAD):
+        vh = follow()
+    for d in maps(r):
         qn = "ya"[d % 2]
         wait(qn, *pz)
         wait(qn, "m%d" % d, ne)
         eng[qn].dma_start(blk(T.big, d)[0:128:16, :], T.mdi[d]).then_inc(T.sem["ld%d" % d], 16)
     for d in sorted(nb):
-        states(d)
+        if d >= HEAD:
+            states(d)
 
-    nc = nu + 1
-    m = 4 * nc
-    n0 = T.n0[:, 1:2]
-    fill(T.s[:, 0:16], 0)
-    fill(T.ee[:, :], 0.0)
-    fill(T.eef[:, :], 0.0)
-    fill(T.mk1[:, :], 0.0, dep=[pz])
-    fill(T.kq[:, 0:128:16], 16.0)
-    ts(n0, m0, -1.0, 1.0, ALU.mult, ALU.add)
-    ts(T.n0[:, 2:3], m0, 16.0, qcol, ALU.mult, ALU.add)
-    ts(T.n0[:, 3:4], qcol, -16.0, None, ALU.add)
-    fill(T.gs[:, 128:144], 0.0)
-    fill(T.val[:, :], 0.0)
-    v = ts(T.iq[:, 0:2], T.iq[:, 0:2], qcol, ONE, ALU.add, ALU.mult)
-    ts(T.gl0[:, :], T.mq[:, 0:8], gcol, T.n0[:, 3:4], ALU.is_equal, ALU.mult, dep=[v])
-    for u in range(nc):
-        d = near[0] - 1 + u
-        for k in range(2):
-            a, b = (4096.0 * (xoff(e) + 128 * (k + 1)) for e in (d, d + 1))
-            ts(T.thr[:, 4 * k + u:4 * k + u + 1], m0, b - a, a, ALU.mult, ALU.add)
-        for o in (blk(T.mk1, 2 * u, 16), blk(T.mk3, u, 16)):
-            if 0 < u < nu:
-                cp(o, T.dg[:, 0:16])
-            else:
-                ts(o, T.dg[:, 0:16], n0 if u else m0, None, ALU.mult)
-    ts(T.tri0[:, :], T.kq[:, :], T.n0[:, 2:3], None, ALU.is_gt)
-    v = ts(T.tri1[:, :], T.kq[:, :], T.n0[:, 2:3], None, ALU.is_lt)
-    ts(T.sga[:, :], T.sg[:, :], n0, None, ALU.mult)
-    ts(T.sgb[:, :], T.sg[:, :], m0, None, ALU.mult)
-    ts(T.gl[:, :], T.gl0[:, :], 16.0, None, ALU.add, dep=[v])
-    tt(T.lt[:, :], T.tri0[:, :], T.sg[:, :], ALU.mult)
-    vs = tt(T.gt[:, :], T.tri1[:, :], T.sg[:, :], ALU.mult)
+    def heads():
+        v = None
+        for d in range(max(near[0] - 1, 0), HEAD):
+            o, col, u = T.s[:, 2 * d + 2:2 * d + 3], T.sr[:, 2 * d + 2:2 * d + 3], d - near[0]
+            v = ts(o, col, T.n0[:, 4 + u:5 + u] if u >= 0 else 0.0, None, ALU.add, dep=head + [acol])
+        return v
 
-    for d in range(near[-1] + 1):
-        win = T.nw[:, 0:128 * (d - near[0] + 1)] if d in near else blk(T.big, d)
-        vs = cp(T.s[:, 2 * d + 2:2 * d + 18], win.indirect(T.s[:, 2 * d:2 * d + 1]),
-                dep=[vs, max(aw[e] for e in near if e <= d) if d in near else ("ld%d" % d, 16)])
+    head = [vh or ("h", ne)]
+    for d in range(HEAD, near[-1] + 1):
+        u = d - near[0]
+        win = blk(T.big, d) if u < 0 else blk(T.nw, u) if d == HEAD else T.nw[:, 0:128 * (u + 1)]
+        vs = cp(T.s[:, 2 * d + 2:2 * d + 18], win.indirect((T.sr if d == HEAD else T.s)[:, 2 * d:2 * d + 1]),
+                dep=[vs, max(aw[e] for e in aw if e != "x" and e <= d) if d in near else
+                     ("ld%d" % d, 16) if d in maps(r) else ("w%d" % d, ne)] + head)
+        if d == HEAD:
+            heads()
+    if near[-1] < HEAD:
+        heads()
+    vs = ("v", cnt["v"])
     a, n1, n3 = 2 * near[0], 32 * nc - 16, 16 * nc
     v = tt(T.g2[:, 0:n1], T.xe[:, 0:128 * nc].indirect(T.s[:, a:a + 2 * nc - 1]), T.mk1[:, 0:n1], ALU.mult,
            dep=[vs, aw["x"]] + [("e%d" % d, ne) for d in nb])
     v = scan(T.sc1[:, 0:n1], T.rs[:, 0:n1], T.g2[:, 0:n1], ALU.mult, ALU.add, dep=[v])
-    ve, vo = T.sc1[:, 15:n1:32], T.sc3[:, 15:n3:16]
+    ve = T.sc1[:, 15:n1:32]
     v = ts(T.ls2[:, 0:nc], ve, 1.0 / 4096, 1.0 / 8192 - 0.5, ALU.mult, ALU.add, dep=[v])
     vi = cp(T.vi[:, 0:nc], ve)
     v = tt(T.g3[:, 0:n3], T.xo[:, 0:384 * nu].indirect(T.ls2[:, 0:nc]), T.mk3[:, 0:n3], ALU.mult, dep=[v])
@@ -350,57 +393,55 @@ def rank_program(g, core, T, topo):
     vf = scan(T.sc3[:, 0:n3], T.rs[:, 0:n3], T.g3[:, 0:n3], ALU.mult, ALU.add, dep=[v])
     v = scan(T.si3[:, 0:n3], T.rs[:, 0:n3], T.g3[:, 0:n3], ALU.mult, ALU.add)
 
-    def numbers(eo, src, dep):
-        ts(T.ei[:, 2 * eo:m:4], src, 63, None, ALU.bitwise_and, dep=[dep])
-        return ts(T.ei[:, 2 * eo + 1:m:4], src, 6, 63, ALU.logical_shift_right, ALU.bitwise_and)
+    def number(x, src, dep):
+        return ts(T.ei[:, x:m:4], src, 6 * (x % 2), 63, ALU.logical_shift_right, ALU.bitwise_and, dep=[dep])
     for k in range(2):
         act(T.cab[:, k:m:4], T.ca[:, 4 * k:4 * k + nc], ACTF.Copy, scale=ONE, dep=[vc])
     ac = ("a", cnt["a"])
-    numbers(0, T.vi[:, 0:nc], vi)
+    number(0, T.vi[:, 0:nc], vi)
     for k in range(2):
-        vc = ts(T.cab[:, 2 + k:m:4], vo, 4096.0 * 128 * (k + 1), ONE, ALU.is_ge, ALU.mult, dep=[vf])
-    v = numbers(1, T.si3[:, 15:n3:16], v)
-    vee = scan(T.ee[:, 1:m + 1], T.cab[:, 0:m], T.cab[:, 0:m], ALU.add, ALU.max, dep=[vc, ac])
-    v = tt(T.val[:, 0:m], T.ei[:, 0:m], T.cab[:, 0:m], ALU.add, dep=[v])
-    ags = act(T.gs[:, 0:128], T.val[:, :].indirect(T.gl[:, :]), ACTF.Relu, bias=1.0 - ONE, dep=[v])
-    told = [d for d in range(N - 1, r, -1) if r in [s for s, _ in tellers(d)]]
-    if told:
-        wait("p", *vee)
-        send(T.ee[:, :], blk(T.cin, r, 24), "c%d" % r, "lc", told)
-    mm(T.pq[:, 0:nc], T.gt[:, :], T.ee[:, 0:m:4], True, False, dep=[vee])
-    tp = mm(T.pq[:, 0:nc], T.lt[:, :], T.ee[:, 4:m + 1:4], False, True)
-
+        vc = ts(T.cab[:, 2 + k:m:4], T.sc3[:, 15:n3:16], 4096.0 * 128 * (k + 1), ONE, ALU.is_ge, ALU.mult, dep=[vf])
+    for k in range(2):
+        number(2 + k, T.si3[:, 15:n3:16], v)
+    vee = scan(T.ee[:, 1:21], T.cab[:, :], T.cab[:, :], ALU.add, ALU.max, dep=[vc, ac])
+    v = number(1, T.vi[:, 0:nc], vi)
+    scan(T.eef[:, 1:m + 1], T.cab[:, 0:m], T.cab[:, 0:m], ALU.add, ALU.max)
+    vv = v = tt(T.val[:, 0:m], T.ei[:, 0:m], T.cab[:, 0:m], ALU.add, dep=[v])
     u0 = 1 if r else 0
     nx_ = 2 * (nc - u0)
-    v = scan(T.eef[:, 1:m + 1], T.cab[:, 0:m], T.cab[:, 0:m], ALU.add, ALU.max)
-    yp = T.py[:, 0:wide]
+    ags = act(T.gs[:, 0:16 * nx_], T.val[:, :].indirect(T.gl[:, 0:nx_]), ACTF.Relu, bias=1.0 - ONE, dep=[v])
+    told = [d for d in range(N - 1, r, -1) if (r, nu - 1) in tellers(d)]
+    if told:
+        wait("p", *vee)
+        send(T.ee[:, 16:24], blk(T.cin, r, 8), "c%d" % r, "lc", told)
+    if r == 0:
+        v = ts(T.c0[:, 0:1], T.ee[:, 4:5], m0, None, ALU.mult, dep=[vee])
+        v = ts(T.c0[:, 1:2], T.ee[:, 8:9], n0, T.c0[:, 0:1], ALU.mult, ALU.add, dep=[v])
+        wait("p", *ts(T.ee[:, 24:28], T.mg[:, 0:4], T.c0[:, 1:2], None, ALU.add, dep=[v]))
+        send(T.ee[:, 24:32], blk(T.cin, r, 8), "c0", "lc", [d for d in range(N - 1, r, -1) if (0, 0) in tellers(d)])
+    sums = [(T.sg, blk(T.cin, s, 8)[:, 0:nc], ("c%d" % s, ne)) for s, c in reversed(tellers(r))]
+    k = len(sums) - (r > 2 * HEAD)
+    sums[k:k] = [(T.gt, T.ee[:, 0:m:4], vee), (T.lt, T.ee[:, 4:m + 1:4], vee)]
+    for k, (lh, rh, dep) in enumerate(sums):
+        tp = mm(T.pq[:, 0:nc], lh[:, :], rh, k == 0, k == len(sums) - 1, dep=[dep])
+
+    yp = T.py[0:8, 0:32]
     for x in range(nx_):
         e = 2 * (x + 2 * u0)
-        vo = ts(T.oh[:, 64 * x:64 * x + wide + 1], T.iot[:, 0:wide + 1], T.eef[:, e:e + 1], T.pq[:, e // 4:e // 4 + 1],
-                ALU.subtract, ALU.is_equal, dep=[tp, v])
+        vo = ts(T.oh[:, 64 * x:64 * x + 33], T.iot[:, 0:33], T.eef[:, e:e + 1], T.pq[:, e // 4:e // 4 + 1],
+                ALU.subtract, ALU.is_equal, dep=[tp, vv])
         for k in range(2):
-            ty = mm(yp, T.gs[:, e + k:e + k + 128], T.oh[:, 64 * x + 1 - k:64 * x + 1 - k + wide], x + k == 0, x + k == nx_,
-                    dep=[vo, ags])
-    if r > 1:
-        sums = []
-        for s, c in reversed(tellers(r)):
-            a = 24 * s + 4 * c + 8
-            sums += [(s, T.sg, a)] if s or c else [(s, T.sga, a), (s, T.sgb, a - 4)]
-        for k, (s, lh, a) in enumerate(sums):
-            tb_ = mm(T.pt[:, 0:1], lh[:, :], T.cin[:, a:a + 1], k == 0, k == len(sums) - 1, dep=[("c%d" % s, ne)])
-        v = cp(T.zl[:, :], yp, dep=[ty])
-        vl = ts(T.lsh[:, 0:2], T.iq[:, 0:2], T.pt[:, 0:1], 1.0 / ONE, ALU.subtract, ALU.mult, dep=[tb_])
-        vy = ts(T.ys[:, :], T.zl[:, :].indirect(T.lsh[:, 0:2]), -1.0, None, ALU.add, dep=[v, vl])
-    else:
-        vy = ts(T.ys[:, :], yp, -1.0, None, ALU.add, dep=[ty])
-    wait("y", *vy)
-    Y.dma_start(T.y[:, :], T.ys[0:128:16, :]).then_inc(T.sem.yo, 16)
+            ty = mm(yp, blk(T.gs, 2 * x + k, 8), T.oh[:, 64 * x + 1 - k:64 * x + 33 - k], x + k == 0, x + k == nx_, dep=[vo, ags])
+    wait("y", *ts(T.ys[0:8, :], yp, -1.0, None, ALU.add, dep=[ty]))
+    Y.dma_start(T.y[:, :], T.ys[0:8, :]).then_inc(T.sem.yo, 16)
 
     wait("y", "yo", 16)
     wait("p", "lx", ne + len(inside(r)))
-    wait("p", "lw", ne)
+    wait("p", "lw", 2 * ne if late else ne)
+    if r < HEAD:
+        wait("p", "lh", ne)
     if told:
-        wait("p", "lc", ne)
+        wait("p", "lc", ne if r else 2 * ne)
     if far:
         wait("p", "lm", ne)
     for name in ("v", "a", "t"):

@@ -5,14 +5,14 @@ ALU = AluOpType
 ACTF = ActivationFunctionType
 F, B, H, I4, U2 = "float32", "bfloat16", "float16", "int32", "uint16"
 SBUF = {
-    I4: "nxi:512 emi:512 ipi:8 qgi:8 vi:8 si3:64 ei:16",
-    B: "ones:128 nil:128 iob:128 jj:2048 wa0:128 wa1:128 wb0:128 wb1:128 wc0:128 wc1:128 wu:128 big:1024 rep:256 sg:128 eye:128 low:128 "
-       "gt:128 lt:128 ee:32 cin:80 gs:96 oh:384",
+    I4: "nxi:512 emi:512 ipi:8 qgi:8 sc1:64 sc3:64 ei:16 xn:1152",
+    B: "ones:128 nil:128 iob:128 jj:2048 wa0:128 wa1:128 wb0:128 wb1:128 wc0:128 wc1:128 wu:128 big:1024 rep:384 sg:128 eye:128 low:128 "
+       "gt:128 lt:128 en:88 e0:56 cin:32 gs:128 oh:512",
     H: "emh:512 sela:128",
-    F: "qgf:8 hm:8 mq:128 kq:128 mg:128 rm:16 n0:8 iot:40 c0:8 tri0:128 tri1:128 nw:384 xe:512 xo:1152 "
-       "rs:128 ms:256 mk1:112 mk3:64 thr:8 val:24 g2:112 g3:64 sc1:112 sc3:64 ca:8 cab:20 eef:24 gl0:8 f0:48 "
+    F: "qgf:8 hm:8 mq:128 kq:128 mg:128 rm:16 n0:8 iot:40 tri0:128 tri1:128 nw:384 xe:512 xo:1152 "
+       "rs:128 ms:256 mk3:64 thr:8 val:32 g2:64 g3:64 ca:8 cab:16 gn:72 mkn:64 g0:56 mk0:48 ce:8 gl0:8 f0:48 "
        "ys:32",
-    U2: "s:48 sr:24 s0:112 lm:16 ls2:8 gl:8",
+    U2: "s:48 sr:24 s0:112 sb:64 lm:32 ls2:8 gl:8",
 }
 SCRATCH = {w.split(":")[0]: ("sbuf", [128, int(w.split(":")[1])], d) for d, ws in SBUF.items() for w in ws.split()}
 SCRATCH.update({
@@ -31,16 +31,20 @@ HEAD = 2
 ONE = 64.0
 
 
+def near_of(r):
+    return list(range(max(min(r, 6) - 1, 0), min(r + 2, 8)))
+
+
+def users(d):
+    return [r for r in (0, 3, 1, 2, 6, 7, 5, 4) if r != d and d in near_of(r)]
+
+
 def tellers(r):
-    m, out = r - 1, []
-    while m > 0:
-        out.append((m - 2, 2) if m >= 3 else (0, m - 1))
-        m -= 3
-    return out
+    return {2: [(0, 0)], 3: [(1, 0)], 4: [(1, 1)], 5: [(2, 1), (0, 0)], 6: [(3, 1), (0, 1)], 7: [(3, 1), (0, 1)]}.get(r, [])
 
 
 def maps(r):
-    return list(range(HEAD, r - 1)) if r > HEAD + 2 else []
+    return list(range(HEAD, near_of(r)[0])) if r > HEAD + 2 else []
 
 
 def rank_program(g, core, T, topo):
@@ -68,12 +72,12 @@ def rank_program(g, core, T, topo):
         return 384 * (d % 3)
 
     def xtab(d, eo, at, k=0):
-        return blk(T.xo, 3 * (d % 3) + k) if eo else blk(T.xe, d - max(at - 1, 0))
+        return blk(T.xo, 3 * (d % 3) + k) if eo else blk(T.xe, d - near_of(at)[0])
     r = T.rank_of(core)
     if r is None:
         for d in range(N):
             if core == helper(d):
-                to = [e for e in (d - 1, d + 1) if 0 <= e < N]
+                to = users(d)
                 out = topo.engines(core, cores[to[0]])
                 g.wait_ge(T.sem.xh, len(inside(d)))
                 g.remote_dma_fused([transfer(xtab(d, 0, d), [xtab(d, 0, e) for e in to], "e%d" % d, [cores[e] for e in to], out)],
@@ -84,8 +88,8 @@ def rank_program(g, core, T, topo):
     eng = {"v": V, "a": A, "t": P, "p": g, "y": Y}
     cnt = {"v": 0, "a": 0, "t": 0, "p": 0}
     seen = {}
-    nb = [d for d in (r + 1, r - 1) if 0 <= d < N]
-    near = sorted(nb + [r])
+    near = near_of(r)
+    nb = [d for d in near if d != r]
     nu = len(near)
     nc = nu + 1
     m = 4 * nc
@@ -142,24 +146,27 @@ def rank_program(g, core, T, topo):
     p1 = iota(T.tri0[:, :], [[0, 128]], 1, 0)
     do("p", lambda: g.affine_select(T.eye[:, :], T.tri0[:, :], [[-1, 128]], ALU.is_equal, 0.0, 0, 1), p1)
     do("p", lambda: g.affine_select(T.rs[:, :], T.tri0[:, :], [[0, 8], [1, 16]], ALU.is_gt, 0.0, 0, 0))
-    for o in (T.ee[:, :], T.eef[:, :], T.val[:, :], T.cab[:, :], T.mk1[:, :]) + ((blk(T.nw, 0),) if r == HEAD else ()):
+    for o in (T.en[:, 0:16], T.val[:, :], T.gn[:, :], T.g0[:, :]):
         iota(o, [[0, o.shape[1]]], 0, 0)
     iota(T.iot[:, 0:33], [[int(ONE), 33]], int(ONE) * (32 * r - 1), 0)
-    iota(T.gl0[:, :], [[2, 8]], (4 if r else 0) - 16, 0)
+    iota(T.gl0[:, :], [[2, 8]], 2 * (r - near[0]) - 8, 0)
     pz = iota(blk(T.xe, nu), [[0, 128]], 0, 0)
     if maps(r):
-        pz = iota(T.big[:, 128 * HEAD:128 * (r - 1)], [[0, 128 * (r - 1 - HEAD)]], 0, 0)
+        pz = iota(T.big[:, 128 * HEAD:128 * near[0]], [[0, 128 * len(maps(r))]], 0, 0)
 
     fill(T.nil[0:1, :], 0.0)
     von = fill(T.ones[0:1, :], 1.0)
     ts(T.qgi[:, 0:1], T.ipi[:, 0:1], 15, None, ALU.bitwise_and, dep=[pi])
     ts(T.qgi[:, 2:3], T.ipi[:, 0:1], 63, None, ALU.bitwise_and)
+    ts(T.qgi[:, 3:4], T.ipi[:, 0:1], 3, 1, ALU.logical_shift_right, ALU.bitwise_and)
+    ts(T.qgi[:, 4:5], T.ipi[:, 0:1], 7, None, ALU.bitwise_and)
     v = ts(T.qgi[:, 1:2], T.ipi[:, 0:1], 4, None, ALU.logical_shift_right)
     qcol, gcol, m0 = T.qgf[:, 0:1], T.qgf[:, 1:2], T.rm[:, 0:1]
     ts(T.hm[:, 0:1], T.ipi[:, 0:1], 64.0, None, ALU.is_lt)
     ts(T.hm[:, 1:2], T.ipi[:, 0:1], 64.0, None, ALU.is_ge)
-    vqg = cp(T.qgf[:, 0:3], T.qgi[:, 0:3], dep=[v])
+    vqg = cp(T.qgf[:, 0:5], T.qgi[:, 0:5], dep=[v])
     vrm = ts(T.rm[:, :], T.rm[:, :], qcol, None, ALU.is_equal, dep=[vqg, pq])
+    ts(T.n0[:, 3:4], T.qgf[:, 4:5], gcol, None, ALU.is_equal)
     px = (T.pe[:, 0:128], T.po[:, 0:128])
     for o in px:
         mm(o, T.ones[0:1, :], T.nil[0:1, :], True, False, dep=[von])
@@ -168,9 +175,9 @@ def rank_program(g, core, T, topo):
         jd[j] = act(blk(T.jj, j), T.iob[:, :], ACTF.Copy, scale=T.rm[:, j:j + 1], dep=[vrm, pib])
     for j in range(12, 16):
         jd[j] = ts(blk(T.jj, j), T.iob[:, :], T.rm[:, j:j + 1], None, ALU.mult, dep=[vrm, pib])
-    for u in range(nu):
-        acol = act(T.n0[:, 4 + u:5 + u], m0, ACTF.Identity, scale=128.0, bias=128.0 * u)
-    n0 = T.n0[:, 1:2]
+    n0, lane0 = T.n0[:, 1:2], T.n0[:, 4:5]
+    act(T.n0[:, 2:3], m0, ACTF.Identity, scale=16.0, bias=qcol)
+    act(lane0, m0, ACTF.Copy, scale=128.0)
     act(n0, m0, ACTF.Identity, scale=-1.0, bias=1.0)
     for u in range(nc):
         d = near[0] - 1 + u
@@ -194,8 +201,8 @@ def rank_program(g, core, T, topo):
     for h in range(2):
         vsm = ts(T.selm[:, :, 16 * h:16 * h + 16], T.sela[:, :], T.hm[:, h:h + 1], None, ALU.mult, dep=[vsa])
     vsg = ts(T.sg[:, :], T.mg[:, :], gcol, None, ALU.is_equal, dep=[pmg])
-    for ch in range(2):
-        j = CUTS[ch + 1] // 2
+    for ch in range(3):
+        j = CUTS[ch + 1] // 2 % 16
         arep = act(blk(T.rep, ch), T.sg[:, :], ACTF.Copy, scale=T.rm[:, j:j + 1], dep=[vsg])
 
     for t in range(4):
@@ -273,9 +280,16 @@ def rank_program(g, core, T, topo):
                 entries(2 + turns.index(ch))
         if n in (3, 4):
             table(4 - n)
+        if n in (3, 5):
+            ts((T.tri0, T.tri1)[n // 4][:, :], T.kq[:, :], T.n0[:, 2:3], None, (ALU.is_gt, ALU.is_le)[n // 4], dep=[pz, acol])
+
+    def earlier():
+        tt(T.lt[:, :], T.tri0[:, :], T.sg[:, :], ALU.mult)
     if r:
         for x in todo:
             listed(*x)
+            if x == todo[0]:
+                earlier()
         v = tt(T.wu[:, :], prev[2][0].indirect(blk(T.lm, 1, 8)), prev[1][0], ALU.add, dep=[vm[1], prev[2][1]])
         vw = tt(blk(T.big, r), T.wu[:, :].indirect(blk(T.lm, 0, 8)), prev[0][0], ALU.add, dep=[v, vm[0]])
     else:
@@ -289,23 +303,23 @@ def rank_program(g, core, T, topo):
         cols = [T.f0[:, 16 * ch + CUTS[ch] // 2:16 * ch + CUTS[ch] // 2 + 1] for ch in range(3)]
         vw = ts(T.s0[:, 2:3], cols[0], cols[1], cols[2], ALU.add, ALU.add, dep=[v])
         ts(T.sr[:, 2:3], cols[0], cols[1], cols[2], ALU.add, ALU.add)
+        earlier()
 
     def send(src, dst, sem, lsem, dests):
         g.remote_dma_fused([transfer(src, [dst] * len(dests), sem, [cores[d] for d in dests], topo.engines(core, cores[dests[0]]))],
                            local_sem=T.sem[lsem])
     ne = len(topo.engines(core, cores[nb[0]]))
     wait("p", *last["t1"])
-    send(xtab(r, 1, r), xtab(r, 1, r), "x%d" % r, "lx", sorted(nb))
+    send(xtab(r, 1, r), xtab(r, 1, r), "x%d" % r, "lx", users(r))
     wait("p", *last["t0"])
     g.remote_dma_fused([transfer(xtab(r, 0, r), [xtab(r, 0, r)], "xh", [helper(r)], inside(r))], local_sem=T.sem.lx)
     far = [d for d in range(N - 1, r + 1, -1) if r in maps(d)]
     wait("p", *vw)
-    late = [r + 2] if r == HEAD else [r + 1] if far and maps(r + 1) else []
-    early = [d for d in reversed(nb) if d not in late]
+    late = [r + 2] if r == HEAD else []
     if r:
-        send(blk(T.big, r), blk(T.big, r), "w%d" % r, "lw", early)
+        send(blk(T.big, r), blk(T.big, r), "w%d" % r, "lw", users(r) if r > 1 else [0, 3])
     else:
-        send(T.s0[:, 0:8], T.sr[:, 0:8], "w0", "lw", [1, 2])
+        send(T.s0[:, 0:8], T.sr[:, 0:8], "w0", "lw", [1, 3])
     if far:
         wait("y", *vw)
         Y.dma_start(T.mdo[:, :], blk(T.big, r)[0:128:16, :]).then_inc(T.sem.mo, 16)
@@ -313,125 +327,160 @@ def rank_program(g, core, T, topo):
         send(T.mdo[:, :], T.mdi[r], "m%d" % r, "lm", far)
     if late:
         send(blk(T.big, r), blk(T.big, r), "w%d" % r, "lw", late)
-    aw = {}
-
-    def states(d):
-        u = d - near[0]
-        aw[d] = act(blk(T.nw, u), blk(T.big, d), ACTF.Identity, bias=T.n0[:, 4 + u:5 + u], dep=[acol, vw if d == r else ("w%d" % d, ne)])
-
-    def thrice(d):
-        for k in (1, 2):
-            aw["x"] = act(xtab(d, 1, r, k), xtab(d, 1, r), ACTF.Copy, dep=[last["t1"] if d == r else ("x%d" % d, ne)])
     for u in range(nc):
-        for o in (blk(T.mk1, 2 * u, 16), blk(T.mk3, u, 16)):
-            act(o, T.rm[:, :], ACTF.Copy, scale=1.0 if 0 < u < nu else n0 if u else m0, dep=[pz])
-    if r >= HEAD:
-        states(r)
-    thrice(r)
-    for d in sorted(nb):
-        thrice(d)
+        v = act(blk(T.mk3, u, 16), T.rm[:, :], ACTF.Copy, scale=1.0 if 0 < u < nu else n0 if u else m0)
+    v = act(T.mkn[:, 0:16 * nc], T.mk3[:, 0:16 * nc], ACTF.Copy, scale=ONE, dep=[v])
+    if r < HEAD:
+        for u in range(nu):
+            act(blk(T.mk0, u, 16), blk(T.mkn, u if u < nu - 1 else nu, 16), ACTF.Copy, dep=[v])
+    for d in [r] + nb:
+        for k in (1, 2):
+            ax = act(xtab(d, 1, r, k), xtab(d, 1, r), ACTF.Copy, dep=[last["t1"] if d == r else ("x%d" % d, ne)])
 
+    trio = [d for d in near if d >= HEAD]
+    lists = {}
+
+    def here(d):
+        return vw if d == r else ("w%d" % d, ne)
+
+    def as_list(k):
+        ps = (T.pt, T.pb)[k][:, 0:128]
+        mm(ps, T.eye[:, :], T.low[:, :], True, False, dep=[vw])
+        v = mm(ps, blk(T.rep, 2), blk(T.big, trio[k]), False, True, dep=[here(trio[k])])
+        v = scan(blk(T.ms, k), T.rs[:, :], ps, ALU.mult, ALU.max, dep=[v])
+        lists[k] = cp(blk(T.lm, 2 + k, 8), blk(T.ms, k)[:, 15:128:16], dep=[v])
     fill(T.s[:, 0:16], 0)
-    ts(T.n0[:, 2:3], m0, 16.0, qcol, ALU.mult, ALU.add)
-    v = ts(T.c0[:, 2:3], qcol, 8.0, None, ALU.is_ge)
-    ts(T.c0[:, 3:4], T.c0[:, 2:3], 8.0, gcol, ALU.mult, ALU.add, dep=[v, pz])
-    v = ts(T.tri0[:, :], T.kq[:, :], T.n0[:, 2:3], None, ALU.is_gt)
-    ts(T.c0[:, 4:5], T.c0[:, 3:4], qcol, None, ALU.is_equal, dep=[v])
-    v = ts(T.tri1[:, :], T.kq[:, :], T.n0[:, 2:3], None, ALU.is_lt)
-    ts(T.gl0[:, :], T.gl0[:, :], T.c0[:, 2:3], T.c0[:, 4:5], ALU.add, ALU.mult, dep=[v])
-    v = tt(T.lt[:, :], T.tri0[:, :], T.sg[:, :], ALU.mult)
+    v = ts(T.gl0[:, :], T.gl0[:, :], T.qgf[:, 3:4], T.n0[:, 3:4], ALU.add, ALU.mult)
+    tt(T.gt[:, :], T.tri1[:, :], T.sg[:, :], ALU.mult)
+    ts(T.gl[:, :], T.gl0[:, :], 8.0, None, ALU.add, dep=[v])
 
     def follow():
         v = cp(T.sr[:, 4:20], blk(T.big, 1).indirect(T.sr[:, 2:3]), dep=[vw] + [("w%d" % d, ne) for d in range(HEAD) if d != r])
         if r < HEAD:
             wait("p", *v)
-            send(T.sr[:, 0:8], T.sr[:, 0:8], "h", "lh", [d for d in (6, 7, 5, 4, 3) if bool(maps(d)) != bool(r)])
+            send(T.sr[:, 0:8], T.sr[:, 0:8], "h", "lh", [2, 5, 4] if r else [6, 7])
         return v
-    vh = follow() if r == 1 else None
-    tt(T.gt[:, :], T.tri1[:, :], T.sg[:, :], ALU.mult)
-    vs = ts(T.gl[:, :], T.gl0[:, :], 16.0, None, ALU.add, dep=[v])
-    if r in (0, HEAD):
+    vh = None
+    if maps(r) and r == trio[1]:
+        as_list(1)
+    told = [d for d in range(N) if (r, 1) in tellers(d)]
+    for u, d in enumerate(near):
+        for k in range(3):
+            vs = ts(blk(T.xn, 3 * (d % 3) + k), xtab(d, 1, r), 2.0 ** -19, k - 0.5 + 2.0 ** -20, ALU.mult, ALU.add,
+                    dep=[last["t1"] if d == r else ("x%d" % d, ne)])
+        if maps(r) and u < 2 and 1 - u not in lists:
+            as_list(1 - u)
+        if r == 1 and u == 0:
+            vh = follow()
+    if r in (0, 3):
         vh = follow()
-    for d in maps(r):
-        qn = "ya"[d % 2]
-        wait(qn, *pz)
-        wait(qn, "m%d" % d, ne)
-        eng[qn].dma_start(blk(T.big, d)[0:128:16, :], T.mdi[d]).then_inc(T.sem["ld%d" % d], 16)
-    for d in sorted(nb):
-        if d >= HEAD:
-            states(d)
-
-    def heads():
-        v = None
-        for d in range(max(near[0] - 1, 0), HEAD):
-            o, col, u = T.s[:, 2 * d + 2:2 * d + 3], T.sr[:, 2 * d + 2:2 * d + 3], d - near[0]
-            v = ts(o, col, T.n0[:, 4 + u:5 + u] if u >= 0 else 0.0, None, ALU.add, dep=head + [acol])
-        return v
-
-    head = [vh or ("h", ne)]
-    for d in range(HEAD, near[-1] + 1):
-        u = d - near[0]
-        win = blk(T.big, d) if u < 0 else blk(T.nw, u) if d == HEAD else T.nw[:, 0:128 * (u + 1)]
-        vs = cp(T.s[:, 2 * d + 2:2 * d + 18], win.indirect((T.sr if d == HEAD else T.s)[:, 2 * d:2 * d + 1]),
-                dep=[vs, max(aw[e] for e in aw if e != "x" and e <= d) if d in near else
-                     ("ld%d" % d, 16) if d in maps(r) else ("w%d" % d, ne)] + head)
-        if d == HEAD:
-            heads()
-    if near[-1] < HEAD:
-        heads()
+    if lists:
+        lists["u"] = act(T.wu[:, :], blk(T.big, trio[2]).indirect(blk(T.lm, 3, 8)), ACTF.Copy, dep=[vw, here(trio[2]), lists[1]])
     vs = ("v", cnt["v"])
-    a, n1, n3 = 2 * near[0], 32 * nc - 16, 16 * nc
-    v = tt(T.g2[:, 0:n1], T.xe[:, 0:128 * nc].indirect(T.s[:, a:a + 2 * nc - 1]), T.mk1[:, 0:n1], ALU.mult,
-           dep=[vs, aw["x"]] + [("e%d" % d, ne) for d in nb])
-    v = scan(T.sc1[:, 0:n1], T.rs[:, 0:n1], T.g2[:, 0:n1], ALU.mult, ALU.add, dep=[v])
-    ve = T.sc1[:, 15:n1:32]
+    for d in maps(r):
+        wait("y", *pz)
+        wait("y", "m%d" % d, ne)
+        Y.dma_start(blk(T.big, d)[0:128:16, :], T.mdi[d]).then_inc(T.sem["ld%d" % d], 16)
+    aw = {}
+    for k, d in enumerate(trio):
+        if k and lists:
+            aw[d] = act(blk(T.nw, k), (blk(T.big, d), T.wu[:, :])[k - 1].indirect(blk(T.lm, 2, 8)), ACTF.Identity, bias=lane0,
+                        dep=[here(d), lists[0], lists["u"]])
+        else:
+            aw[d] = act(blk(T.nw, k), blk(T.big, d), ACTF.Identity, bias=lane0, dep=[here(d)])
+
+    head = vh or ("h", ne)
+    for d in range(HEAD, near[0]):
+        vs = cp(T.s[:, 2 * d + 2:2 * d + 18], blk(T.big, d).indirect((T.sr if d == HEAD else T.s)[:, 2 * d:2 * d + 1]),
+                dep=[vs, head, ("ld%d" % d, 16) if d in maps(r) else here(d)])
+    col = []
+    for u in range(nc):
+        d, o = near[0] - 1 + u, blk(T.sb, u, 16)
+        if u == 0:
+            col.append(((T.sr if 0 <= d < HEAD else T.s)[:, 2 * d + 2:2 * d + 3], vs))
+        elif d < HEAD:
+            col.append((o[:, 0:1], ts(o[:, 0:1], T.sr[:, 2 * d + 2:2 * d + 3], lane0, None, ALU.add, dep=[head, acol])))
+        else:
+            k = trio.index(d)
+            if k and not lists:
+                src, dep = T.nw[:, 128 * k - 128:128 * k + 128].indirect(col[-1][0]), col[-1][1]
+            else:
+                src, dep = blk(T.nw, k).indirect((T.sr if trio[0] == HEAD else T.s)[:, 2 * trio[0]:2 * trio[0] + 1]), vs
+            col.append((o[:, 0:1], cp(o, src, dep=[dep, head, aw[d]])))
+    n3 = 16 * nc
+    for u, (lst, dep) in enumerate(col):
+        a = 128 * max(u - 1, 0)
+        v = tt(blk(T.g2, u, 16), T.xe[:, a:a + 256].indirect(lst), blk(T.mk3, u, 16), ALU.mult,
+               dep=[dep, head, ax] + [("e%d" % d, ne) for d in nb])
+    v = scan(T.sc1[:, 0:n3], T.rs[:, 0:n3], T.g2[:, 0:n3], ALU.mult, ALU.add, dep=[v])
+    ve = T.sc1[:, 15:n3:16]
     v = ts(T.ls2[:, 0:nc], ve, 1.0 / 4096, 1.0 / 8192 - 0.5, ALU.mult, ALU.add, dep=[v])
-    vi = cp(T.vi[:, 0:nc], ve)
-    v = tt(T.g3[:, 0:n3], T.xo[:, 0:384 * nu].indirect(T.ls2[:, 0:nc]), T.mk3[:, 0:n3], ALU.mult, dep=[v])
     for k in range(2):
         vc = tt(T.ca[:, 4 * k:4 * k + nc], ve, T.thr[:, 4 * k:4 * k + nc], ALU.is_ge)
-    vf = scan(T.sc3[:, 0:n3], T.rs[:, 0:n3], T.g3[:, 0:n3], ALU.mult, ALU.add, dep=[v])
-    v = scan(T.si3[:, 0:n3], T.rs[:, 0:n3], T.g3[:, 0:n3], ALU.mult, ALU.add)
+    for k in range(2):
+        ac = act(T.cab[:, k:2 * nc:2], T.ca[:, 4 * k:4 * k + nc], ACTF.Copy, scale=ONE, dep=[vc])
+    u0 = r - near[0]
 
-    def number(x, src, dep):
-        return ts(T.ei[:, x:m:4], src, 6 * (x % 2), 63, ALU.logical_shift_right, ALU.bitwise_and, dep=[dep])
-    for k in range(2):
-        act(T.cab[:, k:m:4], T.ca[:, 4 * k:4 * k + nc], ACTF.Copy, scale=ONE, dep=[vc])
-    ac = ("a", cnt["a"])
-    number(0, T.vi[:, 0:nc], vi)
-    for k in range(2):
-        vc = ts(T.cab[:, 2 + k:m:4], T.sc3[:, 15:n3:16], 4096.0 * 128 * (k + 1), ONE, ALU.is_ge, ALU.mult, dep=[vf])
-    for k in range(2):
-        number(2 + k, T.si3[:, 15:n3:16], v)
-    vee = scan(T.ee[:, 1:21], T.cab[:, :], T.cab[:, :], ALU.add, ALU.max, dep=[vc, ac])
-    v = number(1, T.vi[:, 0:nc], vi)
-    scan(T.eef[:, 1:m + 1], T.cab[:, 0:m], T.cab[:, 0:m], ALU.add, ALU.max)
-    vv = v = tt(T.val[:, 0:m], T.ei[:, 0:m], T.cab[:, 0:m], ALU.add, dep=[v])
-    u0 = 1 if r else 0
-    nx_ = 2 * (nc - u0)
-    ags = act(T.gs[:, 0:16 * nx_], T.val[:, :].indirect(T.gl[:, 0:nx_]), ACTF.Relu, bias=1.0 - ONE, dep=[v])
-    told = [d for d in range(N - 1, r, -1) if (r, nu - 1) in tellers(d)]
+    def counts():
+        return tt(T.gn[:, 0:n3], T.xn[:, 0:384 * nu].indirect(T.ls2[:, 0:nc]), T.mkn[:, 0:n3], ALU.mult, dep=[v])
+
+    def entry():
+        return tt(T.g3[:, 0:n3], T.xo[:, 0:384 * nu].indirect(T.ls2[:, 0:nc]), T.mk3[:, 0:n3], ALU.mult, dep=[v])
+
+    def running():
+        return scan(T.en[:, 16:n3 + 24], T.gn[:, 0:n3 + 8], T.gn[:, 0:n3 + 8], ALU.add, ALU.max, dep=[vn])
+
+    def number(eo, k, src):
+        return ts(T.ei[:, 8 * eo + k:8 * eo + 2 * nc:2], src, 6 * k, 63, ALU.logical_shift_right, ALU.bitwise_and)
+
+    def spread(eo, dep):
+        cs = slice(8 * eo, 8 * eo + 2 * nc)
+        v = tt(blk(T.val, eo, 16)[:, 0:2 * nc], T.ei[:, cs], T.cab[:, cs], ALU.add, dep=dep)
+        return act(blk(T.gs, eo, 64)[:, 0:16 * (nc - u0)], blk(T.val, eo, 16).indirect(T.gl[:, 0:nc - u0]), ACTF.Relu,
+                   bias=1.0 - ONE, dep=[v])
     if told:
-        wait("p", *vee)
-        send(T.ee[:, 16:24], blk(T.cin, r, 8), "c%d" % r, "lc", told)
-    if r == 0:
-        v = ts(T.c0[:, 0:1], T.ee[:, 4:5], m0, None, ALU.mult, dep=[vee])
-        v = ts(T.c0[:, 1:2], T.ee[:, 8:9], n0, T.c0[:, 0:1], ALU.mult, ALU.add, dep=[v])
-        wait("p", *ts(T.ee[:, 24:28], T.mg[:, 0:4], T.c0[:, 1:2], None, ALU.add, dep=[v]))
-        send(T.ee[:, 24:32], blk(T.cin, r, 8), "c0", "lc", [d for d in range(N - 1, r, -1) if (0, 0) in tellers(d)])
+        vn = counts()
+        if r < HEAD:
+            v0 = tt(T.g0[:, 0:16 * nu], T.xn[:, 0:384 * nu].indirect(T.ls2[:, 0:nu]), T.mk0[:, 0:16 * nu], ALU.mult)
+        vg = entry()
+        vn = running()
+        wait("p", *vn)
+        send(T.en[:, n3 + 16:n3 + 24], blk(T.cin, r, 8), "c%d" % r, "lc", told)
+        if r < HEAD:
+            wait("p", *scan(T.e0[:, :], T.g0[:, :], T.g0[:, :], ALU.add, ALU.max, dep=[v0]))
+            send(T.e0[:, 48:56], blk(T.cin, r, 8), "c%d" % r, "lc", [d for d in range(N - 1, r, -1) if (r, 0) in tellers(d)])
+    else:
+        vg, vn = entry(), counts()
+    vg = scan(T.sc3[:, 0:n3], T.rs[:, 0:n3], T.g3[:, 0:n3], ALU.mult, ALU.add, dep=[vg])
+    vo = T.sc3[:, 15:n3:16]
+    number(0, 0, ve)
+    if not told:
+        vn = running()
+    ve1 = number(0, 1, ve)
+    for k in range(2):
+        ts(T.cab[:, 8 + k:8 + 2 * nc:2], vo, 4096.0 * 128 * (k + 1), ONE, ALU.is_ge, ALU.mult, dep=[vg])
+    for k in range(2):
+        vo1 = number(1, k, vo)
+    ags = [spread(0, [ve1, ac])]
+    vc = tt(T.ce[:, 0:nc], T.cab[:, 0:2 * nc:2], T.cab[:, 1:2 * nc:2], ALU.add)
+    ags.append(spread(1, [vo1]))
     sums = [(T.sg, blk(T.cin, s, 8)[:, 0:nc], ("c%d" % s, ne)) for s, c in reversed(tellers(r))]
     k = len(sums) - (r > 2 * HEAD)
-    sums[k:k] = [(T.gt, T.ee[:, 0:m:4], vee), (T.lt, T.ee[:, 4:m + 1:4], vee)]
+    sums[k:k] = [(T.gt, T.en[:, 15:n3:16], vn), (T.lt, T.en[:, 31:n3 + 16:16], vn)]
     for k, (lh, rh, dep) in enumerate(sums):
         tp = mm(T.pq[:, 0:nc], lh[:, :], rh, k == 0, k == len(sums) - 1, dep=[dep])
 
     yp = T.py[0:8, 0:32]
-    for x in range(nx_):
-        e = 2 * (x + 2 * u0)
-        vo = ts(T.oh[:, 64 * x:64 * x + 33], T.iot[:, 0:33], T.eef[:, e:e + 1], T.pq[:, e // 4:e // 4 + 1],
-                ALU.subtract, ALU.is_equal, dep=[tp, vv])
-        for k in range(2):
-            ty = mm(yp, blk(T.gs, 2 * x + k, 8), T.oh[:, 64 * x + 1 - k:64 * x + 33 - k], x + k == 0, x + k == nx_, dep=[vo, ags])
+    for eo in range(2):
+        for u in range(u0, nc):
+            oh, at = blk(T.oh, 4 * eo + u, 64), T.pq[:, u:u + 1]
+            if eo:
+                v = ts(oh[:, 0:33], T.iot[:, 0:33], T.ce[:, u:u + 1], at, ALU.subtract, ALU.is_equal, dep=[vc])
+            else:
+                v = ts(oh[:, 0:33], T.iot[:, 0:33], at, None, ALU.is_equal, dep=[tp])
+            for k in range(2):
+                ty = mm(yp, blk(T.gs, 8 * eo + 2 * (u - u0) + k, 8), oh[:, 1 - k:33 - k], (eo, u, k) == (0, u0, 0), (eo, u, k) == (1, nu, 1),
+                        dep=[v, ags[eo]])
     wait("y", *ts(T.ys[0:8, :], yp, -1.0, None, ALU.add, dep=[ty]))
     Y.dma_start(T.y[:, :], T.ys[0:8, :]).then_inc(T.sem.yo, 16)
 
@@ -441,7 +490,7 @@ def rank_program(g, core, T, topo):
     if r < HEAD:
         wait("p", "lh", ne)
     if told:
-        wait("p", "lc", ne if r else 2 * ne)
+        wait("p", "lc", 2 * ne if r < HEAD else ne)
     if far:
         wait("p", "lm", ne)
     for name in ("v", "a", "t"):

@@ -6,28 +6,28 @@ ACTF = ActivationFunctionType
 F, B, H, I4, U2 = "float32", "bfloat16", "float16", "int32", "uint16"
 SBUF = {
     I4: "nxi:512 emi:512 ipi:8 qgi:8 sc1:64 sc3:64 ei:16 xn:1152",
-    B: "ones:128 nil:128 iob:128 jj:2048 wa0:128 wa1:128 wb0:128 wb1:128 wc0:128 wc1:128 wu:128 big:1024 rep:384 sg:128 eye:128 low:128 "
-       "gt:128 lt:128 en:88 e0:56 cin:32 gs:128 oh:512",
+    B: "ones:128 nil:128 half:128 iob:128 jj:2048 wa0:128 wa1:128 wb0:128 wb1:128 wc0:128 wc1:128 wu:128 big:1024 rep:384 sg:128 eye:128 low:128 "
+       "gt:128 lt:128 en:88 e0:40 cin:32 gs:128 oh:512",
     H: "emh:512 sela:128",
     F: "qgf:8 hm:8 mq:128 kq:128 mg:128 rm:16 n0:8 iot:40 tri0:128 tri1:128 nw:384 xe:512 xo:1152 "
-       "rs:128 ms:256 mk3:64 thr:8 val:32 g2:64 g3:64 ca:8 cab:16 gn:72 mkn:64 g0:56 mk0:48 ce:8 gl0:8 f0:48 "
+       "rs:128 ms:256 mk3:64 thr:8 val:32 g2:64 g3:64 ca:8 cab:16 gn:72 mkn:64 g0:40 mk0:32 ce:8 gl0:8 f0:48 "
        "ys:32",
-    U2: "s:48 sr:24 s0:112 sb:64 lm:32 ls2:8 gl:8",
+    U2: "s:48 sr:24 s0:112 sb:64 ml:40 lz:8 lm:32 ls2:8 gl:8",
 }
 SCRATCH = {w.split(":")[0]: ("sbuf", [128, int(w.split(":")[1])], d) for d, ws in SBUF.items() for w in ws.split()}
 SCRATCH.update({
-    "syi": ("sbuf", [128, 8, 32], I4), "syr": ("sbuf", [128, 16, 16], B),
+    "syi": ("sbuf", [128, 4, 32], I4), "syr": ("sbuf", [128, 8, 16], B),
     "selm": ("sbuf", [128, 8, 32], H), "tb": ("sbuf", [128, 32, 32], H),
     "oi": ("sbuf", [128, 4, 64], I4), "oi2": ("sbuf", [128, 4, 64], I4), "off": ("sbuf", [128, 4, 64], U2),
-    "mdo": ("dram", [128, 8], B), "mdi": ("dram", [8, 128, 8], B),
     "pl": ("psum", [128, 8, 64], F),
 })
 SCRATCH.update({n: ("psum", [128, 512], F) for n in "pb pe po pq pt py".split()})
-SEMAPHORES = ("v a t p ds mo yo xh h lh lx lw lm lc".split() + [s + str(t) for s in ("dn", "de") for t in range(4)]
-              + [s + str(r) for s in ("x", "e", "w", "m", "c", "ld") for r in range(8)])
+SEMAPHORES = ("v a t p ds yo xh h lh lx lw lm lc".split() + [s + str(t) for s in ("dn", "de") for t in range(4)]
+              + [s + str(r) for s in ("x", "e", "w", "m", "c") for r in range(8)])
 CUTS = (0, 10, 20, 32)
 TURNS = (1, 2, 0)
 HEAD = 2
+FIRST = (0, 3, 1, 2, 6, 7, 5, 4)
 ONE = 64.0
 
 
@@ -36,11 +36,11 @@ def near_of(r):
 
 
 def users(d):
-    return [r for r in (0, 3, 1, 2, 6, 7, 5, 4) if r != d and d in near_of(r)]
+    return [r for r in FIRST if r != d and d in near_of(r)]
 
 
 def tellers(r):
-    return {2: [(0, 0)], 3: [(1, 0)], 4: [(1, 1)], 5: [(2, 1), (0, 0)], 6: [(3, 1), (0, 1)], 7: [(3, 1), (0, 1)]}.get(r, [])
+    return {2: [(0, 0)], 3: [(0, 1)], 4: [(1, 1)], 5: [(2, 1), (0, 0)], 6: [(3, 1), (0, 1)], 7: [(3, 1), (0, 1)]}.get(r, [])
 
 
 def maps(r):
@@ -128,7 +128,7 @@ def rank_program(g, core, T, topo):
         return do("a", lambda: A.activation(out, in_, func, **kw), *dep)
 
     for h in range(2):
-        (Y, A)[h].dma_start(T.syi[0:1, 4 * h:4 * h + 4, :], T.sy[h::2, :]).then_inc(T.sem.ds, 16)
+        (Y, A)[h].dma_start(T.syi[h:h + 1, :, :], T.sy[h::2, :]).then_inc(T.sem.ds, 16)
     for t in range(4):
         (Y, A)[t % 2].dma_start(blk(T.nxi, t), T.nx[2 * t:2 * t + 2, :]).then_inc(T.sem["dn%d" % t], 16)
     wait("y", "dn0", 16)
@@ -151,8 +151,6 @@ def rank_program(g, core, T, topo):
     iota(T.iot[:, 0:33], [[int(ONE), 33]], int(ONE) * (32 * r - 1), 0)
     iota(T.gl0[:, :], [[2, 8]], 2 * (r - near[0]) - 8, 0)
     pz = iota(blk(T.xe, nu), [[0, 128]], 0, 0)
-    if maps(r):
-        pz = iota(T.big[:, 128 * HEAD:128 * near[0]], [[0, 128 * len(maps(r))]], 0, 0)
 
     fill(T.nil[0:1, :], 0.0)
     von = fill(T.ones[0:1, :], 1.0)
@@ -167,28 +165,22 @@ def rank_program(g, core, T, topo):
     vqg = cp(T.qgf[:, 0:5], T.qgi[:, 0:5], dep=[v])
     vrm = ts(T.rm[:, :], T.rm[:, :], qcol, None, ALU.is_equal, dep=[vqg, pq])
     ts(T.n0[:, 3:4], T.qgf[:, 4:5], gcol, None, ALU.is_equal)
+    ts(T.half[0:2, :], T.iob[0:2, :], 64.0, qcol[0:2, :], ALU.is_ge, ALU.is_equal, dep=[pib])
     px = (T.pe[:, 0:128], T.po[:, 0:128])
     for o in px:
         mm(o, T.ones[0:1, :], T.nil[0:1, :], True, False, dep=[von])
     jd = {}
     for j in range(12):
         jd[j] = act(blk(T.jj, j), T.iob[:, :], ACTF.Copy, scale=T.rm[:, j:j + 1], dep=[vrm, pib])
-    for j in range(12, 16):
-        jd[j] = ts(blk(T.jj, j), T.iob[:, :], T.rm[:, j:j + 1], None, ALU.mult, dep=[vrm, pib])
     n0, lane0 = T.n0[:, 1:2], T.n0[:, 4:5]
     act(T.n0[:, 2:3], m0, ACTF.Identity, scale=16.0, bias=qcol)
     act(lane0, m0, ACTF.Copy, scale=128.0)
-    act(n0, m0, ACTF.Identity, scale=-1.0, bias=1.0)
-    for u in range(nc):
-        d = near[0] - 1 + u
-        for k in range(2):
-            a, b = (4096.0 * (xoff(e) + 128 * (k + 1)) for e in (d, d + 1))
-            acol = act(T.thr[:, 4 * k + u:4 * k + u + 1], m0, ACTF.Identity, scale=b - a, bias=a)
+    acol = act(n0, m0, ACTF.Identity, scale=-1.0, bias=1.0)
     for eo in range(2):
-        vrow = cp(T.syr[0:1, eo:16:2, :], T.syi[0:1, :, eo:32:2], dep=[("ds", 32)])
-    for h in range(2):
-        tbc = mm(T.pb[64 * h:64 * h + 64, 0:128], T.ones[0:1, 0:64], T.syr[0:1, 8 * h:8 * h + 8, :], True, True, dep=[vrow])
-    vlow = ts(T.low[:, :], T.mq[:, :], qcol, -256.0, ALU.not_equal, ALU.mult, dep=[pmq])
+        vrow = cp(T.syr[0:2, eo:8:2, :], T.syi[0:2, :, eo:32:2], dep=[("ds", 32)])
+    tbc = mm(T.pb[:, 0:128], T.half[0:2, :], T.syr[0:2, :, :], True, True, dep=[vrow])
+    for j in range(12, 16):
+        jd[j] = ts(blk(T.jj, j), T.iob[:, :], T.rm[:, j:j + 1], None, ALU.mult, dep=[vrm, pib])
     vt = []
     last = {}
     for t in range(4):
@@ -201,6 +193,7 @@ def rank_program(g, core, T, topo):
     for h in range(2):
         vsm = ts(T.selm[:, :, 16 * h:16 * h + 16], T.sela[:, :], T.hm[:, h:h + 1], None, ALU.mult, dep=[vsa])
     vsg = ts(T.sg[:, :], T.mg[:, :], gcol, None, ALU.is_equal, dep=[pmg])
+    vlow = ts(T.low[:, :], T.mq[:, :], qcol, -256.0, ALU.not_equal, ALU.mult)
     for ch in range(3):
         j = CUTS[ch + 1] // 2 % 16
         arep = act(blk(T.rep, ch), T.sg[:, :], ACTF.Copy, scale=T.rm[:, j:j + 1], dep=[vsg])
@@ -313,24 +306,17 @@ def rank_program(g, core, T, topo):
     send(xtab(r, 1, r), xtab(r, 1, r), "x%d" % r, "lx", users(r))
     wait("p", *last["t0"])
     g.remote_dma_fused([transfer(xtab(r, 0, r), [xtab(r, 0, r)], "xh", [helper(r)], inside(r))], local_sem=T.sem.lx)
-    far = [d for d in range(N - 1, r + 1, -1) if r in maps(d)]
+    far = [d for d in FIRST if r in maps(d)]
     wait("p", *vw)
     late = [r + 2] if r == HEAD else []
     if r:
-        send(blk(T.big, r), blk(T.big, r), "w%d" % r, "lw", users(r) if r > 1 else [0, 3])
+        send(blk(T.big, r), blk(T.big, r), "w%d" % r, "lw", users(r) if r > 1 else [0, 3, 2])
     else:
-        send(T.s0[:, 0:8], T.sr[:, 0:8], "w0", "lw", [1, 3])
-    if far:
-        wait("y", *vw)
-        Y.dma_start(T.mdo[:, :], blk(T.big, r)[0:128:16, :]).then_inc(T.sem.mo, 16)
-        wait("p", "mo", 16)
-        send(T.mdo[:, :], T.mdi[r], "m%d" % r, "lm", far)
-    if late:
-        send(blk(T.big, r), blk(T.big, r), "w%d" % r, "lw", late)
+        send(T.s0[:, 0:8], T.sr[:, 0:8], "w0", "lw", [1, 3, 2])
     for u in range(nc):
         v = act(blk(T.mk3, u, 16), T.rm[:, :], ACTF.Copy, scale=1.0 if 0 < u < nu else n0 if u else m0)
     v = act(T.mkn[:, 0:16 * nc], T.mk3[:, 0:16 * nc], ACTF.Copy, scale=ONE, dep=[v])
-    if r < HEAD:
+    if r == 0:
         for u in range(nu):
             act(blk(T.mk0, u, 16), blk(T.mkn, u if u < nu - 1 else nu, 16), ACTF.Copy, dep=[v])
     for d in [r] + nb:
@@ -343,10 +329,10 @@ def rank_program(g, core, T, topo):
     def here(d):
         return vw if d == r else ("w%d" % d, ne)
 
-    def as_list(k):
+    def as_list(k, d):
         ps = (T.pt, T.pb)[k][:, 0:128]
         mm(ps, T.eye[:, :], T.low[:, :], True, False, dep=[vw])
-        v = mm(ps, blk(T.rep, 2), blk(T.big, trio[k]), False, True, dep=[here(trio[k])])
+        v = mm(ps, blk(T.rep, 2), blk(T.big, d), False, True, dep=[here(d)])
         v = scan(blk(T.ms, k), T.rs[:, :], ps, ALU.mult, ALU.max, dep=[v])
         lists[k] = cp(blk(T.lm, 2 + k, 8), blk(T.ms, k)[:, 15:128:16], dep=[v])
     fill(T.s[:, 0:16], 0)
@@ -358,41 +344,60 @@ def rank_program(g, core, T, topo):
         v = cp(T.sr[:, 4:20], blk(T.big, 1).indirect(T.sr[:, 2:3]), dep=[vw] + [("w%d" % d, ne) for d in range(HEAD) if d != r])
         if r < HEAD:
             wait("p", *v)
-            send(T.sr[:, 0:8], T.sr[:, 0:8], "h", "lh", [2, 5, 4] if r else [6, 7])
+            send(T.sr[:, 0:8], T.sr[:, 0:8], "h", "lh", [6, 7, 5] if r else [4])
         return v
     vh = None
-    if maps(r) and r == trio[1]:
-        as_list(1)
-    told = [d for d in range(N) if (r, 1) in tellers(d)]
+    if HEAD <= r < N - 1:
+        as_list(1, r)
+    if far:
+        wait("p", *lists[1])
+        send(blk(T.lm, 3, 8), blk(T.ml, r, 8), "m%d" % r, "lm", far)
+    if late:
+        send(blk(T.big, r), blk(T.big, r), "w%d" % r, "lw", late)
+    told = [d for d in (6, 7, 5, 4, 3) if (r, 1) in tellers(d)]
     for u, d in enumerate(near):
         for k in range(3):
             vs = ts(blk(T.xn, 3 * (d % 3) + k), xtab(d, 1, r), 2.0 ** -19, k - 0.5 + 2.0 ** -20, ALU.mult, ALU.add,
                     dep=[last["t1"] if d == r else ("x%d" % d, ne)])
-        if maps(r) and u < 2 and 1 - u not in lists:
-            as_list(1 - u)
+        if r > 3 and u and 2 - u not in lists:
+            as_list(2 - u, trio[2 - u])
+        if r == 0 and u == 0:
+            for k, lst in enumerate((T.s[:, 0:1], T.sr[:, 2:3])):
+                v = tt(blk(T.g2, k, 16), T.xe[:, 0:128].indirect(lst), blk(T.mk3, 2 * k, 16), ALU.mult, dep=[vs, ax, last["t0"]])
+            v = scan(T.sc1[:, 0:32], T.rs[:, 0:32], T.g2[:, 0:32], ALU.mult, ALU.add, dep=[v])
+            v = ts(T.lz[:, 0:2], T.sc1[:, 15:32:16], 1.0 / 4096, 1.0 / 8192 - 0.5, ALU.mult, ALU.add, dep=[v])
+            v = tt(T.g0[:, 0:32], T.xn[:, 0:384].indirect(T.lz[:, 0:2]), T.mk0[:, :], ALU.mult, dep=[v])
+            vh = follow()
+            wait("p", *scan(T.e0[:, :], T.g0[:, :], T.g0[:, :], ALU.add, ALU.max, dep=[v]))
+            send(T.e0[:, 32:40], blk(T.cin, 0, 8), "c0", "lc", [d for d in range(N - 1, 0, -1) if (0, 0) in tellers(d)])
         if r == 1 and u == 0:
             vh = follow()
-    if r in (0, 3):
+    if r in (2, 3):
         vh = follow()
-    if lists:
+    if r > 3:
         lists["u"] = act(T.wu[:, :], blk(T.big, trio[2]).indirect(blk(T.lm, 3, 8)), ACTF.Copy, dep=[vw, here(trio[2]), lists[1]])
     vs = ("v", cnt["v"])
-    for d in maps(r):
-        wait("y", *pz)
-        wait("y", "m%d" % d, ne)
-        Y.dma_start(blk(T.big, d)[0:128:16, :], T.mdi[d]).then_inc(T.sem["ld%d" % d], 16)
     aw = {}
+    for d in maps(r):
+        aw[d] = act(blk(T.big, d), T.iob[:, :].indirect(blk(T.ml, d, 8)), ACTF.Copy, dep=[("m%d" % d, ne)])
     for k, d in enumerate(trio):
-        if k and lists:
+        if k and r > 3:
             aw[d] = act(blk(T.nw, k), (blk(T.big, d), T.wu[:, :])[k - 1].indirect(blk(T.lm, 2, 8)), ACTF.Identity, bias=lane0,
                         dep=[here(d), lists[0], lists["u"]])
+        elif k and d > r:
+            aw[d] = act(blk(T.nw, k), blk(T.big, d).indirect(blk(T.lm, 3, 8)), ACTF.Identity, bias=lane0, dep=[here(d), lists[1]])
         else:
             aw[d] = act(blk(T.nw, k), blk(T.big, d), ACTF.Identity, bias=lane0, dep=[here(d)])
+    for u in range(nc):
+        d = near[0] - 1 + u
+        for k in range(2):
+            a, b = (4096.0 * (xoff(e) + 128 * (k + 1)) for e in (d, d + 1))
+            athr = act(T.thr[:, 4 * k + u:4 * k + u + 1], m0, ACTF.Identity, scale=b - a, bias=a)
 
     head = vh or ("h", ne)
     for d in range(HEAD, near[0]):
         vs = cp(T.s[:, 2 * d + 2:2 * d + 18], blk(T.big, d).indirect((T.sr if d == HEAD else T.s)[:, 2 * d:2 * d + 1]),
-                dep=[vs, head, ("ld%d" % d, 16) if d in maps(r) else here(d)])
+                dep=[vs, head, aw[d] if d in maps(r) else here(d)])
     col = []
     for u in range(nc):
         d, o = near[0] - 1 + u, blk(T.sb, u, 16)
@@ -402,8 +407,8 @@ def rank_program(g, core, T, topo):
             col.append((o[:, 0:1], ts(o[:, 0:1], T.sr[:, 2 * d + 2:2 * d + 3], lane0, None, ALU.add, dep=[head, acol])))
         else:
             k = trio.index(d)
-            if k and not lists:
-                src, dep = T.nw[:, 128 * k - 128:128 * k + 128].indirect(col[-1][0]), col[-1][1]
+            if k and r == 3:
+                src, dep = T.nw[:, 128 * k - 128:128 * k + 128].indirect(col[1][0]), col[1][1]
             else:
                 src, dep = blk(T.nw, k).indirect((T.sr if trio[0] == HEAD else T.s)[:, 2 * trio[0]:2 * trio[0] + 1]), vs
             col.append((o[:, 0:1], cp(o, src, dep=[dep, head, aw[d]])))
@@ -416,7 +421,7 @@ def rank_program(g, core, T, topo):
     ve = T.sc1[:, 15:n3:16]
     v = ts(T.ls2[:, 0:nc], ve, 1.0 / 4096, 1.0 / 8192 - 0.5, ALU.mult, ALU.add, dep=[v])
     for k in range(2):
-        vc = tt(T.ca[:, 4 * k:4 * k + nc], ve, T.thr[:, 4 * k:4 * k + nc], ALU.is_ge)
+        vc = tt(T.ca[:, 4 * k:4 * k + nc], ve, T.thr[:, 4 * k:4 * k + nc], ALU.is_ge, dep=[athr])
     for k in range(2):
         ac = act(T.cab[:, k:2 * nc:2], T.ca[:, 4 * k:4 * k + nc], ACTF.Copy, scale=ONE, dep=[vc])
     u0 = r - near[0]
@@ -440,15 +445,10 @@ def rank_program(g, core, T, topo):
                    bias=1.0 - ONE, dep=[v])
     if told:
         vn = counts()
-        if r < HEAD:
-            v0 = tt(T.g0[:, 0:16 * nu], T.xn[:, 0:384 * nu].indirect(T.ls2[:, 0:nu]), T.mk0[:, 0:16 * nu], ALU.mult)
         vg = entry()
         vn = running()
         wait("p", *vn)
         send(T.en[:, n3 + 16:n3 + 24], blk(T.cin, r, 8), "c%d" % r, "lc", told)
-        if r < HEAD:
-            wait("p", *scan(T.e0[:, :], T.g0[:, :], T.g0[:, :], ALU.add, ALU.max, dep=[v0]))
-            send(T.e0[:, 48:56], blk(T.cin, r, 8), "c%d" % r, "lc", [d for d in range(N - 1, r, -1) if (r, 0) in tellers(d)])
     else:
         vg, vn = entry(), counts()
     vg = scan(T.sc3[:, 0:n3], T.rs[:, 0:n3], T.g3[:, 0:n3], ALU.mult, ALU.add, dep=[vg])
@@ -490,7 +490,7 @@ def rank_program(g, core, T, topo):
     if r < HEAD:
         wait("p", "lh", ne)
     if told:
-        wait("p", "lc", 2 * ne if r < HEAD else ne)
+        wait("p", "lc", ne if r else 2 * ne)
     if far:
         wait("p", "lm", ne)
     for name in ("v", "a", "t"):

from concourse.bass import DstId, RemoteDMATransfer
from concourse.mybir import AluOpType, ActivationFunctionType

ALU = AluOpType
ACTF = ActivationFunctionType
F, B, H, I4, U2 = "float32", "bfloat16", "float16", "int32", "uint16"
SBUF = {
    I4: "nxi:512 emi:512 ipi:8 qgi:8 sc1:64 sc3:64 ei:16 xn:1152",
    B: "ones:128 nil:128 half:128 iob:128 jj:2048 wa0:128 wa1:128 wb0:128 wb1:128 wc0:128 wc1:128 wu:128 big:1024 rep:384 sg:128 eye:128 low:128 "
       "gt:128 lt:128 en:88 e0:40 cin:32 gs:128 oh:512",
    H: "emh:512 sela:128",
    F: "qgf:8 hm:8 mq:128 kq:128 mg:128 rm:16 n0:8 iot:40 tri0:128 tri1:128 nw:384 xe:512 xo:1152 "
       "rs:128 ms:256 mk3:64 thr:8 val:32 g2:64 g3:64 ca:8 cab:16 gn:72 mkn:64 g0:40 mk0:32 ce:8 gl0:8 f0:48 "
       "ys:32",
    U2: "s:48 sr:24 s0:112 sb:64 ml:40 lz:8 lm:32 ls2:8 gl:8",
}
SCRATCH = {w.split(":")[0]: ("sbuf", [128, int(w.split(":")[1])], d) for d, ws in SBUF.items() for w in ws.split()}
SCRATCH.update({
    "syi": ("sbuf", [128, 4, 32], I4), "syr": ("sbuf", [128, 8, 16], B),
    "selm": ("sbuf", [128, 8, 32], H), "tb": ("sbuf", [128, 32, 32], H),
    "oi": ("sbuf", [128, 4, 64], I4), "oi2": ("sbuf", [128, 4, 64], I4), "off": ("sbuf", [128, 4, 64], U2),
    "pl": ("psum", [128, 8, 64], F),
})
SCRATCH.update({n: ("psum", [128, 512], F) for n in "pb pe po pq pt py".split()})
SEMAPHORES = ("v a t p ds yo xh h lh lx lw lm lc".split() + [s + str(t) for s in ("dn", "de") for t in range(4)]
              + [s + str(r) for s in ("x", "e", "w", "m", "c") for r in range(8)])
CUTS = (0, 10, 20, 32)
TURNS = (1, 2, 0)
HEAD = 2
FIRST = (0, 3, 1, 2, 6, 7, 5, 4)
ONE = 64.0


def near_of(r):
    return list(range(max(min(r, 6) - 1, 0), min(r + 2, 8)))


def users(d):
    return [r for r in FIRST if r != d and d in near_of(r)]


def tellers(r):
    return {2: [(0, 0)], 3: [(0, 1)], 4: [(1, 1)], 5: [(2, 1), (0, 0)], 6: [(3, 1), (0, 1)], 7: [(3, 1), (0, 1)]}.get(r, [])


def maps(r):
    return list(range(HEAD, near_of(r)[0])) if r > HEAD + 2 else []


def rank_program(g, core, T, topo):
    cores = T.cores
    N = len(cores)

    def transfer(src, dsts, sem, to, engines):
        ids = []
        for c in to:
            rid, pid = topo.addr(c, core)
            ids.append(DstId(rid=rid, pnc=pid))
        return RemoteDMATransfer(dst_ids=ids, dma_engine_mask=sum(1 << e for e in engines), remote_sem=T.sem[sem],
                                 srcs=[src], dsts=dsts)

    def helper(d):
        return [c for c in topo.cores_of(cores[d]) if topo.die(c) != topo.die(cores[d])][0]

    def inside(d):
        return [e for e in topo.engines(cores[d], helper(d)) if e not in topo.engines(cores[d], cores[(d + 1) % N])]

    def blk(buf, d, n=128):
        return buf[:, n * d:n * d + n]

    def xoff(d):
        return 384 * (d % 3)

    def xtab(d, eo, at, k=0):
        return blk(T.xo, 3 * (d % 3) + k) if eo else blk(T.xe, d - near_of(at)[0])
    r = T.rank_of(core)
    if r is None:
        for d in range(N):
            if core == helper(d):
                to = users(d)
                out = topo.engines(core, cores[to[0]])
                g.wait_ge(T.sem.xh, len(inside(d)))
                g.remote_dma_fused([transfer(xtab(d, 0, d), [xtab(d, 0, e) for e in to], "e%d" % d, [cores[e] for e in to], out)],
                                   local_sem=T.sem.lx)
                g.wait_ge(T.sem.lx, len(out))
        return
    V, A, P, Y = g.vector, g.scalar, g.tensor, g.sync
    eng = {"v": V, "a": A, "t": P, "p": g, "y": Y}
    cnt = {"v": 0, "a": 0, "t": 0, "p": 0}
    seen = {}
    near = near_of(r)
    nb = [d for d in near if d != r]
    nu = len(near)
    nc = nu + 1
    m = 4 * nc

    def wait(q, name, val):
        if val > seen.get((q, name), 0):
            seen[(q, name)] = val
            eng[q].wait_ge(T.sem[name], val)

    def do(q, fn, *deps):
        for name, val in deps:
            wait(q, name, val)
        fn().then_inc(T.sem[q], 1)
        cnt[q] += 1
        return (q, cnt[q])

    def ts(out, in0, s1, s2, op0, *op1, dep=()):
        return do("v", lambda: V.tensor_scalar(out, in0, s1, s2, op0, *op1), *dep)

    def tt(out, in0, in1, op, dep=()):
        return do("v", lambda: V.tensor_tensor(out, in0, in1, op), *dep)

    def cp(out, in_, dep=()):
        return do("v", lambda: V.tensor_copy(out, in_), *dep)

    def fill(out, x, dep=()):
        return do("v", lambda: V.memset(out, x), *dep)

    def scan(out, d0, d1, op0, op1, dep=()):
        return do("v", lambda: V.tensor_tensor_scan(out, d0, d1, 0.0, op0, op1), *dep)

    def mm(out, lh, rh, start, stop, dep=()):
        return do("t", lambda: P.matmul(out, lh, rh, start, stop), *dep)

    def act(out, in_, func, dep=(), **kw):
        return do("a", lambda: A.activation(out, in_, func, **kw), *dep)

    for h in range(2):
        (Y, A)[h].dma_start(T.syi[h:h + 1, :, :], T.sy[h::2, :]).then_inc(T.sem.ds, 16)
    for t in range(4):
        (Y, A)[t % 2].dma_start(blk(T.nxi, t), T.nx[2 * t:2 * t + 2, :]).then_inc(T.sem["dn%d" % t], 16)
    wait("y", "dn0", 16)
    for t in range(4):
        Y.dma_start(blk(T.emi, t), T.em[2 * t:2 * t + 2, :]).then_inc(T.sem["de%d" % t], 16)

    def iota(ap, pattern, base, cm):
        return do("p", lambda: g.iota(ap, pattern, base, cm, allow_small_or_imprecise_dtypes=True))
    pi = iota(T.ipi[:, 0:1], [[0, 1]], 0, 1)
    pq = iota(T.rm[:, 0:16], [[1, 16]], 0, 0)
    pib = iota(T.iob[:, :], [[1, 128]], 0, 0)
    pmq = iota(T.mq[:, :], [[0, 8], [1, 16]], 0, 0)
    pmg = iota(T.mg[:, :], [[1, 8], [0, 16]], 0, 0)
    do("p", lambda: g.affine_select(T.kq[:, :], T.mq[:, :], [[0, 8], [1, 16]], ALU.is_gt, 16.0, 0, 0), pmq)
    p1 = iota(T.tri0[:, :], [[0, 128]], 1, 0)
    do("p", lambda: g.affine_select(T.eye[:, :], T.tri0[:, :], [[-1, 128]], ALU.is_equal, 0.0, 0, 1), p1)
    do("p", lambda: g.affine_select(T.rs[:, :], T.tri0[:, :], [[0, 8], [1, 16]], ALU.is_gt, 0.0, 0, 0))
    for o in (T.en[:, 0:16], T.val[:, :], T.gn[:, :], T.g0[:, :]):
        iota(o, [[0, o.shape[1]]], 0, 0)
    iota(T.iot[:, 0:33], [[int(ONE), 33]], int(ONE) * (32 * r - 1), 0)
    iota(T.gl0[:, :], [[2, 8]], 2 * (r - near[0]) - 8, 0)
    pz = iota(blk(T.xe, nu), [[0, 128]], 0, 0)

    fill(T.nil[0:1, :], 0.0)
    von = fill(T.ones[0:1, :], 1.0)
    ts(T.qgi[:, 0:1], T.ipi[:, 0:1], 15, None, ALU.bitwise_and, dep=[pi])
    ts(T.qgi[:, 2:3], T.ipi[:, 0:1], 63, None, ALU.bitwise_and)
    ts(T.qgi[:, 3:4], T.ipi[:, 0:1], 3, 1, ALU.logical_shift_right, ALU.bitwise_and)
    ts(T.qgi[:, 4:5], T.ipi[:, 0:1], 7, None, ALU.bitwise_and)
    v = ts(T.qgi[:, 1:2], T.ipi[:, 0:1], 4, None, ALU.logical_shift_right)
    qcol, gcol, m0 = T.qgf[:, 0:1], T.qgf[:, 1:2], T.rm[:, 0:1]
    ts(T.hm[:, 0:1], T.ipi[:, 0:1], 64.0, None, ALU.is_lt)
    ts(T.hm[:, 1:2], T.ipi[:, 0:1], 64.0, None, ALU.is_ge)
    vqg = cp(T.qgf[:, 0:5], T.qgi[:, 0:5], dep=[v])
    vrm = ts(T.rm[:, :], T.rm[:, :], qcol, None, ALU.is_equal, dep=[vqg, pq])
    ts(T.n0[:, 3:4], T.qgf[:, 4:5], gcol, None, ALU.is_equal)
    ts(T.half[0:2, :], T.iob[0:2, :], 64.0, qcol[0:2, :], ALU.is_ge, ALU.is_equal, dep=[pib])
    px = (T.pe[:, 0:128], T.po[:, 0:128])
    for o in px:
        mm(o, T.ones[0:1, :], T.nil[0:1, :], True, False, dep=[von])
    jd = {}
    for j in range(12):
        jd[j] = act(blk(T.jj, j), T.iob[:, :], ACTF.Copy, scale=T.rm[:, j:j + 1], dep=[vrm, pib])
    n0, lane0 = T.n0[:, 1:2], T.n0[:, 4:5]
    act(T.n0[:, 2:3], m0, ACTF.Identity, scale=16.0, bias=qcol)
    act(lane0, m0, ACTF.Copy, scale=128.0)
    acol = act(n0, m0, ACTF.Identity, scale=-1.0, bias=1.0)
    for eo in range(2):
        vrow = cp(T.syr[0:2, eo:8:2, :], T.syi[0:2, :, eo:32:2], dep=[("ds", 32)])
    tbc = mm(T.pb[:, 0:128], T.half[0:2, :], T.syr[0:2, :, :], True, True, dep=[vrow])
    for j in range(12, 16):
        jd[j] = ts(blk(T.jj, j), T.iob[:, :], T.rm[:, j:j + 1], None, ALU.mult, dep=[vrm, pib])
    vt = []
    last = {}
    for t in range(4):
        for h in range(2):
            v = ts(T.tb[:, 8 * t:8 * t + 8, 16 * h:16 * h + 16], blk(T.nxi, t), T.hm[:, h:h + 1], None, ALU.mult,
                   dep=[("dn%d" % t, 16)])
        vt.append(v)
        if t == 0:
            vsa = ts(T.sela[:, :], T.pb[:, 0:128], T.qgf[:, 2:3], None, ALU.is_equal, dep=[tbc])
    for h in range(2):
        vsm = ts(T.selm[:, :, 16 * h:16 * h + 16], T.sela[:, :], T.hm[:, h:h + 1], None, ALU.mult, dep=[vsa])
    vsg = ts(T.sg[:, :], T.mg[:, :], gcol, None, ALU.is_equal, dep=[pmg])
    vlow = ts(T.low[:, :], T.mq[:, :], qcol, -256.0, ALU.not_equal, ALU.mult)
    for ch in range(3):
        j = CUTS[ch + 1] // 2 % 16
        arep = act(blk(T.rep, ch), T.sg[:, :], ACTF.Copy, scale=T.rm[:, j:j + 1], dep=[vsg])

    for t in range(4):
        for c in range(8):
            tof = mm(T.pl[32 * t:32 * t + 32, 0:4, c:64:8], T.tb[:, 8 * t + c, :], T.sela[:, 32 * t:32 * t + 32], True, True,
                     dep=[vt[t], vsa])
    done = [0] * 4
    for b in (3, 2, 1, 3, 2, 0, 3, 2, 1, 0, 1, 0):
        if done[b] == 0:
            last[b] = cp(T.oi[:, b, :], T.pl[:, b, :], dep=[tof])
        elif done[b] == 1:
            last[b] = ts(T.oi2[:, b, :], T.oi[:, b, :], 127, None, ALU.bitwise_and, dep=[last[b]])
        else:
            last[b] = cp(T.off[:, b, :], T.oi2[:, b, :], dep=[last[b]])
        done[b] += 1

    def add(t, eo, rhs, dep):
        mm(px[eo][32 * t:32 * t + 32, :], T.selm[:, 2 * t + eo, :], rhs, False, False, dep=dep)

    def nexts(t, eo):
        for h in range(2):
            add(t, eo, T.tb[:, 8 * t:8 * t + 8, 16 * h:16 * h + 16], [vsm])
    for t in range(4):
        nexts(t, 1)

    def entries(t):
        v = ts(blk(T.emh, t), blk(T.emi, t), -2048, 1.0 / 4096, ALU.add, ALU.mult, dep=[("de%d" % t, 16)])
        if t < 3:
            nexts(t, 0)
        add(t, 1, blk(T.emh, t), [v])
        if t == 3:
            last["e1"] = mm(px[1], T.ones[0:1, :], T.nil[0:1, :], False, True)
            nexts(t, 0)
            for k in range(4):
                add(k, 0, blk(T.emh, k), [])
            last["e0"] = mm(px[0], T.ones[0:1, :], T.nil[0:1, :], False, True)

    def table(eo):
        last["t%d" % eo] = act(xtab(r, eo, r), px[eo], ACTF.Copy, scale=4096.0, bias=2048.0 + (0 if eo else 4096.0 * xoff(r)),
                               dep=[last["e%d" % eo]])
    entries(0)
    entries(1)

    prev = [(blk(T.jj, e // 2 % 16), jd[e // 2 % 16]) for e in CUTS[1:]]
    vm = {}

    def listed(ch, part):
        ps = (T.pt, T.pb)[ch][:, 0:128]
        if part == 0:
            mm(ps, T.eye[:, :], T.low[:, :], True, False, dep=[vlow, pz])
            v = mm(ps, blk(T.rep, ch), prev[ch][0], False, True, dep=[arep, prev[ch][1]])
            vm[ch] = scan(blk(T.ms, ch), T.rs[:, :], ps, ALU.mult, ALU.max, dep=[v, pz])
        else:
            vm[ch] = cp(blk(T.lm, ch, 8), blk(T.ms, ch)[:, 15:128:16], dep=[vm[ch]])
    todo = [(ch, part) for part in range(2) for ch in (1, 0)]
    turns = TURNS if r else TURNS[::-1]
    for n in range(CUTS[3] - CUTS[2]):
        for ch in turns:
            i = CUTS[ch + 1] - 1 - n
            if i < CUTS[ch]:
                continue
            win, dw = prev[ch]
            o = T["w%s%d" % ("abc"[ch], i % 2)][:, :]
            b, c = 2 * (i % 2) + i // 16, 8 * (i % 16 // 2)
            src = win.indirect(T.off[:, b, c:c + 8])
            dep = [last[b], dw]
            if i % 2 or i == CUTS[2]:
                dw = act(o, src, ACTF.Copy, dep=dep)
            elif i == CUTS[ch]:
                dw = cp(o, src, dep=dep)
            else:
                dw = tt(o, src, blk(T.jj, i // 2), ALU.add, dep=dep + [jd[i // 2]])
            prev[ch] = (o, dw)
            if n == 1 and ch != turns[2]:
                entries(2 + turns.index(ch))
        if n in (3, 4):
            table(4 - n)
        if n in (3, 5):
            ts((T.tri0, T.tri1)[n // 4][:, :], T.kq[:, :], T.n0[:, 2:3], None, (ALU.is_gt, ALU.is_le)[n // 4], dep=[pz, acol])

    def earlier():
        tt(T.lt[:, :], T.tri0[:, :], T.sg[:, :], ALU.mult)
    if r:
        for x in todo:
            listed(*x)
            if x == todo[0]:
                earlier()
        v = tt(T.wu[:, :], prev[2][0].indirect(blk(T.lm, 1, 8)), prev[1][0], ALU.add, dep=[vm[1], prev[2][1]])
        vw = tt(blk(T.big, r), T.wu[:, :].indirect(blk(T.lm, 0, 8)), prev[0][0], ALU.add, dep=[v, vm[0]])
    else:
        fill(T.s0[:, :], 0)
        v = fill(T.sr[:, :], 0)
        for ch in range(3):
            lst, j = T.s0[:, 16 + 32 * ch:17 + 32 * ch], CUTS[ch] // 2
            v = cp(blk(T.f0, ch, 16), prev[ch][0].indirect(lst), dep=[v, prev[ch][1]])
            if ch < 2:
                v = cp(T.s0[:, 48 + 32 * ch - j:64 + 32 * ch - j], prev[ch][0].indirect(lst))
        cols = [T.f0[:, 16 * ch + CUTS[ch] // 2:16 * ch + CUTS[ch] // 2 + 1] for ch in range(3)]
        vw = ts(T.s0[:, 2:3], cols[0], cols[1], cols[2], ALU.add, ALU.add, dep=[v])
        ts(T.sr[:, 2:3], cols[0], cols[1], cols[2], ALU.add, ALU.add)
        earlier()

    def send(src, dst, sem, lsem, dests):
        g.remote_dma_fused([transfer(src, [dst] * len(dests), sem, [cores[d] for d in dests], topo.engines(core, cores[dests[0]]))],
                           local_sem=T.sem[lsem])
    ne = len(topo.engines(core, cores[nb[0]]))
    wait("p", *last["t1"])
    send(xtab(r, 1, r), xtab(r, 1, r), "x%d" % r, "lx", users(r))
    wait("p", *last["t0"])
    g.remote_dma_fused([transfer(xtab(r, 0, r), [xtab(r, 0, r)], "xh", [helper(r)], inside(r))], local_sem=T.sem.lx)
    far = [d for d in FIRST if r in maps(d)]
    wait("p", *vw)
    late = [r + 2] if r == HEAD else []
    if r:
        send(blk(T.big, r), blk(T.big, r), "w%d" % r, "lw", users(r) if r > 1 else [0, 3, 2])
    else:
        send(T.s0[:, 0:8], T.sr[:, 0:8], "w0", "lw", [1, 3, 2])
    for u in range(nc):
        v = act(blk(T.mk3, u, 16), T.rm[:, :], ACTF.Copy, scale=1.0 if 0 < u < nu else n0 if u else m0)
    v = act(T.mkn[:, 0:16 * nc], T.mk3[:, 0:16 * nc], ACTF.Copy, scale=ONE, dep=[v])
    if r == 0:
        for u in range(nu):
            act(blk(T.mk0, u, 16), blk(T.mkn, u if u < nu - 1 else nu, 16), ACTF.Copy, dep=[v])
    for d in [r] + nb:
        for k in (1, 2):
            ax = act(xtab(d, 1, r, k), xtab(d, 1, r), ACTF.Copy, dep=[last["t1"] if d == r else ("x%d" % d, ne)])

    trio = [d for d in near if d >= HEAD]
    lists = {}

    def here(d):
        return vw if d == r else ("w%d" % d, ne)

    def as_list(k, d):
        ps = (T.pt, T.pb)[k][:, 0:128]
        mm(ps, T.eye[:, :], T.low[:, :], True, False, dep=[vw])
        v = mm(ps, blk(T.rep, 2), blk(T.big, d), False, True, dep=[here(d)])
        v = scan(blk(T.ms, k), T.rs[:, :], ps, ALU.mult, ALU.max, dep=[v])
        lists[k] = cp(blk(T.lm, 2 + k, 8), blk(T.ms, k)[:, 15:128:16], dep=[v])
    fill(T.s[:, 0:16], 0)
    v = ts(T.gl0[:, :], T.gl0[:, :], T.qgf[:, 3:4], T.n0[:, 3:4], ALU.add, ALU.mult)
    tt(T.gt[:, :], T.tri1[:, :], T.sg[:, :], ALU.mult)
    ts(T.gl[:, :], T.gl0[:, :], 8.0, None, ALU.add, dep=[v])

    def follow():
        v = cp(T.sr[:, 4:20], blk(T.big, 1).indirect(T.sr[:, 2:3]), dep=[vw] + [("w%d" % d, ne) for d in range(HEAD) if d != r])
        if r < HEAD:
            wait("p", *v)
            send(T.sr[:, 0:8], T.sr[:, 0:8], "h", "lh", [6, 7, 5] if r else [4])
        return v
    vh = None
    if HEAD <= r < N - 1:
        as_list(1, r)
    if far:
        wait("p", *lists[1])
        send(blk(T.lm, 3, 8), blk(T.ml, r, 8), "m%d" % r, "lm", far)
    if late:
        send(blk(T.big, r), blk(T.big, r), "w%d" % r, "lw", late)
    told = [d for d in (6, 7, 5, 4, 3) if (r, 1) in tellers(d)]
    for u, d in enumerate(near):
        for k in range(3):
            vs = ts(blk(T.xn, 3 * (d % 3) + k), xtab(d, 1, r), 2.0 ** -19, k - 0.5 + 2.0 ** -20, ALU.mult, ALU.add,
                    dep=[last["t1"] if d == r else ("x%d" % d, ne)])
        if r > 3 and u and 2 - u not in lists:
            as_list(2 - u, trio[2 - u])
        if r == 0 and u == 0:
            for k, lst in enumerate((T.s[:, 0:1], T.sr[:, 2:3])):
                v = tt(blk(T.g2, k, 16), T.xe[:, 0:128].indirect(lst), blk(T.mk3, 2 * k, 16), ALU.mult, dep=[vs, ax, last["t0"]])
            v = scan(T.sc1[:, 0:32], T.rs[:, 0:32], T.g2[:, 0:32], ALU.mult, ALU.add, dep=[v])
            v = ts(T.lz[:, 0:2], T.sc1[:, 15:32:16], 1.0 / 4096, 1.0 / 8192 - 0.5, ALU.mult, ALU.add, dep=[v])
            v = tt(T.g0[:, 0:32], T.xn[:, 0:384].indirect(T.lz[:, 0:2]), T.mk0[:, :], ALU.mult, dep=[v])
            vh = follow()
            wait("p", *scan(T.e0[:, :], T.g0[:, :], T.g0[:, :], ALU.add, ALU.max, dep=[v]))
            send(T.e0[:, 32:40], blk(T.cin, 0, 8), "c0", "lc", [d for d in range(N - 1, 0, -1) if (0, 0) in tellers(d)])
        if r == 1 and u == 0:
            vh = follow()
    if r in (2, 3):
        vh = follow()
    if r > 3:
        lists["u"] = act(T.wu[:, :], blk(T.big, trio[2]).indirect(blk(T.lm, 3, 8)), ACTF.Copy, dep=[vw, here(trio[2]), lists[1]])
    vs = ("v", cnt["v"])
    aw = {}
    for d in maps(r):
        aw[d] = act(blk(T.big, d), T.iob[:, :].indirect(blk(T.ml, d, 8)), ACTF.Copy, dep=[("m%d" % d, ne)])
    for k, d in enumerate(trio):
        if k and r > 3:
            aw[d] = act(blk(T.nw, k), (blk(T.big, d), T.wu[:, :])[k - 1].indirect(blk(T.lm, 2, 8)), ACTF.Identity, bias=lane0,
                        dep=[here(d), lists[0], lists["u"]])
        elif k and d > r:
            aw[d] = act(blk(T.nw, k), blk(T.big, d).indirect(blk(T.lm, 3, 8)), ACTF.Identity, bias=lane0, dep=[here(d), lists[1]])
        else:
            aw[d] = act(blk(T.nw, k), blk(T.big, d), ACTF.Identity, bias=lane0, dep=[here(d)])
    for u in range(nc):
        d = near[0] - 1 + u
        for k in range(2):
            a, b = (4096.0 * (xoff(e) + 128 * (k + 1)) for e in (d, d + 1))
            athr = act(T.thr[:, 4 * k + u:4 * k + u + 1], m0, ACTF.Identity, scale=b - a, bias=a)

    head = vh or ("h", ne)
    for d in range(HEAD, near[0]):
        vs = cp(T.s[:, 2 * d + 2:2 * d + 18], blk(T.big, d).indirect((T.sr if d == HEAD else T.s)[:, 2 * d:2 * d + 1]),
                dep=[vs, head, aw[d] if d in maps(r) else here(d)])
    col = []
    for u in range(nc):
        d, o = near[0] - 1 + u, blk(T.sb, u, 16)
        if u == 0:
            col.append(((T.sr if 0 <= d < HEAD else T.s)[:, 2 * d + 2:2 * d + 3], vs))
        elif d < HEAD:
            col.append((o[:, 0:1], ts(o[:, 0:1], T.sr[:, 2 * d + 2:2 * d + 3], lane0, None, ALU.add, dep=[head, acol])))
        else:
            k = trio.index(d)
            if k and r == 3:
                src, dep = T.nw[:, 128 * k - 128:128 * k + 128].indirect(col[1][0]), col[1][1]
            else:
                src, dep = blk(T.nw, k).indirect((T.sr if trio[0] == HEAD else T.s)[:, 2 * trio[0]:2 * trio[0] + 1]), vs
            col.append((o[:, 0:1], cp(o, src, dep=[dep, head, aw[d]])))
    n3 = 16 * nc
    for u, (lst, dep) in enumerate(col):
        a = 128 * max(u - 1, 0)
        v = tt(blk(T.g2, u, 16), T.xe[:, a:a + 256].indirect(lst), blk(T.mk3, u, 16), ALU.mult,
               dep=[dep, head, ax] + [("e%d" % d, ne) for d in nb])
    v = scan(T.sc1[:, 0:n3], T.rs[:, 0:n3], T.g2[:, 0:n3], ALU.mult, ALU.add, dep=[v])
    ve = T.sc1[:, 15:n3:16]
    v = ts(T.ls2[:, 0:nc], ve, 1.0 / 4096, 1.0 / 8192 - 0.5, ALU.mult, ALU.add, dep=[v])
    for k in range(2):
        vc = tt(T.ca[:, 4 * k:4 * k + nc], ve, T.thr[:, 4 * k:4 * k + nc], ALU.is_ge, dep=[athr])
    for k in range(2):
        ac = act(T.cab[:, k:2 * nc:2], T.ca[:, 4 * k:4 * k + nc], ACTF.Copy, scale=ONE, dep=[vc])
    u0 = r - near[0]

    def counts():
        return tt(T.gn[:, 0:n3], T.xn[:, 0:384 * nu].indirect(T.ls2[:, 0:nc]), T.mkn[:, 0:n3], ALU.mult, dep=[v])

    def entry():
        return tt(T.g3[:, 0:n3], T.xo[:, 0:384 * nu].indirect(T.ls2[:, 0:nc]), T.mk3[:, 0:n3], ALU.mult, dep=[v])

    def running():
        return scan(T.en[:, 16:n3 + 24], T.gn[:, 0:n3 + 8], T.gn[:, 0:n3 + 8], ALU.add, ALU.max, dep=[vn])

    def number(eo, k, src):
        return ts(T.ei[:, 8 * eo + k:8 * eo + 2 * nc:2], src, 6 * k, 63, ALU.logical_shift_right, ALU.bitwise_and)

    def spread(eo, dep):
        cs = slice(8 * eo, 8 * eo + 2 * nc)
        v = tt(blk(T.val, eo, 16)[:, 0:2 * nc], T.ei[:, cs], T.cab[:, cs], ALU.add, dep=dep)
        return act(blk(T.gs, eo, 64)[:, 0:16 * (nc - u0)], blk(T.val, eo, 16).indirect(T.gl[:, 0:nc - u0]), ACTF.Relu,
                   bias=1.0 - ONE, dep=[v])
    if told:
        vn = counts()
        vg = entry()
        vn = running()
        wait("p", *vn)
        send(T.en[:, n3 + 16:n3 + 24], blk(T.cin, r, 8), "c%d" % r, "lc", told)
    else:
        vg, vn = entry(), counts()
    vg = scan(T.sc3[:, 0:n3], T.rs[:, 0:n3], T.g3[:, 0:n3], ALU.mult, ALU.add, dep=[vg])
    vo = T.sc3[:, 15:n3:16]
    number(0, 0, ve)
    if not told:
        vn = running()
    ve1 = number(0, 1, ve)
    for k in range(2):
        ts(T.cab[:, 8 + k:8 + 2 * nc:2], vo, 4096.0 * 128 * (k + 1), ONE, ALU.is_ge, ALU.mult, dep=[vg])
    for k in range(2):
        vo1 = number(1, k, vo)
    ags = [spread(0, [ve1, ac])]
    vc = tt(T.ce[:, 0:nc], T.cab[:, 0:2 * nc:2], T.cab[:, 1:2 * nc:2], ALU.add)
    ags.append(spread(1, [vo1]))
    sums = [(T.sg, blk(T.cin, s, 8)[:, 0:nc], ("c%d" % s, ne)) for s, c in reversed(tellers(r))]
    k = len(sums) - (r > 2 * HEAD)
    sums[k:k] = [(T.gt, T.en[:, 15:n3:16], vn), (T.lt, T.en[:, 31:n3 + 16:16], vn)]
    for k, (lh, rh, dep) in enumerate(sums):
        tp = mm(T.pq[:, 0:nc], lh[:, :], rh, k == 0, k == len(sums) - 1, dep=[dep])

    yp = T.py[0:8, 0:32]
    for eo in range(2):
        for u in range(u0, nc):
            oh, at = blk(T.oh, 4 * eo + u, 64), T.pq[:, u:u + 1]
            if eo:
                v = ts(oh[:, 0:33], T.iot[:, 0:33], T.ce[:, u:u + 1], at, ALU.subtract, ALU.is_equal, dep=[vc])
            else:
                v = ts(oh[:, 0:33], T.iot[:, 0:33], at, None, ALU.is_equal, dep=[tp])
            for k in range(2):
                ty = mm(yp, blk(T.gs, 8 * eo + 2 * (u - u0) + k, 8), oh[:, 1 - k:33 - k], (eo, u, k) == (0, u0, 0), (eo, u, k) == (1, nu, 1),
                        dep=[v, ags[eo]])
    wait("y", *ts(T.ys[0:8, :], yp, -1.0, None, ALU.add, dep=[ty]))
    Y.dma_start(T.y[:, :], T.ys[0:8, :]).then_inc(T.sem.yo, 16)

    wait("y", "yo", 16)
    wait("p", "lx", ne + len(inside(r)))
    wait("p", "lw", 2 * ne if late else ne)
    if r < HEAD:
        wait("p", "lh", ne)
    if told:
        wait("p", "lc", ne if r else 2 * ne)
    if far:
        wait("p", "lm", ne)
    for name in ("v", "a", "t"):
        wait("p", name, cnt[name])
    wait("v", "p", cnt["p"])
